import numpy as np, ml_dtypes
CORES = [2,6,10,14,18,22,26,30]
N = 8
BF = ml_dtypes.bfloat16
def gentries(a):
    return np.ascontiguousarray(a.reshape(8, 16, -1).transpose(0, 2, 1)).reshape(8, -1)
def gtable(e):
    e = np.asarray(e); return np.ascontiguousarray(e.reshape(8, -1, 16).transpose(0, 2, 1)).reshape(128, -1).astype(np.int32)
def f(rng, *shape):
    return (rng.standard_normal(shape, dtype=np.float32) * np.exp2(rng.integers(-2, 3, shape[:-1] + (1,)))).astype(BF)
def wide(rng, *shape):
    v = f(rng, *shape).astype(np.float32); k = shape[:-2] + (1, shape[-1])
    return (v * np.exp2(rng.integers(-6, 7, k)) * (rng.random(k) > 0.0625)).astype(BF)
W, K, S, RO, FI, CAP = 6144, 1024, 3, 2, 8, 128
def parts(rng):
    b = rng.random((N, 8, S, W)) < rng.choice(np.array([0.5, 0.6, 0.75]), (N, 8, S, 1)); b[..., 0] = True; b[..., W - 1] = True
    nx = np.zeros((N, 8, S, W), np.int64); cur = np.zeros((N, 8, S, K), np.int64)
    for a in range(N):
        for g in range(8):
            for i in range(S):
                v = np.nonzero(b[a, g, i])[0]
                nx[a, g, i] = rng.choice(v, W); nx[a, g, i, v] = rng.permutation(v); cur[a, g, i] = rng.choice(v, K)
    return b, nx, cur, rng.integers(0, S, (N, 8, K)), rng.integers(0, W, (N, 8, W))
def pack(x, b, nx, cur, typ, fro, w):
    mem = np.add.reduce(b.astype(np.int64) << np.arange(S)[:, None], axis=2)
    return {"x": x.astype(BF).reshape(N, 128, W), "nxt": nx.reshape(N, 8, S * W).astype(np.int32), "mem": mem.astype(np.int32), "fro": fro.astype(np.int32),
            "cur": np.stack([gtable(a.reshape(8, S * K)) for a in cur]), "typ": np.stack([gtable(a) for a in typ]), "w0": w.astype(BF).reshape(N, 128, K)}
def setup_inputs(rng):
    b, nx, cur, typ, fro = parts(rng)
    return pack(f(rng, N, 128, W), b, nx, cur, typ, fro, f(rng, N, 128, K))
def setup_inputs_room(rng):
    b, nx, cur, typ, fro = parts(rng)
    x = np.minimum(f(rng, N, 128, W).astype(np.float32), 24); w = f(rng, N, 128, K).astype(np.float32).reshape(N, 8, 16, K)
    w[:, ::2] = np.abs(w[:, ::2]) + 32; w[:, 1] = np.abs(w[:, 1]) + 32
    at = np.take_along_axis(cur, typ[:, :, None, :], 2)[:, :, 0]
    for q in range(FI): at = np.take_along_axis(nx.reshape(N, 8, S * W), typ * W + at, 2)
    z = np.where(typ == S - 1, 0, typ + 1)
    for a in range(N):
        m, zz, cc, i = at[a, 1], z[a, 1], cur[a, 1], a % S
        o = rng.permutation(np.arange(1, K - 1)); o = o[b[a, 1, zz[o], m[o]] & (m[o] > 0) & (m[o] < W - 2)]
        o = rng.permutation(o[np.unique(m[o], return_index=True)[1]])
        by = [o[zz[o] == j] for j in range(S)]
        cc[zz, np.arange(K)] = m
        for j in range(S): cc[j, by[j][:3]] = (0, W - 2, W - 1)
        u, v, p, q, e1, e2 = by[i][3:9]
        ends = [K - 1, 0] if a % 2 == 0 else [0, K - 1]
        typ[a, 1, ends] = typ[a, 1, [u, v]]; cc[:, ends] = cc[:, [u, v]]
        cc[i, ends[0]] = m[q]; cc[i, p] = m[v]
        r = rng.choice(np.nonzero(~b[a, 1, i, :W - 2])[0]); nx[a, 1, i, r] = nx[a, 1, i, m[e1]]; cc[i, e1] = r; cc[i, e2] = r
        b[a, 1, typ[a, 1, [u, p]], m[[u, p]]] = False
    for a in range(N):
        for g in range(0, 8, 2):
            m = at[a, g]; zz = z[a, g]; e = rng.permutation(np.nonzero(b[a, g, zz, m])[0])
            k = int(rng.choice(np.array([0, 1, CAP - 1, CAP, CAP + 1, len(e)])))
            if a < 2: k = ((CAP, CAP + 1, CAP - 1, 0), (1, CAP, len(e), CAP + 1))[a][g // 2]
            cur[a, g, zz[e], e] = m[e]
            one = e[(zz[e] == 0) & (m[e] != 0)][:1] if k == 1 else e[:0]
            e = np.concatenate([one, e])[:k]; k = len(e)
            c = rng.choice(np.concatenate([rng.permutation(W)[:int(rng.choice(np.array([24, 150, 600, W])))], m[e[:k // 4]]]), k)
            cur[a, g, zz[e], e] = np.where(c == m[e], (c + 1) % W, c)
            cur[a, g, 0, one] = 0
    return pack(x, b, nx, cur, typ, fro, w)
def setup_inputs_ties(rng):
    b, nx, cur, typ, fro = parts(rng)
    x = 4.0 * rng.integers(-3, 4, (N, 8, 16, W)); w = 4.0 * rng.integers(-3, 4, (N, 8, 16, K))
    x[::2, 5] = rng.choice(np.array([7.96875, 8, 8, 8, 8.0625]), (N // 2, 16, W)); x[1::2, 5] = 64
    w[:, 5] = rng.choice(np.array([-1.0, 1.0]), (N, 16, K)) * np.exp2(-1.0 * rng.integers(14, 21, (N, 16, K)))
    return pack(x, b, nx, cur, typ, fro, w)
def setup_inputs_alike(rng):
    b, nx, cur, typ, fro = parts(rng)
    cur[:, 0] = rng.choice(np.array([0, W - 1]), (N, S, K)); nx[:, 1] = rng.choice(np.array([0, 3, W // 2, W - 1]), (N, S, W)); nx[:, 2] = np.arange(W)
    fro[:, 3] = rng.choice(np.array([0, W - 1]), (N, W)); b[:, 4] = True; b[:, 5] = False; typ[:, 6] = 0; cur[:, 7] = np.repeat(cur[:, 7, :1], S, axis=1)
    return pack(f(rng, N, 128, W), b, nx, cur, typ, fro, f(rng, N, 128, K))
def setup_inputs_hot(rng):
    b, nx, cur, typ, fro = parts(rng)
    sh = rng.choice(np.array([-64, 0, 64]), (N, 8, 1, 1)); sh[0, :4, 0, 0] = (-64, 64, -64, 0); sh[1, 4:, 0, 0] = (0, -64, 64, -64)
    b[rng.random((N, 8)) < 0.3] = True; b[0, 0] = True; b[1, 5] = True
    x = f(rng, N, 128, W).reshape(N, 8, 16, W); w = f(rng, N, 128, K).astype(np.float32).reshape(N, 8, 16, K) + sh
    for g in (3, 6):
        b[:, g] = True; w[:, g] = 4
        x[::2, g] = (rng.integers(0, 25, x[::2, g].shape) * 0.125).astype(BF); x[1::2, g] = (rng.integers(-32, -7, x[1::2, g].shape) * 0.125).astype(BF)
    for a in range(0, N, 2):
        o = np.concatenate([CAP // 2 + rng.permutation(CAP // 2)[:CAP // 4], CAP + rng.permutation(K - CAP)[:CAP // 8]])
        w[a, 6][:, o] = 1000
    return pack(x, b, nx, cur, typ, fro, w)
def setup_inputs_spread(rng):
    b, nx, cur, typ, fro = parts(rng)
    return pack(wide(rng, N, 128, W), b, nx, cur, typ, fro, wide(rng, N, 128, K))
def check_inputs(d):
    bad = []
    for k, hi in (("nxt", W - 1), ("mem", 2 ** S - 1), ("fro", W - 1), ("cur", W - 1), ("typ", S - 1)):
        if np.min(d[k]) < 0 or np.max(d[k]) > hi: bad.append("range of " + k)
    for k in ("x", "w0"):
        if not np.all(np.abs(d[k].astype(np.float32)) < 2.0 ** 60): bad.append("size of " + k)
    return bad
def reference(x, nxt, mem, fro, cur, typ, w0):
    pick = np.take_along_axis
    X = x.astype(np.float32).reshape(N, 8, 16, W); w = w0.astype(np.float32).reshape(N, 8, 16, K)
    nx = nxt.astype(np.int64); mb = mem.astype(np.int64); fo = fro.astype(np.int64)
    c = np.stack([gentries(a) for a in cur]).astype(np.int64).reshape(N, 8, S, K); s = np.stack([gentries(a) for a in typ]).astype(np.int64)
    for t in range(RO):
        for q in range(FI):
            at = pick(c, s[:, :, None, :], 2)[:, :, 0]
            m = pick(nx, s * W + at, 2)
            hit = np.add.reduce((pick(X, m[:, :, None, :], 3) >= w).astype(np.int64), axis=2) >= 9
            bits = pick(mb, m, 2)
            for i in range(S): c[:, :, i] = np.where((s == i) | (hit & (((bits >> i) & 1) == 1)), m, c[:, :, i])
            s = np.where(hit, np.where(s == S - 1, 0, s + 1), s)
        z = np.where(s == S - 1, 0, s + 1)
        m = pick(c, s[:, :, None, :], 2)[:, :, 0]; e = pick(c, z[:, :, None, :], 2)[:, :, 0]
        want = (((pick(mb, m, 2) >> z) & 1) == 1) & (m != e)
        slot = want & (np.add.accumulate(want.astype(np.int64), axis=2) <= CAP)
        for a in range(N):
            for g in range(8):
                j = np.nonzero(slot[a, g])[0]
                p1 = z[a, g, j] * W + m[a, g, j]; p2 = z[a, g, j] * W + e[a, g, j]
                named = np.bincount(np.concatenate([p1, p2]), minlength=S * W)
                ok = (named[p1] == 1) & (named[p2] == 1); p1 = p1[ok]; p2 = p2[ok]
                v1 = nx[a, g, p1]; v2 = nx[a, g, p2]
                nx[a, g, p1] = v2; nx[a, g, p2] = v1
        k = pick(fo, m, 2)
        y = np.stack([pick(X[(a + 1 + t) % N], k[a][:, None, :], 2) for a in range(N)])
        w = w + np.minimum(np.maximum(y - w, np.float32(-8)), np.float32(8))
    return {"yc": np.stack([gtable(a.reshape(8, S * K)) for a in c]).astype(np.float32), "yw": w.reshape(N, 128, K).astype(np.float32), "yn": nx.astype(np.float32)}

@@ -1,0 +1,604 @@
+from concourse.mybir import AluOpType, ActivationFunctionType
+
+A = AluOpType
+AF = ActivationFunctionType
+W, K, NT, ROUNDS, FINDS, CAP = 6144, 1024, 3, 2, 8, 128
+H = K // 2
+STAMP = 8192
+BIG = 1 << 18
+NEQ = 4
+MS = 3
+FB, CB, PB, LB = 0.0, 0.3, 0.4, 0.4
+WP = 0.001
+SB, BF, FP, I32, U16 = "sbuf", "bfloat16", "float32", "int32", "uint16"
+SCRATCH = {
+    "xs": (SB, [128, W], BF), "x1": (SB, [128, W], BF), "x2": (SB, [128, W], BF),
+    "inf": (SB, [128, W], BF), "pw": (SB, [128, 3 * W + 2 * CAP], BF),
+    "wb": (SB, [128, K], BF), "wf": (SB, [128, K], FP), "dd": (SB, [128, K], FP),
+    "n32": (SB, [128, 1152], I32), "nhi": (SB, [128, 1152], BF), "nlo": (SB, [128, 1152], BF),
+    "m32": (SB, [128, 384], I32), "mi": (SB, [128, 768], I32), "bits": (SB, [128, 1152], BF),
+    "f32": (SB, [128, 384], I32), "fhi": (SB, [128, 384], BF), "flo": (SB, [128, 384], BF),
+    "pv": (SB, [128, 1152], FP), "phi": (SB, [128, 1152], BF), "plo": (SB, [128, 1152], BF),
+    "cur32": (SB, [128, 192], I32), "typ32": (SB, [128, 64], I32), "tf": (SB, [128, 64], FP),
+    "lst": (SB, [128, 192], U16), "ci": (SB, [128, 384], I32), "ycf": (SB, [128, 192], FP),
+    "ones": (SB, [128, 192], BF), "idf": (SB, [128, 8, 4, 4], FP), "idb": (SB, [128, 128], BF), "idn": (SB, [128, 8 * 128], BF),
+    "stl": (SB, [128, 128 * (ROUNDS * FINDS + 1)], BF), "c72": (SB, [128, 128], BF),
+    "wnx": (SB, [128, 24], BF), "wv": (SB, [128, 24], BF), "wx": (SB, [128, 48], BF), "wbit": (SB, [128, 24], BF), "wcnt": (SB, [128, 48], BF),
+    "sel": (SB, [128, 32], FP), "selr": (SB, [128, 32], FP),
+    "pid": (SB, [128, 1], I32), "pm": (SB, [128, 4], I32), "cols": (SB, [128, 16], FP),
+    "bo": (SB, [128, 128], BF), "lm": (SB, [128, 128], BF), "plw": (SB, [128, 128], BF), "km": (SB, [128, 128], BF),
+    "eqm": (SB, [128, 16, 8, 16], BF), "dp": (SB, [128, 16, 8, 16], BF), "db": (SB, [128, 16, 8, 16], BF), "df": (SB, [128, 16, 8, 16], BF),
+    "kc": (SB, [128, 8], FP), "kch": (SB, [128, 8], FP), "dumc": (SB, [128, 16], FP), "kio": (SB, [128, 128], FP),
+    "ttl": (SB, [128, 256], FP), "eq": (SB, [128, 256 * NEQ], BF), "lk": (SB, [128, 128], BF),
+    "mz": (SB, [128, 128], FP), "mzi": (SB, [128, 256], I32), "mp4": (SB, [128, 32, 4], FP),
+    "lte": (SB, [128, 32, 4, 4], FP), "ltc": (SB, [128, 48, 4, 4], FP),
+    "ot": (SB, [128, 128], U16), "otf": (SB, [128, 64], FP), "nq": (SB, [128, 64], BF),
+    "ra": (SB, [128, K + 16], BF), "rb": (SB, [128, K + 16], BF),
+    "wt": (SB, [128, 64], BF), "pc": (SB, [128, 64], BF), "rt": (SB, [128, 72], FP), "junk": (SB, [128, 512], BF),
+    "ck": (SB, [128, 8], FP), "ckl": (SB, [128, 8], U16), "ckb": (SB, [128, 8], BF), "le": (SB, [128, 128], BF), "jk": (SB, [128, 8], U16),
+    "sab": (SB, [128, 256], BF), "plr": (SB, [128, 256], U16), "plt": (SB, [128, 16], FP),
+    "cb": (SB, [128, 128], BF), "cp": (SB, [128, 128], FP), "dab": (SB, [128, 128], FP), "dmv": (SB, [128, 128], FP),
+    "nv": (SB, [128, 256], BF), "pd": (SB, [128, 16], FP), "of": (SB, [128, 32], FP), "ofl": (SB, [128, 16], U16),
+    "kl": (SB, [128, 64], U16), "yh": (SB, [128, 1152], BF), "yl": (SB, [128, 1152], BF), "yf": (SB, [128, 1152], FP),
+}
+for _b in range(2):
+    for _n, _s, _d in (("ge", [128, H], BF), ("rw", [128, H], BF), ("off", [128, 32], U16), ("st", [128, 192], FP), ("gt", [128, 192], BF),
+                       ("sg", [128, 192], BF), ("ab", [128, 96], BF), ("ac", [128, 96], FP), ("tt", [128, 96], FP),
+                       ("tu", [128, 32], FP), ("mp", [128, 8, 4], FP), ("lt", [128, 8, 4, 4], FP), ("oi", [128, 32], I32), ("oj", [128, 32], I32)):
+        SCRATCH["%s%d" % (_n, _b)] = (SB, _s, _d)
+for _i in range(8):
+    SCRATCH["b%d" % _i] = ("psum", [128, 512], FP)
+ENG = {"V": "cv", "S": "cs", "P": "cp_", "G": "cg"}
+DMAS = ["l_m", "l_c", "l_t", "l_x", "l_w", "l_f", "d_i0", "d_i1", "d_i2", "d_bi", "d_fl", "d_pf", "d_pw", "d_rb", "d_y1", "d_yc", "d_yw0", "d_yw1", "d_yn1"]
+SEMAPHORES = sorted(ENG.values()) + DMAS + ["rx1", "rx2", "tx"]
+
+
+def rank_program(g, core, T, topo):
+    rank = T.rank_of(core)
+    if rank is None:
+        return
+    N = len(T.cores)
+    queues = {"V": g.vector, "S": g.scalar, "P": g.tensor, "G": g, "Y": g.sync}
+    clock = {q: {} for q in queues}
+    total = {}
+    snap = {}
+    acc = {}
+    free = {q: 0.0 for q in queues}
+    done = {}
+    rec = [None]
+
+    def know(q, sem, val):
+        c = clock[q]
+        if c.get(sem, 0) >= val:
+            return
+        queues[q].wait_ge(T.sem[sem], val)
+        for s, v in snap.get((sem, val), {}).items():
+            if v > c.get(s, 0):
+                c[s] = v
+        c[sem] = val
+
+    def region(r):
+        buf, lo, hi, tag = (r + (0, 1 << 20, None))[:4] if len(r) == 1 else (r + (None,))[:4]
+        if SCRATCH.get(buf, ("", 0, 0))[0] == "psum":
+            return buf, 0, 512, None, True
+        return buf, lo, hi, tag, False
+
+    def needs(q, reads, writes, dma):
+        need = {}
+        t = free[q]
+        for lst, wr in ((reads, False), (writes, True)):
+            for r in lst:
+                buf, lo, hi, tag, bank = region(r)
+                for a in acc.get(buf, ()):
+                    if a[1] <= lo or hi <= a[0] or (tag is not None and a[2] is not None and a[2] != tag):
+                        continue
+                    same = a[3] == q and not dma and a[4] not in DMAS
+                    if not (wr or a[6]) and (not bank or same):
+                        continue
+                    if same and (q == "P" or not a[6]):
+                        continue
+                    need[a[4]] = max(need.get(a[4], 0), a[5])
+                    t = max(t, done.get((a[4], a[5]), 0.0) + 0.06)
+        return need, t
+
+    def emit(q, fn, reads, writes, dma, cost):
+        need, t = needs(q, reads, writes, dma)
+        for s in sorted(need):
+            know(q, s, total[s] if s in DMAS else need[s])
+        ins = fn(queues[q])
+        sem, inc = (dma, 16) if dma else (ENG[q], 1)
+        ins.then_inc(T.sem[sem], inc)
+        total[sem] = total.get(sem, 0) + inc
+        val = total[sem]
+        s = dict(clock[q])
+        for k2, v2 in snap.get((sem, val - inc), {}).items():
+            s[k2] = max(v2, s.get(k2, 0))
+        s[sem] = val
+        snap[(sem, val)] = s
+        free[q] = t + (0.06 if dma else cost)
+        done[(sem, val)] = t + (4.0 if dma else cost)
+        for lst, wr in ((writes, True), (reads, False)):
+            for r in lst:
+                buf, lo, hi, tag, bank = region(r)
+                keep = []
+                for a in acc.get(buf, []):
+                    inside = lo <= a[0] and a[1] <= hi and (tag is None or tag == a[2])
+                    if inside and (wr or (not a[6] and a[3] == q and a[4] == sem)):
+                        continue
+                    keep.append(a)
+                keep.append((lo, hi, tag, q, sem, val, wr))
+                acc[buf] = keep
+
+    def op(q, fn, reads, writes, dma=None, cost=0.1):
+        if rec[0] is not None:
+            rec[0].append((q, fn, reads, writes, dma, cost))
+        else:
+            emit(q, fn, reads, writes, dma, cost)
+
+    def record(f, *args):
+        rec[0] = []
+        f(*args)
+        r, rec[0] = rec[0], None
+        return r
+
+    def merge(*streams):
+        st = [[s, 0, b] for s, b in streams]
+        while True:
+            best = None
+            for x in st:
+                if x[1] < len(x[0]) and x[0][x[1]] is None and all(y[1] == len(y[0]) for y in st[2:]):
+                    x[1] += 1
+                if x[1] < len(x[0]) and x[0][x[1]] is not None:
+                    o = x[0][x[1]]
+                    t = needs(o[0], o[2], o[3], o[4])[1] + x[2] + WP * x[1]
+                    if best is None or t < best[0]:
+                        best = (t, x)
+            if best is None:
+                return
+            x = best[1]
+            emit(*x[0][x[1]])
+            x[1] += 1
+
+    scaled = [(T.idn[:, 128 * n:128 * n + 128], ("idn", 128 * n, 128 * n + 128)) for n in range(8)]
+    I16, IH, IMH, IM, IBIG, IW1, IW2, IPEN = scaled
+
+    def cols(ap):
+        n = 1
+        for d in list(ap.shape)[1:]:
+            n *= d
+        return n
+
+    def us(cycles):
+        return 0.03 + 0.00104 * cycles
+
+    def tt(q, out, o, a, ra, b, rb, f):
+        n = cols(out)
+        bank = any(region(r)[4] for r in (ra, rb))
+        op(q, lambda e: e.tensor_tensor(out, a, b, f), [ra, rb], [o], None, us(max(64, n if bank else 2 * n)))
+
+    def ts(out, o, a, ra, s1, s2, f1, f2=None, extra=()):
+        c = us(max(64, cols(out)))
+        if f2 is None:
+            op("V", lambda e: e.tensor_scalar(out, a, s1, None, f1), [ra] + list(extra), [o], None, c)
+        else:
+            op("V", lambda e: e.tensor_scalar(out, a, s1, s2, f1, f2), [ra] + list(extra), [o], None, c)
+
+    def cpy(out, o, a, ra):
+        op("V", lambda e: e.tensor_copy(out, a), [ra], [o], None, us(max(64, cols(out))))
+
+    def act(out, o, a, ra, f, bias=0.0, scale=1.0, extra=(), accum=None, ao=None):
+        c = us(cols(out))
+        if accum is None:
+            op("S", lambda e: e.activation(out, a, f, bias=bias, scale=scale), [ra] + list(extra), [o], None, c)
+        else:
+            op("S", lambda e: e.activation(out, a, f, bias=bias, scale=scale, accum_out=accum), [ra] + list(extra), [o, ao], None, c)
+
+    def mm(out, bank, l, rl, r, rr, start, stop):
+        op("P", lambda e: e.matmul(out, l, r, start, stop), [rl, rr], [(bank,)], None, max(64, cols(r)) * (0.0024 if rl[0][:2] in ("lt", "tt") else 0.0006))
+
+    def dma(q, out, o, a, ra, sem):
+        op(q, lambda e: e.dma_start(out, a), [ra] if ra else [], [o] if o else [], dma=sem)
+
+    def fill(name, v, lo=None, hi=None):
+        if lo is None:
+            op("V", lambda e: e.memset(T[name][:], v), [], [(name,)])
+        else:
+            op("V", lambda e: e.memset(T[name][:, lo:hi], v), [], [(name, lo, hi)])
+
+    def aff(out, src, pat, cmp, base, mult):
+        op("G", lambda e: e.affine_select(T[out][:], T[src][:], pat, cmp, 0.0, base, mult), [(src,)], [(out,)])
+
+    def gather(q, out, oreg, win, wn, n0, n1, off, offreg):
+        src = win[:, n0:n1].indirect(off)
+        c = us(1.5 * cols(out))
+        if q == "V":
+            op("V", lambda e: e.tensor_copy(out, src), [(wn, n0, n1), offreg], [oreg], None, c)
+        else:
+            op("S", lambda e: e.activation(out, src, AF.Copy), [(wn, n0, n1), offreg], [oreg], None, c)
+
+    for i in range(NT):
+        dma("Y", T.n32[:, 384 * i:384 * i + 384], ("n32", 384 * i, 384 * i + 384), T.nxt[:, W * i:W * i + W], None, "d_i%d" % i)
+    dma("S", T.m32[:], ("m32",), T.mem[:], None, "l_m")
+    dma("S", T.cur32[:], ("cur32",), T.cur[:], None, "l_c")
+    dma("S", T.typ32[:], ("typ32",), T.typ[:], None, "l_t")
+    dma("S", T.wb[:], ("wb",), T.w0[:], None, "l_w")
+    for k in range(11, 16):
+        dma("Y", T.inf[k::16, :], ("inf", 0, W, k), T.x[k::16, :], None, "d_fl")
+
+    fill("ones", 1.0)
+    for n in ("wnx", "wv", "wcnt"):
+        fill(n, 1.0)
+    fill("wbit", 16.0)
+    fill("idf", 1.0)
+    fill("sel", 1.0)
+
+    def stamp(t):
+        fill("stl", (BIG if t == 0 else STAMP * t) / 128.0, 128 * t, 128 * t + 128)
+
+    for t in range(5):
+        stamp(t)
+    fill("bo", 1.0)
+    for be in range(2):
+        fill("gt%d" % be, 0.0, 96, 192)
+    op("G", lambda e: e.iota(T.pid[:], [[1, 1]], 0, 1), [], [("pid",)])
+    op("G", lambda e: e.iota(T.pv[:, 0:384], [[1, 384]], 0, 384, allow_small_or_imprecise_dtypes=True), [], [("pv", 0, 384)])
+    aff("idf", "idf", [[-1, 128]], A.is_equal, 0, 1)
+    aff("sel", "sel", [[-4, 32]], A.is_ge, 0, 1)
+    aff("sel", "sel", [[4, 32]], A.is_ge, 3, -1)
+    aff("wnx", "wnx", [[-2, 3], [-16, 8]], A.is_ge, 0, 1)
+    aff("wnx", "wnx", [[2, 3], [16, 8]], A.is_ge, 1, -1)
+    aff("wv", "wv", [[0, 3], [-16, 8]], A.is_ge, -9, 1)
+    aff("wv", "wv", [[0, 3], [16, 8]], A.is_ge, 10, -1)
+    aff("wcnt", "wcnt", [[0, 6], [-16, 8]], A.is_ge, 0, 1)
+    aff("wcnt", "wcnt", [[0, 6], [16, 8]], A.is_ge, 15, -1)
+    op("G", lambda e: e.iota(T.pv[:, 384:1152], [[W, 2], [1, 384]], W, 384, allow_small_or_imprecise_dtypes=True), [], [("pv", 384, 1152)])
+    aff("wbit", "wbit", [[-1, 3], [-16, 8]], A.is_equal, -6, 1)
+    pm, co = T.pm, T.cols
+    ts(pm[:, 0:1], ("pm", 0, 1), T.pid[:], ("pid",), 3, None, A.bitwise_and)
+    ts(pm[:, 1:2], ("pm", 1, 2), T.pid[:], ("pid",), 2, 3, A.arith_shift_right, A.bitwise_and)
+    ts(pm[:, 2:3], ("pm", 2, 3), T.pid[:], ("pid",), 15, None, A.bitwise_and)
+    ts(pm[:, 3:4], ("pm", 3, 4), T.pid[:], ("pid",), 4, None, A.arith_shift_right)
+    for h in range(4):
+        ts(co[:, h:h + 1], ("cols", h, h + 1), pm[:, 0:1], ("pm", 0, 1), h, None, A.is_equal)
+        ts(co[:, 4 + h:5 + h], ("cols", 4 + h, 5 + h), pm[:, 1:2], ("pm", 1, 2), h, None, A.is_equal)
+    ts(co[:, 9:10], ("cols", 9, 10), pm[:, 3:4], ("pm", 3, 4), -W, None, A.mult)
+
+    def split(hi, lo, src, n0, n1, scalar=False):
+        if scalar:
+            act(T[hi][:, n0:n1], (hi, n0, n1), T[src][:, n0:n1], (src, n0, n1), AF.Copy)
+        else:
+            cpy(T[hi][:, n0:n1], (hi, n0, n1), T[src][:, n0:n1], (src, n0, n1))
+        tt("V", T[lo][:, n0:n1], (lo, n0, n1), T[src][:, n0:n1], (src, n0, n1), T[hi][:, n0:n1], (hi, n0, n1), A.subtract)
+
+    def to_inf(k, src, n0):
+        dma("Y", T.inf[k::16, :], ("inf", 0, W, k), T[src][:, n0:n0 + 384], (src, n0, n0 + 384), "d_bi")
+
+    def to_pw(k, i, src, n0):
+        dma("Y", T.pw[k::16, W * i:W * i + W], ("pw", W * i, W * i + W, k), T[src][:, n0:n0 + 384], (src, n0, n0 + 384), "d_pw")
+
+    act(T.pv[:, 0:384], ("pv", 0, 384), T.pv[:, 0:384], ("pv", 0, 384), AF.Identity, bias=co[:, 9:10], extra=[("cols", 9, 10)])
+    for i in range(NT):
+        split("nhi", "nlo", "n32", 384 * i, 384 * i + 384)
+        to_inf(2 * i, "nhi", 384 * i)
+        to_inf(2 * i + 1, "nlo", 384 * i)
+    split("phi", "plo", "pv", 0, 384, True)
+    to_inf(9, "phi", 0)
+    to_inf(10, "plo", 0)
+    ts(T.mi[:, 0:384], ("mi", 0, 384), T.m32[:], ("m32",), 1, None, A.bitwise_and)
+    ts(T.mi[:, 384:768], ("mi", 384, 768), T.m32[:], ("m32",), 2, None, A.bitwise_and)
+    ts(T.bits[:, 768:1152], ("bits", 768, 1152), T.m32[:], ("m32",), 4, None, A.is_ge)
+    ts(T.bits[:, 0:768], ("bits", 0, 768), T.mi[:], ("mi",), 1, None, A.is_ge)
+    for i in range(NT):
+        to_inf(6 + i, "bits", 384 * i)
+    dma("Y", T.xs[:], ("xs",), T.x[:], None, "l_x")
+    act(T.wf[:], ("wf",), T.wb[:], ("wb",), AF.Copy)
+    dma("S", T.f32[:], ("f32",), T.fro[:], None, "l_f")
+
+    cpy(T.lst[:], ("lst",), T.cur32[:], ("cur32",))
+    cpy(T.tf[:], ("tf",), T.typ32[:], ("typ32",))
+    cpy(T.idb[:], ("idb",), T.idf[:], ("idf",))
+    for n, v in enumerate((16.0, 0.5, -0.5, -1.0, float(BIG), W / 2.0, float(W), float(BIG))):
+        ts(T.idn[:, 128 * n:128 * n + 128], ("idn", 128 * n, 128 * n + 128), T.idb[:], ("idb",), v, None, A.mult)
+    tt("V", T.selr[:], ("selr",), T.idf[:, :, 0, :], ("idf",), T.idf[:, :, 1, :], ("idf",), A.add)
+    for h in (2, 3):
+        tt("V", T.selr[:], ("selr",), T.selr[:], ("selr",), T.idf[:, :, h, :], ("idf",), A.add)
+    cpy(T.wx[:, 0:24], ("wx", 0, 24), T.wnx[:], ("wnx",))
+    cpy(T.wx[:, 24:48], ("wx", 24, 48), T.wv[:], ("wv",))
+    for t in range(5, ROUNDS * FINDS + 1):
+        stamp(t)
+    fill("c72", 1.5 * W / 128)
+
+    aff("bo", "bo", [[-16, 8], [0, 16]], A.is_ge, 0, 1)
+    aff("bo", "bo", [[16, 8], [0, 16]], A.is_ge, 15, -1)
+    aff("plw", "bo", [[-16, 8], [0, 16]], A.is_ge, -2, 1)
+    aff("plw", "plw", [[16, 8], [0, 16]], A.is_ge, 3, -1)
+    aff("lm", "bo", [[-1, 128]], A.is_gt, 0, 1)
+    op("G", lambda e: e.iota(T.kc[:], [[16, 8]], 0, 1, allow_small_or_imprecise_dtypes=True), [], [("kc",)])
+    op("G", lambda e: e.iota(T.kio[:], [[1, 128]], 0, 0, allow_small_or_imprecise_dtypes=True), [], [("kio",)])
+    op("G", lambda e: e.iota(T.km[:], [[0, 8], [1, 16]], 0, 0, allow_small_or_imprecise_dtypes=True), [], [("km",)])
+
+    know("G", "l_x", total["l_x"])
+    total["tx"] = 0
+    for t, buf in ((0, "x1"), (1, "x2")):
+        dst, src = T.cores[(rank - 1 - t) % N], T.cores[(rank + 1 + t) % N]
+        rid, pid, _s = topo.addr(dst)
+        rx = "rx%d" % (t + 1)
+        g.remote_dma(T[buf][:], T.xs[:], T.sem[rx], T.sem.tx, pid, rid, topo.mask(core, dst))
+        total["tx"] += len(topo.engines(core, dst))
+        total[rx] = len(topo.engines(src, core))
+        acc[buf] = [(0, 1 << 20, None, "R", rx, total[rx], True)]
+
+    fill("eqm", 1.0)
+    aff("eqm", "eqm", [[1, 16], [0, 8], [-1, 16]], A.is_equal, 0, 0)
+    aff("db", "eqm", [[0, 16], [-16, 8], [0, 16]], A.is_equal, -4, 1)
+    aff("df", "eqm", [[0, 16], [-16, 8], [0, 16]], A.is_ge, -5, 1)
+    aff("df", "df", [[0, 16], [16, 8], [0, 16]], A.is_ge, 6, -1)
+    aff("dp", "eqm", [[0, 16], [-16, 8], [0, 16]], A.is_ge, -2, 1)
+    aff("dp", "dp", [[0, 16], [16, 8], [0, 16]], A.is_ge, 3, -1)
+
+    def later():
+        act(T.pv[:, 384:1152], ("pv", 384, 1152), T.pv[:, 384:1152], ("pv", 384, 1152), AF.Identity, bias=co[:, 9:10], extra=[("cols", 9, 10)])
+        for i in range(1, NT):
+            split("phi", "plo", "pv", 384 * i, 384 * i + 384, True)
+        split("fhi", "flo", "f32", 0, 384)
+        for i in range(NT):
+            for k, (src, n0) in enumerate((("nhi", 384 * i), ("nlo", 384 * i), ("phi", 384 * i), ("plo", 384 * i), ("bits", 384 * i), ("fhi", 0), ("flo", 0))):
+                to_pw(k, i, src, n0)
+        for i in range(NT):
+            for k in range(7, 16):
+                dma("Y", T.pw[k::16, W * i:W * i + W], ("pw", W * i, W * i + W, k), T.x[k::16, :], None, "d_pf")
+        cpy(co[:, 8:9], ("cols", 8, 9), pm[:, 2:3], ("pm", 2, 3))
+        ts(co[:, 10:11], ("cols", 10, 11), pm[:, 2:3], ("pm", 2, 3), 2, None, A.is_lt)
+        ts(co[:, 11:12], ("cols", 11, 12), pm[:, 3:4], ("pm", 3, 4), -16, None, A.mult)
+        ts(T.kc[:], ("kc",), T.kc[:], ("kc",), co[:, 11:12], None, A.add, extra=[("cols", 11, 12)])
+        ts(T.km[:], ("km",), T.km[:], ("km",), co[:, 8:9], None, A.is_equal, extra=[("cols", 8, 9)])
+        ts(T.kch[:], ("kch",), T.kc[:], ("kc",), 0.5, None, A.add)
+        ts(T.dumc[:, 0:8], ("dumc", 0, 8), T.kc[:], ("kc",), 3 * W, None, A.add)
+        ts(T.dumc[:, 8:16], ("dumc", 8, 16), T.kc[:], ("kc",), 3 * W + CAP, None, A.add)
+        ts(T.lm[:], ("lm",), T.lm[:], ("lm",), -1.0, None, A.mult)
+        fill("rt", 65536.0, 64, 72)
+        fill("ra", 16384.0, K, K + 16)
+        fill("rb", 16384.0, K, K + 16)
+
+    def masks(out, obuf, n0, n1, src, sreg, nscalar):
+        for h in range(4):
+            o = (obuf, n0, n1, h)
+            if h < nscalar:
+                act(out(h), o, src, sreg, AF.Copy, scale=co[:, h:h + 1], extra=[("cols", h, h + 1)])
+            else:
+                ts(out(h), o, src, sreg, co[:, h:h + 1], None, A.mult, extra=[("cols", h, h + 1)])
+
+    def types_in():
+        for be in range(2):
+            for h in range(4):
+                ts(T.ttl[:, 128 * be + h:128 * be + 128:4], ("ttl", 128 * be, 128 * be + 128, h), T.tf[:, 32 * be:32 * be + 32], ("tf",), co[:, 4 + h:5 + h], None, A.mult, extra=[("cols", 4 + h, 5 + h)])
+            O, ob = T["b%d" % (6 + be)], "b%d" % (6 + be)
+            mm(O[:, 0:32], ob, T.ttl[:, 128 * be:128 * be + 128], ("ttl", 128 * be, 128 * be + 128), T.selr[:], ("selr",), True, True)
+            ac, gt = "ac%d" % be, "gt%d" % be
+            for i in range(NT):
+                act(T[ac][:, 32 * i:32 * i + 32], (ac, 32 * i, 32 * i + 32), O[:, 0:32], (ob,), AF.Abs, bias=-float(i))
+            act(T[gt][:, 0:96], (gt, 0, 96), T[ac][:], (ac,), AF.Sign, bias=0.5, scale=-1.0)
+
+    def pick(be, s0, own="gt%d"):
+        st, t, u = T["st%d" % be], T["tt%d" % be], T["tu%d" % be]
+        P, pb = T["b%d" % (4 + be)], "b%d" % (4 + be)
+        mm(P[:, 128:224], pb, *IPEN, T[own % be][:, 0:96], (own % be, 0, 96), True, True)
+        tt("V", t[:], ("tt%d" % be,), P[:, 128:224], (pb,), st[:, s0:s0 + 96], ("st%d" % be, s0, s0 + 96), A.add)
+        tt("V", u[:], ("tu%d" % be,), t[:, 0:32], ("tt%d" % be,), t[:, 32:64], ("tt%d" % be,), A.max)
+
+    def next_list(be, more=None, own="gt%d"):
+        t, u, mp, lt = T["tt%d" % be], T["tu%d" % be], T["mp%d" % be], T["lt%d" % be]
+        pick(be, 0, own)
+        tt("V", mp[:], ("mp%d" % be,), u[:], ("tu%d" % be,), t[:, 64:96], ("tt%d" % be,), A.max)
+        masks(lambda h: lt[:, :, h, :], "lt%d" % be, 0, 128, mp[:], ("mp%d" % be,), MS)
+        if more:
+            more()
+        O, ob = T["b%d" % (6 + be)], "b%d" % (6 + be)
+        mm(O[:, 0:32], ob, lt[:], ("lt%d" % be,), T.sel[:], ("sel",), True, True)
+        oi, oj, off = "oi%d" % be, "oj%d" % be, "off%d" % be
+        cpy(T[oi][:], (oi,), O[:, 0:32], (ob,))
+        ts(T[oj][:], (oj,), T[oi][:], (oi,), STAMP - 1, None, A.bitwise_and)
+        cpy(T[off][:], (off,), T[oj][:], (oj,))
+
+    def round_start(be, t):
+        X, xb, st = T["b%d" % be], "b%d" % be, "st%d" % be
+        n = 96 if t else 192
+        mm(X[:, 0:n], xb, T.stl[:, 0:128], ("stl", 0, 128), T.ones[:, 0:n], ("ones",), True, False)
+        for i in range(NT):
+            buf = ("rw%d" if i % 2 == 0 else "ge%d") % be
+            l0 = 64 * i + 32 * be
+            q = "S" if (i + be) % 2 == 0 else "V"
+            lst = (T.lst[:, l0:l0 + 32], ("lst",))
+            if t:
+                gather(q, T[buf][:], (buf,), T.pw, "pw", 0, 3 * W, *lst)
+            else:
+                gather(q, T[buf][:], (buf,), T.inf, "inf", 0, W, *lst)
+            for b in range(4):
+                end = i == NT - 1 and b == 3
+                w0 = 0 if t else 8 * i
+                mm(X[:, 32 * i + b:32 * i + 32:4], xb, T[buf][:, b::4], (buf,), T.wx[:, w0:w0 + 8], ("wx",), False, end and t > 0)
+                if t == 0:
+                    mm(X[:, 96 + 32 * i + b:128 + 32 * i:4], xb, T[buf][:, b::4], (buf,), T.wx[:, 24 + 8 * i:32 + 8 * i], ("wx",), False, end)
+        cpy(T[st][:, 0:n], (st, 0, n), X[:, 0:n], (xb,))
+        next_list(be)
+
+    def find(be, q, last):
+        ge, rw, off, gt = "ge%d" % be, "rw%d" % be, "off%d" % be, "gt%d" % be
+        sg, ab, st = "sg%d" % be, "ab%d" % be, "st%d" % be
+        (X, xb), (Y, yb), (Z, zb) = [(T["b%d" % (n + be)], "b%d" % (n + be)) for n in (0, 2, 4)]
+        src = T.xs[:, 0:W].indirect(T[off][:])
+        op("V", lambda e: e.tensor_tensor(T[ge][:], src, T.wf[:, H * be:H * be + H], A.is_ge), [("xs",), (off,), ("wf", H * be, H * be + H)], [(ge,)], None, us(1.5 * H))
+        gather("S", T[rw][:], (rw,), T.inf, "inf", 0, W, T[off][:], (off,))
+        mm(Y[:, 0:192], yb, *I16, T[gt][:], (gt,), True, False)
+        mm(X[:, 0:192], xb, T.stl[:, 128 * q:128 * q + 128], ("stl", 128 * q, 128 * q + 128), T.ones[:], ("ones",), True, False)
+        mm(Z[:, 0:96], zb, *IH, T[gt][:, 0:96], (gt, 0, 96), True, False)
+        mm(Z[:, 0:32], zb, *IMH, T[gt][:, 64:96], (gt, 0, 96), False, False)
+        mm(Z[:, 32:96], zb, *IMH, T[gt][:, 0:64], (gt, 0, 96), False, False)
+        for b in range(4):
+            mm(Y[:, b:96:4], yb, T[rw][:, b::4], (rw,), T.wbit[:], ("wbit",), False, False)
+        for b in range(4):
+            mm(Y[:, b:192:4], yb, T[ge][:, b::4], (ge,), T.wcnt[:], ("wcnt",), False, b == 3)
+        for b in range(4):
+            mm(X[:, b:192:4], xb, T[rw][:, b::4], (rw,), T.wx[:], ("wx",), False, False)
+        act(T[sg][:], (sg,), Y[:, 0:192], (yb,), AF.Sign, bias=-8.5)
+        mm(Z[:, 0:96], zb, *IM, T[sg][:, 96:192], (sg,), False, True)
+        mm(X[:, 0:96], xb, *IBIG, T[sg][:, 0:96], (sg,), False, False)
+        mm(X[:, 96:192], xb, *IBIG, T[sg][:, 0:96], (sg,), False, True)
+        act(T[ab][:], (ab,), Z[:, 0:96], (zb,), AF.Abs)
+        act(T[gt][:, 0:96], (gt, 0, 96), T[ab][:], (ab,), AF.Sign, bias=-1.5)
+        tt("V", T[st][:, 0:96], (st, 0, 96), X[:, 0:96], (xb,), T[st][:, 0:96], (st, 0, 96), A.max)
+
+        def cursors_too():
+            tt("V", T[st][:, 96:192], (st, 96, 192), X[:, 96:192], (xb,), T[st][:, 96:192], (st, 96, 192), A.max)
+        if last:
+            cursors_too()
+        else:
+            next_list(be, cursors_too, "ab%d")
+
+    def finds(be, t):
+        round_start(be, t)
+        for q in range(FINDS):
+            find(be, FINDS * t + q + 1, q == FINDS - 1)
+        rec[0].append(None)
+        places(be)
+
+    def diag(bank, c0, c1, d, src, s0, s1):
+        for i in range(16):
+            mm(T[bank][:, c0:c1], bank, T[d][:, i, :, :], (d,), T[src][:, s0 + i:s1:16], (src, s0, s1), i == 0, i == 15)
+
+    def slot_list(bank, src, stop):
+        P = T[bank]
+        mm(P[:, 128:256], bank, T[src][:], (src,), T.bo[:], ("bo",), True, True)
+        tt("V", T.lk[:], ("lk",), P[:, 128:256], (bank,), T.km[:], ("km",), A.mult)
+        mm(P[:, 0:8], bank, T.lk[:], ("lk",), T.bo[:, 0:128:16], ("bo",), True, stop)
+
+    def places(be):
+        st, gt, tb, ub, ac, mp = [n % be for n in ("st%d", "gt%d", "tt%d", "tu%d", "ac%d", "mp%d")]
+        Y, yb, O, ob = T["b%d" % (2 + be)], "b%d" % (2 + be), T["b%d" % (6 + be)], "b%d" % (6 + be)
+        a, b = 64 * be, 64 * be + 64
+        mm(Y[:, 0:64], yb, T.c72[:], ("c72",), T.ones[:, 0:64], ("ones",), True, False)
+        for s in range(2):
+            mm(Y[:, 32 * s:32 * s + 32], yb, *IW1, T[gt][:, 0:32], (gt, 0, 96), False, False)
+            mm(Y[:, 32 * s:32 * s + 32], yb, *IW2, T[gt][:, 32:64], (gt, 0, 96), False, s == 1)
+        tt("V", T[ac][:, 0:32], (ac, 0, 32), T[st][:, 96:128], (st,), T[gt][:, 64:96], (gt, 0, 96), A.mult)
+        tt("V", T[ac][:, 32:96], (ac, 32, 96), T[st][:, 128:192], (st,), T[gt][:, 0:64], (gt, 0, 96), A.mult)
+        pick(be, 96)
+        tt("V", T.mz[:, a:a + 32], ("mz", a, a + 32), T[ub][:], (ub,), T[tb][:, 64:96], (tb,), A.max)
+        tt("V", T[mp][:], (mp,), T[ac][:, 0:32], (ac,), T[ac][:, 32:64], (ac,), A.max)
+        tt("V", T.mz[:, a + 32:b], ("mz", a + 32, b), T[mp][:], (mp,), T[ac][:, 64:96], (ac,), A.max)
+        cpy(T.mzi[:, a:b], ("mzi", a, b), T.mz[:, a:b], ("mz", a, b))
+        ts(T.mzi[:, 128 + a:128 + b], ("mzi", 128 + a, 128 + b), T.mzi[:, a:b], ("mzi", a, b), STAMP - 1, None, A.bitwise_and)
+        tt("V", T.mp4[:, 16 * be:16 * be + 16, :], ("mp4", a, b), Y[:, 0:64], (yb,), T.mzi[:, 128 + a:128 + b], ("mzi", 128 + a, 128 + b), A.add)
+        masks(lambda h: T.lte[:, 16 * be:16 * be + 16, h, :], "lte", 256 * be, 256 * be + 256, T.mp4[:, 16 * be:16 * be + 16, :], ("mp4", a, b), 2)
+        for s in range(2):
+            n = 16 * be + 8 * s
+            mm(O[:, 32 * s:32 * s + 32], ob, T.lte[:, n:n + 8, :, :], ("lte", 256 * be, 256 * be + 256), T.sel[:], ("sel",), True, True)
+        cpy(T.ot[:, a:b], ("ot", a, b), O[:, 0:64], (ob,))
+        gather("S" if be else "V", T.ra[:, H * be:H * be + H], ("ra", H * be, H * be + H), T.pw, "pw", 0, 3 * W, T.ot[:, a:a + 32], ("ot", a, b))
+        cpy(T.otf[:, a // 2:b // 2], ("otf", a // 2, b // 2), O[:, 0:32], (ob,))
+        tt("V", T.nq[:, a // 2:b // 2], ("nq", a // 2, b // 2), O[:, 32:64], (ob,), T.otf[:, a // 2:b // 2], ("otf", a // 2, b // 2), A.not_equal)
+
+    def swap(last):
+        gather("S", T.rb[:, H:K], ("rb", H, K), T.pw, "pw", 0, 3 * W, T.ot[:, 96:128], ("ot", 64, 128))
+        gather("V", T.rb[:, 0:H], ("rb", 0, H), T.pw, "pw", 0, 3 * W, T.ot[:, 32:64], ("ot", 0, 64))
+        diag("b2", 0, 64, "db", "ra", 0, K)
+        tt("V", T.wt[:], ("wt",), T.b2[:, 0:64], ("b2",), T.nq[:], ("nq",), A.mult)
+        op("V", lambda e: e.tensor_tensor_scan(T.pc[:], T.ones[:, 0:64], T.wt[:], 0.0, A.mult, A.add), [("ones",), ("wt",)], [("pc",)])
+        mm(T.b3[:, 0:64], "b3", T.bo[:], ("bo",), T.pc[:], ("pc",), True, True)
+        mm(T.b2[:, 64:128], "b2", T.bo[:], ("bo",), T.pc[:], ("pc",), True, False)
+        mm(T.b2[:, 64:128], "b2", T.lm[:], ("lm",), T.wt[:], ("wt",), False, True)
+        cpy(T.rt[:, 0:64], ("rt", 0, 64), T.b2[:, 64:128], ("b2",))
+        for n in range(8):
+            act(T.junk[:, 64 * n:64 * n + 64], ("junk", 64 * n, 64 * n + 64), T.b3[:, 0:64], ("b3",), AF.Sign, bias=T.kch[:, n:n + 1], scale=-1.0, extra=[("kch",)], accum=T.ck[:, n:n + 1], ao=("ck", n, n + 1))
+        ts(T.ckl[:], ("ckl",), T.ck[:], ("ck",), 0.5, 32.0, A.mult, A.add)
+        src = T.rt[:, 0:72].indirect(T.ckl[:])
+        op("V", lambda e: e.tensor_tensor(T.le[:], src, T.kio[:], A.is_le), [("rt",), ("ckl",), ("kio",)], [("le",)])
+        ts(T.ckb[:], ("ckb",), T.ck[:], ("ck",), 0.5, 32.0, A.mult, A.add)
+        slot_list("b2", "le", False)
+        mm(T.b2[:, 0:8], "b2", *I16, T.ckb[:], ("ckb",), False, True)
+        cpy(T.jk[:], ("jk",), T.b2[:, 0:8], ("b2",))
+        gather("V", T.sab[:, 0:128], ("sab", 0, 128), T.ra, "ra", 0, K + 16, T.jk[:], ("jk",))
+        gather("S", T.sab[:, 128:256], ("sab", 128, 256), T.rb, "rb", 0, K + 16, T.jk[:], ("jk",))
+        mm(T.b3[:, 0:256], "b3", T.plw[:], ("plw",), T.sab[:], ("sab",), True, True)
+        diag("b6", 0, 16, "dp", "sab", 0, 256)
+        cpy(T.plr[:], ("plr",), T.b3[:, 0:256], ("b3",))
+        cpy(T.plt[:], ("plt",), T.b6[:, 0:16], ("b6",))
+        for n in range(16):
+            a = 256 * (n % NEQ)
+            ts(T.eq[:, a:a + 256], ("eq", a, a + 256), T.plr[:], ("plr",), T.plt[:, n:n + 1], None, A.is_equal, extra=[("plt",)])
+            for s in range(2):
+                mm(T.b7[:, 0:128], "b7", T.bo[:], ("bo",), T.eq[:, a + 128 * s:a + 128 * s + 128], ("eq", a, a + 256), n == 0 and s == 0, n == 15 and s == 1)
+        tt("V", T.dab[:], ("dab",), T.sab[:, 128:256], ("sab",), T.sab[:, 0:128], ("sab",), A.subtract)
+        tt("V", T.pd[:], ("pd",), T.plt[:], ("plt",), T.dumc[:], ("dumc",), A.subtract)
+        ts(T.cb[:], ("cb",), T.b7[:, 0:128], ("b7",), 2.0, 1.0 / 16, A.is_equal, A.mult)
+        ts(T.cp[:], ("cp",), T.b7[:, 0:128], ("b7",), 2.0, co[:, 10:11], A.is_equal, A.mult, extra=[("cols", 10, 11)])
+        slot_list("b3", "cb", True)
+        tt("V", T.dmv[:], ("dmv",), T.dab[:], ("dab",), T.cp[:], ("cp",), A.mult)
+        for s in range(2):
+            tt("V", T.of[:, 8 * s:8 * s + 8], ("of", 8 * s, 8 * s + 8), T.b3[:, 0:8], ("b3",), T.pd[:, 8 * s:8 * s + 8], ("pd",), A.mult)
+        tt("V", T.nv[:, 0:128], ("nv", 0, 128), T.sab[:, 0:128], ("sab",), T.dmv[:], ("dmv",), A.add)
+        tt("V", T.of[:, 16:32], ("of", 16, 32), T.of[:, 0:16], ("of", 0, 16), T.dumc[:], ("dumc",), A.add)
+        tt("V", T.nv[:, 128:256], ("nv", 128, 256), T.sab[:, 128:256], ("sab",), T.dmv[:], ("dmv",), A.subtract)
+        cpy(T.ofl[:], ("ofl",), T.of[:, 16:32], ("of", 16, 32))
+        out = T.pw[:, 0:3 * W + 2 * CAP].indirect(T.ofl[:])
+        op("V", lambda e: e.tensor_copy(out, T.nv[:]), [("nv",), ("ofl",)], [("pw",)], None, 1.0)
+        if not last:
+            for i in range(NT):
+                for k in range(2):
+                    dma("Y", T.inf[2 * i + k::16, :], ("inf", 0, W, 2 * i + k), T.pw[k::16, W * i:W * i + W], ("pw", W * i, W * i + W, k), "d_rb")
+            return
+        dma("Y", T.yh[:], ("yh",), T.pw[0::16, 0:3 * W], ("pw", 0, 3 * W, 0), "d_y1")
+        dma("Y", T.yl[:], ("yl",), T.pw[1::16, 0:3 * W], ("pw", 0, 3 * W, 1), "d_y1")
+        parts = [(384 * i, 384 * i + 384, ("b3", "b6", "b7")[i]) for i in range(NT)]
+        for a, b, bank in parts:
+            mm(T[bank][:, 0:384], bank, T.idb[:], ("idb",), T.yh[:, a:b], ("yh",), True, False)
+            mm(T[bank][:, 0:384], bank, T.idb[:], ("idb",), T.yl[:, a:b], ("yl",), False, True)
+        for n, (a, b, bank) in enumerate(parts):
+            if n == 1:
+                act(T.yf[:, a:b], ("yf", a, b), T[bank][:, 0:384], (bank,), AF.Copy)
+            else:
+                cpy(T.yf[:, a:b], ("yf", a, b), T[bank][:, 0:384], (bank,))
+        dma("Y", T.yn[:], None, T.yf[:], ("yf",), "d_yn1")
+
+    def cursors(last):
+        for be in range(2):
+            for h in range(4):
+                act(T.ltc[:, 24 * be:24 * be + 24, h, :], ("ltc", 384 * be, 384 * be + 384, h), T["st%d" % be][:, 96:192], ("st%d" % be,), AF.Copy, scale=co[:, h:h + 1], extra=[("cols", h, h + 1)])
+        for be in range(2):
+            for i in range(NT):
+                n = 3 * be + i
+                mm(T.b5[:, 64 * i + 32 * be:64 * i + 32 * be + 32], "b5", T.ltc[:, 8 * n:8 * n + 8, :, :], ("ltc", 384 * be, 384 * be + 384), T.sel[:], ("sel",), True, True)
+        cpy(T.ci[:, 0:192], ("ci", 0, 192), T.b5[:, 0:192], ("b5",))
+        ts(T.ci[:, 192:384], ("ci", 192, 384), T.ci[:, 0:192], ("ci", 0, 192), STAMP - 1, None, A.bitwise_and)
+        if last:
+            cpy(T.ycf[:], ("ycf",), T.ci[:, 192:384], ("ci", 192, 384))
+            dma("Y", T.yc[:], None, T.ycf[:], ("ycf",), "d_yc")
+        else:
+            for i in range(NT):
+                a, b = 64 * i, 64 * i + 64
+                ts(T.lst[:, a:b], ("lst", a, b), T.ci[:, 192 + a:192 + b], ("ci", 192, 384), W * i, None, A.add)
+
+    def pull(t, last):
+        diag("b4", 64, 128, "df", "ra", 0, K)
+        cpy(T.kl[:], ("kl",), T.b4[:, 64:128], ("b4",))
+        xn = "x%d" % (t + 1)
+        for be in range(2):
+            a, b = H * be, H * be + H
+            ysrc = T[xn][:, 0:W].indirect(T.kl[:, 32 * be:32 * be + 32])
+            op("V", lambda e, ysrc=ysrc, a=a, b=b: e.tensor_tensor(T.dd[:, a:b], ysrc, T.wf[:, a:b], A.subtract), [(xn,), ("kl",), ("wf", a, b)], [("dd", a, b)], None, us(1.5 * H))
+            D, dn = T["b%d" % be], "b%d" % be
+            ts(D[:], (dn,), T.dd[:, a:b], ("dd", a, b), 8.0, -8.0, A.min, A.max)
+            tt("V", T.wf[:, a:b], ("wf", a, b), D[:], (dn,), T.wf[:, a:b], ("wf", a, b), A.add)
+            if last:
+                dma("S", T.yw[:, a:b], None, T.wf[:, a:b], ("wf", a, b), "d_yw%d" % be)
+
+    types_in()
+    for t in range(ROUNDS):
+        last = t == ROUNDS - 1
+        streams = [(record(finds, 0, t), 0.0), (record(finds, 1, t), FB)]
+        if t == 0:
+            streams.append((record(later), LB))
+        merge(*streams)
+        merge((record(swap, last), 0.0), (record(cursors, last), CB), (record(pull, t, last), PB))
+    for s in sorted(total):
+        know("G", s, total[s])

@@ -1,56 +1,54 @@
-from concourse.mybir import AluOpType, ActivationFunctionType
+from concourse.mybir import AluOpType, ActivationFunctionType, AxisListType
 
 A = AluOpType
 AF = ActivationFunctionType
 W, K, NT, ROUNDS, FINDS, CAP = 6144, 1024, 3, 2, 8, 128
 H = K // 2
-STAMP = 8192
-BIG = 1 << 18
+Q = W // 4
+TS = 8192
+PW = 2 * TS + W
+B, B2, STAMP = 16384.0, 32768.0, 16384.0
 NEQ = 4
-MS = 3
-FB, CB, PB, LB = 0.0, 0.3, 0.4, 0.4
-WP = 0.001
+MS = 2
+NV = 3
+XA = 2048
+FB = 1.5
+SOON = 4.0
+WAKE, FLY, RATE = 0.05, 2.0, 3e5
 SB, BF, FP, I32, U16 = "sbuf", "bfloat16", "float32", "int32", "uint16"
 SCRATCH = {
-    "xs": (SB, [128, W], BF), "x1": (SB, [128, W], BF), "x2": (SB, [128, W], BF),
-    "inf": (SB, [128, W], BF), "pw": (SB, [128, 3 * W + 2 * CAP], BF),
-    "wb": (SB, [128, K], BF), "wf": (SB, [128, K], FP), "dd": (SB, [128, K], FP),
-    "n32": (SB, [128, 1152], I32), "nhi": (SB, [128, 1152], BF), "nlo": (SB, [128, 1152], BF),
-    "m32": (SB, [128, 384], I32), "mi": (SB, [128, 768], I32), "bits": (SB, [128, 1152], BF),
-    "f32": (SB, [128, 384], I32), "fhi": (SB, [128, 384], BF), "flo": (SB, [128, 384], BF),
-    "pv": (SB, [128, 1152], FP), "phi": (SB, [128, 1152], BF), "plo": (SB, [128, 1152], BF),
-    "cur32": (SB, [128, 192], I32), "typ32": (SB, [128, 64], I32), "tf": (SB, [128, 64], FP),
-    "lst": (SB, [128, 192], U16), "ci": (SB, [128, 384], I32), "ycf": (SB, [128, 192], FP),
-    "ones": (SB, [128, 192], BF), "idf": (SB, [128, 8, 4, 4], FP), "idb": (SB, [128, 128], BF), "idn": (SB, [128, 8 * 128], BF),
-    "stl": (SB, [128, 128 * (ROUNDS * FINDS + 1)], BF), "c72": (SB, [128, 128], BF),
-    "wnx": (SB, [128, 24], BF), "wv": (SB, [128, 24], BF), "wx": (SB, [128, 48], BF), "wbit": (SB, [128, 24], BF), "wcnt": (SB, [128, 48], BF),
-    "sel": (SB, [128, 32], FP), "selr": (SB, [128, 32], FP),
-    "pid": (SB, [128, 1], I32), "pm": (SB, [128, 4], I32), "cols": (SB, [128, 16], FP),
-    "bo": (SB, [128, 128], BF), "lm": (SB, [128, 128], BF), "plw": (SB, [128, 128], BF), "km": (SB, [128, 128], BF),
-    "eqm": (SB, [128, 16, 8, 16], BF), "dp": (SB, [128, 16, 8, 16], BF), "db": (SB, [128, 16, 8, 16], BF), "df": (SB, [128, 16, 8, 16], BF),
-    "kc": (SB, [128, 8], FP), "kch": (SB, [128, 8], FP), "dumc": (SB, [128, 16], FP), "kio": (SB, [128, 128], FP),
-    "ttl": (SB, [128, 256], FP), "eq": (SB, [128, 256 * NEQ], BF), "lk": (SB, [128, 128], BF),
-    "mz": (SB, [128, 128], FP), "mzi": (SB, [128, 256], I32), "mp4": (SB, [128, 32, 4], FP),
-    "lte": (SB, [128, 32, 4, 4], FP), "ltc": (SB, [128, 48, 4, 4], FP),
-    "ot": (SB, [128, 128], U16), "otf": (SB, [128, 64], FP), "nq": (SB, [128, 64], BF),
-    "ra": (SB, [128, K + 16], BF), "rb": (SB, [128, K + 16], BF),
-    "wt": (SB, [128, 64], BF), "pc": (SB, [128, 64], BF), "rt": (SB, [128, 72], FP), "junk": (SB, [128, 512], BF),
-    "ck": (SB, [128, 8], FP), "ckl": (SB, [128, 8], U16), "ckb": (SB, [128, 8], BF), "le": (SB, [128, 128], BF), "jk": (SB, [128, 8], U16),
-    "sab": (SB, [128, 256], BF), "plr": (SB, [128, 256], U16), "plt": (SB, [128, 16], FP),
-    "cb": (SB, [128, 128], BF), "cp": (SB, [128, 128], FP), "dab": (SB, [128, 128], FP), "dmv": (SB, [128, 128], FP),
-    "nv": (SB, [128, 256], BF), "pd": (SB, [128, 16], FP), "of": (SB, [128, 32], FP), "ofl": (SB, [128, 16], U16),
-    "kl": (SB, [128, 64], U16), "yh": (SB, [128, 1152], BF), "yl": (SB, [128, 1152], BF), "yf": (SB, [128, 1152], FP),
+    "xs": (SB, [128, W], BF), "x1": (SB, [128, W], BF), "x2": (SB, [128, W], BF), "inf": (SB, [128, W], BF),
+    "pwb": (SB, [128, PW], BF), "pwf": (SB, [128, PW], FP),
+    "wf": (SB, [128, K], FP), "n32": (SB, [128, Q], I32), "m32": (SB, [128, 384], I32),
+    "cur32": (SB, [128, 3, 2, 32], I32), "typ32": (SB, [128, 64], I32), "lst": (SB, [128, 192], U16), "ycf": (SB, [128, 3, 2, 32], FP),
+    "ones": (SB, [128, 384], BF), "id1": (SB, [128, 8, 4, 4], BF), "idn": (SB, [128, 4, 128], BF), "stl": (SB, [128, FINDS, 128], BF),
+    "wr": (SB, [128, 8, 8, 3], BF), "wg": (SB, [128, 72], BF), "sel": (SB, [128, 32], FP), "tri": (SB, [128, 64], FP), "selr": (SB, [128, 32], BF),
+    "rs3": (SB, [128, 288], FP), "r16": (SB, [128, 256], FP), "kz": (SB, [128, 32, 4], BF),
+    "pid": (SB, [128, 1], I32), "pm": (SB, [128, 8], I32), "cols": (SB, [128, 16], FP), "ttl": (SB, [128, 64, 4], BF),
+    "bo": (SB, [128, 128], BF), "bof": (SB, [128, 128], FP), "lm": (SB, [128, 128], BF), "wn": (SB, [128, 8, 16], BF),
+    "km": (SB, [128, 256], BF), "k3": (SB, [128, 128], BF),
+    "kc": (SB, [128, 8], FP), "kch": (SB, [128, 8], FP), "dum": (SB, [128, 32], FP), "kio": (SB, [128, 128], FP),
+    "pl": (SB, [128, 2, 72], FP), "wp": (SB, [128, 2, 64], BF), "rt": (SB, [128, 72], FP),
+    "ck": (SB, [128, 8], FP), "ckl": (SB, [128, 8], U16), "oh": (SB, [128, 128], FP), "pr": (SB, [128, 256], FP),
+    "mk": (SB, [128, 256], FP), "plt": (SB, [128, 256], FP), "plr": (SB, [128, 256], U16), "eq": (SB, [128, 256 * NEQ], BF),
+    "si": (SB, [128, 32], I32), "sl": (SB, [128, 16], U16), "ab": (SB, [128, 128], FP), "gs": (SB, [128, 256], BF), "gz": (SB, [128, 256], BF),
+    "nvb": (SB, [128, 256], BF), "nvf": (SB, [128, 256], FP), "lk": (SB, [128, 128], BF),
+    "pd": (SB, [128, 16], FP), "of": (SB, [128, 32], FP), "ofl": (SB, [128, 16], U16),
+    "mi": (SB, [128, 128], I32), "ml": (SB, [128, 64], U16), "kl": (SB, [128, 64], U16),
 }
+ROOMS = {"fm": ("pwb", 0), "vr": ("pwb", 1152), "wb": ("pwb", 2 * TS), "nhi": ("pwb", W + 2 * CAP), "nlo": ("pwb", TS + W),
+         "pv": ("pwf", W + 2 * CAP), "dd": ("pwf", TS + W)}
 for _b in range(2):
-    for _n, _s, _d in (("ge", [128, H], BF), ("rw", [128, H], BF), ("off", [128, 32], U16), ("st", [128, 192], FP), ("gt", [128, 192], BF),
-                       ("sg", [128, 192], BF), ("ab", [128, 96], BF), ("ac", [128, 96], FP), ("tt", [128, 96], FP),
-                       ("tu", [128, 32], FP), ("mp", [128, 8, 4], FP), ("lt", [128, 8, 4, 4], FP), ("oi", [128, 32], I32), ("oj", [128, 32], I32)):
+    for _n, _s, _d in (("ge", [128, H], BF), ("rw", [128, H], BF), ("off", [128, 32], U16), ("st", [128, 192], FP), ("sg", [128, 96, 3], BF),
+                       ("tb", [128, 288], FP), ("sc", [128, 288], FP), ("lt", [128, 8, 4, 4], FP), ("lte", [128, 24, 4, 4], FP),
+                       ("ltc", [128, 8, 4, 12], FP), ("ci", [128, 288], I32), ("cf", [128, 96], FP)):
         SCRATCH["%s%d" % (_n, _b)] = (SB, _s, _d)
 for _i in range(8):
-    SCRATCH["b%d" % _i] = ("psum", [128, 512], FP)
+    SCRATCH["b%d" % _i] = ("psum", [128, 128, 4], FP)
 ENG = {"V": "cv", "S": "cs", "P": "cp_", "G": "cg"}
-DMAS = ["l_m", "l_c", "l_t", "l_x", "l_w", "l_f", "d_i0", "d_i1", "d_i2", "d_bi", "d_fl", "d_pf", "d_pw", "d_rb", "d_y1", "d_yc", "d_yw0", "d_yw1", "d_yn1"]
+DMAS = ["l_n", "l_m", "l_c", "l_t", "l_x", "l_w", "d_bi", "d_pb", "d_pf", "d_rb", "d_yc", "d_yw0", "d_yw1", "d_yn"]
 SEMAPHORES = sorted(ENG.values()) + DMAS + ["rx1", "rx2", "tx"]
+PLANS = {}
 
 
 def rank_program(g, core, T, topo):
@@ -63,9 +61,9 @@ def rank_program(g, core, T, topo):
     total = {}
     snap = {}
     acc = {}
-    free = {q: 0.0 for q in queues}
-    done = {}
-    rec = [None]
+    calls = []
+
+    late = [0.0]
 
     def know(q, sem, val):
         c = clock[q]
@@ -85,7 +83,6 @@ def rank_program(g, core, T, topo):
 
     def needs(q, reads, writes, dma):
         need = {}
-        t = free[q]
         for lst, wr in ((reads, False), (writes, True)):
             for r in lst:
                 buf, lo, hi, tag, bank = region(r)
@@ -98,14 +95,15 @@ def rank_program(g, core, T, topo):
                     if same and (q == "P" or not a[6]):
                         continue
                     need[a[4]] = max(need.get(a[4], 0), a[5])
-                    t = max(t, done.get((a[4], a[5]), 0.0) + 0.06)
-        return need, t
+        return need
 
     def emit(q, fn, reads, writes, dma, cost):
-        need, t = needs(q, reads, writes, dma)
+        need = needs(q, reads, writes, dma)
         for s in sorted(need):
             know(q, s, total[s] if s in DMAS else need[s])
         ins = fn(queues[q])
+        if dma == "tx":
+            return
         sem, inc = (dma, 16) if dma else (ENG[q], 1)
         ins.then_inc(T.sem[sem], inc)
         total[sem] = total.get(sem, 0) + inc
@@ -115,8 +113,6 @@ def rank_program(g, core, T, topo):
             s[k2] = max(v2, s.get(k2, 0))
         s[sem] = val
         snap[(sem, val)] = s
-        free[q] = t + (0.06 if dma else cost)
-        done[(sem, val)] = t + (4.0 if dma else cost)
         for lst, wr in ((writes, True), (reads, False)):
             for r in lst:
                 buf, lo, hi, tag, bank = region(r)
@@ -130,37 +126,74 @@ def rank_program(g, core, T, topo):
                 acc[buf] = keep
 
     def op(q, fn, reads, writes, dma=None, cost=0.1):
-        if rec[0] is not None:
-            rec[0].append((q, fn, reads, writes, dma, cost))
-        else:
-            emit(q, fn, reads, writes, dma, cost)
+        calls.append((q, fn, reads, writes, dma, cost, late[0]))
 
-    def record(f, *args):
-        rec[0] = []
-        f(*args)
-        r, rec[0] = rec[0], None
-        return r
+    def plan():
+        seen, before, g0 = {}, [], None
+        for n, (q, _f, reads, writes, dm, cost, _l) in enumerate(calls):
+            dep = {}
+            for lst, wr in ((reads, False), (writes, True)):
+                for r in lst:
+                    buf, lo, hi, tag, bank = region(r)
+                    for a in seen.get((buf, True), []) + (seen.get((buf, False), []) if wr or bank else []):
+                        same = calls[a[4]][0] == q and not dm and not calls[a[4]][4]
+                        if a[0] < hi and lo < a[1] and (tag is None or a[2] is None or a[2] == tag) and (wr or a[3] or bank and not same):
+                            dep[a[4]] = max(dep.get(a[4], 0.0), 0.0 if same and (q == "P" or not a[3]) else WAKE)
+            if q == "G":
+                if g0 is not None:
+                    dep.setdefault(g0, None)
+                g0 = n
+            before.append(dep)
+            for lst, wr in ((writes, True), (reads, False)):
+                for r in lst:
+                    buf, lo, hi, tag, bank = region(r)
+                    for key in ((buf, True), (buf, False)) if wr else ():
+                        seen[key] = [a for a in seen.get(key, []) if not (lo <= a[0] and a[1] <= hi and (tag is None or tag == a[2]))]
+                    seen.setdefault((buf, wr), []).append((lo, hi, tag, wr, n))
+        way = [0.0] * len(calls)
+        for n in range(len(calls) - 1, -1, -1):
+            c = calls[n]
+            way[n] += c[5] + (FLY if c[4] and c[4] != "tx" else 0.0)
+            for m, lat in before[n].items():
+                way[m] = max(way[m], way[n] + (lat or 0.0))
+        busy = {q: [] for q in list(queues) + ["D"]}
 
-    def merge(*streams):
-        st = [[s, 0, b] for s, b in streams]
-        while True:
-            best = None
-            for x in st:
-                if x[1] < len(x[0]) and x[0][x[1]] is None and all(y[1] == len(y[0]) for y in st[2:]):
-                    x[1] += 1
-                if x[1] < len(x[0]) and x[0][x[1]] is not None:
-                    o = x[0][x[1]]
-                    t = needs(o[0], o[2], o[3], o[4])[1] + x[2] + WP * x[1]
-                    if best is None or t < best[0]:
-                        best = (t, x)
-            if best is None:
-                return
-            x = best[1]
-            emit(*x[0][x[1]])
-            x[1] += 1
+        def place(q, t, c):
+            line = busy[q]
+            k = len(line)
+            while k and line[k - 1][0] >= t:
+                k -= 1
+            t = max(t, line[k - 1][1]) if k else t
+            while k < len(line) and line[k][0] < t + c:
+                t = line[k][1]
+                k += 1
+            line.insert(k, (t, t + c))
+            return t
+        start, end, left = {}, {}, [len(d) for d in before]
+        after = [[] for _c in calls]
+        for n, d in enumerate(before):
+            for m in d:
+                after[m].append(n)
+        ready = [n for n in range(len(calls)) if not left[n]]
+        while ready:
+            n = max(ready, key=lambda n: (way[n] - calls[n][6], -n))
+            ready.remove(n)
+            q, _f, _r, _w, dm, cost, _l = calls[n]
+            t = max([0.0] + [start[m] + 1e-6 if lat is None else end[m] + lat for m, lat in before[n].items()])
+            if dm and dm != "tx":
+                start[n] = place(q, t, 0.05)
+                end[n] = place("D", start[n] + 0.7 * FLY, cost) + cost + 0.3 * FLY
+            else:
+                start[n] = place(q, t, cost)
+                end[n] = start[n] + cost
+            for m in after[n]:
+                left[m] -= 1
+                if not left[m]:
+                    ready.append(m)
+        return sorted(range(len(calls)), key=lambda n: (start[n], n))
 
-    scaled = [(T.idn[:, 128 * n:128 * n + 128], ("idn", 128 * n, 128 * n + 128)) for n in range(8)]
-    I16, IH, IMH, IM, IBIG, IW1, IW2, IPEN = scaled
+    I1 = (T.id1[:], ("id1",))
+    I16, IB, IMB, IB2 = [(T.idn[:, n, :], ("idn",)) for n in range(4)]
 
     def cols(ap):
         n = 1
@@ -169,15 +202,25 @@ def rank_program(g, core, T, topo):
         return n
 
     def us(cycles):
-        return 0.03 + 0.00104 * cycles
+        return 0.04 + 0.00096 * cycles
 
-    def tt(q, out, o, a, ra, b, rb, f):
+    def blk(bank, q0, q1=None, i0=0, i1=3):
+        return T[bank][:, 32 * q0:32 * (q0 + 1 if q1 is None else q1), i0:i1]
+
+    def room(name, a, b, p0=0, p1=128):
+        buf, c = ROOMS[name]
+        return T[buf][p0:p1, c + a:c + b], (buf, c + a, c + b)
+
+    def flat(bank, a, b):
+        return T[bank][:, a // 4:b // 4, :]
+
+    def tt(out, o, a, ra, b, rb, f):
         n = cols(out)
         bank = any(region(r)[4] for r in (ra, rb))
-        op(q, lambda e: e.tensor_tensor(out, a, b, f), [ra, rb], [o], None, us(max(64, n if bank else 2 * n)))
+        op("V", lambda e: e.tensor_tensor(out, a, b, f), [ra, rb], [o], None, us(max(64, n if bank else 2 * n)))
 
-    def ts(out, o, a, ra, s1, s2, f1, f2=None, extra=()):
-        c = us(max(64, cols(out)))
+    def ts(out, o, a, ra, s1, s2, f1, f2=None, extra=(), fast=1.0):
+        c = us(max(64, fast * cols(out)))
         if f2 is None:
             op("V", lambda e: e.tensor_scalar(out, a, s1, None, f1), [ra] + list(extra), [o], None, c)
         else:
@@ -186,419 +229,446 @@ def rank_program(g, core, T, topo):
     def cpy(out, o, a, ra):
         op("V", lambda e: e.tensor_copy(out, a), [ra], [o], None, us(max(64, cols(out))))
 
+    def scan(out, o, d0, r0, d1, r1, f):
+        op("V", lambda e: e.tensor_tensor_scan(out, d0, d1, 0.0, A.mult, f), [r0, r1], [o], None, us(max(64, cols(out))))
+
     def act(out, o, a, ra, f, bias=0.0, scale=1.0, extra=(), accum=None, ao=None):
-        c = us(cols(out))
+        c = us(cols(out)) + 0.03
         if accum is None:
             op("S", lambda e: e.activation(out, a, f, bias=bias, scale=scale), [ra] + list(extra), [o], None, c)
         else:
             op("S", lambda e: e.activation(out, a, f, bias=bias, scale=scale, accum_out=accum), [ra] + list(extra), [o, ao], None, c)
 
     def mm(out, bank, l, rl, r, rr, start, stop):
-        op("P", lambda e: e.matmul(out, l, r, start, stop), [rl, rr], [(bank,)], None, max(64, cols(r)) * (0.0024 if rl[0][:2] in ("lt", "tt") else 0.0006))
+        four = 4 if SCRATCH[rl[0]][2] == FP else 1
+        op("P", lambda e: e.matmul(out, l, r, start, stop), [rl, rr], [(bank,)], None, max(64, cols(r)) * 0.0005 * four)
 
-    def dma(q, out, o, a, ra, sem):
-        op(q, lambda e: e.dma_start(out, a), [ra] if ra else [], [o] if o else [], dma=sem)
+    def dma(q, out, o, a, ra, sem, also=()):
+        size = out.shape[0] * cols(out) * (2 if o and SCRATCH[o[0]][2] == BF else 4)
+        op(q, lambda e: e.dma_start(out, a), [ra] if ra else [], ([o] if o else []) + list(also), sem, size / RATE)
 
-    def fill(name, v, lo=None, hi=None):
-        if lo is None:
-            op("V", lambda e: e.memset(T[name][:], v), [], [(name,)])
-        else:
-            op("V", lambda e: e.memset(T[name][:, lo:hi], v), [], [(name, lo, hi)])
+    def fill(ap, o, v):
+        op("V", lambda e: e.memset(ap, v), [], [o])
 
-    def aff(out, src, pat, cmp, base, mult):
-        op("G", lambda e: e.affine_select(T[out][:], T[src][:], pat, cmp, 0.0, base, mult), [(src,)], [(out,)])
+    def aff(ap, o, pat, cmp, base, mult=1, val=0.0, src=None):
+        s, rs = src or (ap, o)
+        op("G", lambda e: e.affine_select(ap, s, pat, cmp, val, base, mult), [rs], [o], None, 0.17 + 0.002 * cols(ap))
 
-    def gather(q, out, oreg, win, wn, n0, n1, off, offreg):
-        src = win[:, n0:n1].indirect(off)
-        c = us(1.5 * cols(out))
+    def iota(ap, o, pat, base, mult):
+        op("G", lambda e: e.iota(ap, pat, base, mult, allow_small_or_imprecise_dtypes=True), [], [o], None, 0.13 + 0.002 * cols(ap))
+
+    def gather(q, out, oreg, win, wreg, off, offreg):
+        src = win.indirect(off)
+        c = us(1.56 * cols(out))
         if q == "V":
-            op("V", lambda e: e.tensor_copy(out, src), [(wn, n0, n1), offreg], [oreg], None, c)
+            op("V", lambda e: e.tensor_copy(out, src), [wreg, offreg], [oreg], None, c)
         else:
-            op("S", lambda e: e.activation(out, src, AF.Copy), [(wn, n0, n1), offreg], [oreg], None, c)
+            op("S", lambda e: e.activation(out, src, AF.Copy), [wreg, offreg], [oreg], None, c)
+
+    def gather_tt(out, oreg, win, wreg, off, offreg, b, rb, f):
+        src = win.indirect(off)
+        op("V", lambda e: e.tensor_tensor(out, src, b, f), [wreg, offreg, rb], [oreg], None, us(1.56 * cols(out)))
 
     for i in range(NT):
-        dma("Y", T.n32[:, 384 * i:384 * i + 384], ("n32", 384 * i, 384 * i + 384), T.nxt[:, W * i:W * i + W], None, "d_i%d" % i)
-    dma("S", T.m32[:], ("m32",), T.mem[:], None, "l_m")
-    dma("S", T.cur32[:], ("cur32",), T.cur[:], None, "l_c")
+        dma("YS"[i % 2], T.n32[32 * i:32 * i + 32, :], ("n32", 0, Q, i), T.nxt[:, W * i:W * i + W], None, "l_n")
+    dma("S", T.n32[96:128, :], ("n32", 0, Q, 3), T.fro[:], None, "l_n")
+    dma("Y", T.m32[:], ("m32",), T.mem[:], None, "l_m")
     dma("S", T.typ32[:], ("typ32",), T.typ[:], None, "l_t")
-    dma("S", T.wb[:], ("wb",), T.w0[:], None, "l_w")
-    for k in range(11, 16):
-        dma("Y", T.inf[k::16, :], ("inf", 0, W, k), T.x[k::16, :], None, "d_fl")
+    dma("Y", T.cur32[:], ("cur32",), T.cur[:], None, "l_c")
+    if XA:
+        dma("Y", T.xs[:, 0:XA], ("xs", 0, XA), T.x[:, 0:XA], ("cur32",), "l_x")
 
-    fill("ones", 1.0)
-    for n in ("wnx", "wv", "wcnt"):
-        fill(n, 1.0)
-    fill("wbit", 16.0)
-    fill("idf", 1.0)
-    fill("sel", 1.0)
-
-    def stamp(t):
-        fill("stl", (BIG if t == 0 else STAMP * t) / 128.0, 128 * t, 128 * t + 128)
-
-    for t in range(5):
-        stamp(t)
-    fill("bo", 1.0)
-    for be in range(2):
-        fill("gt%d" % be, 0.0, 96, 192)
-    op("G", lambda e: e.iota(T.pid[:], [[1, 1]], 0, 1), [], [("pid",)])
-    op("G", lambda e: e.iota(T.pv[:, 0:384], [[1, 384]], 0, 384, allow_small_or_imprecise_dtypes=True), [], [("pv", 0, 384)])
-    aff("idf", "idf", [[-1, 128]], A.is_equal, 0, 1)
-    aff("sel", "sel", [[-4, 32]], A.is_ge, 0, 1)
-    aff("sel", "sel", [[4, 32]], A.is_ge, 3, -1)
-    aff("wnx", "wnx", [[-2, 3], [-16, 8]], A.is_ge, 0, 1)
-    aff("wnx", "wnx", [[2, 3], [16, 8]], A.is_ge, 1, -1)
-    aff("wv", "wv", [[0, 3], [-16, 8]], A.is_ge, -9, 1)
-    aff("wv", "wv", [[0, 3], [16, 8]], A.is_ge, 10, -1)
-    aff("wcnt", "wcnt", [[0, 6], [-16, 8]], A.is_ge, 0, 1)
-    aff("wcnt", "wcnt", [[0, 6], [16, 8]], A.is_ge, 15, -1)
-    op("G", lambda e: e.iota(T.pv[:, 384:1152], [[W, 2], [1, 384]], W, 384, allow_small_or_imprecise_dtypes=True), [], [("pv", 384, 1152)])
-    aff("wbit", "wbit", [[-1, 3], [-16, 8]], A.is_equal, -6, 1)
     pm, co = T.pm, T.cols
-    ts(pm[:, 0:1], ("pm", 0, 1), T.pid[:], ("pid",), 3, None, A.bitwise_and)
+    op("G", lambda e: e.iota(T.pid[:], [[1, 1]], 0, 1), [], [("pid",)])
+    iota(*room("pv", 0, 384), [[1, 3], [0, 128]], 0, 3)
+    iota(*room("vr", 0, 384), [[0, 3], [1, 128]], 0, 0)
+    fill(T.ones[:], ("ones",), 1.0)
+    fill(T.wr[:], ("wr",), 0.0)
+    fill(T.id1[:], ("id1",), 1.0)
+    for n, v in enumerate((16.0, B, -B, B2)):
+        fill(T.idn[:, n, :], ("idn", n, n + 1), v)
+    fill(T.wg[:, 0:24], ("wg", 0, 24), -1.0)
+    fill(T.wg[:, 24:72], ("wg", 24, 72), 1.0)
+    fill(T.sel[:], ("sel",), 1.0)
+    fill(T.rs3[:], ("rs3",), 1.0)
+    fill(T.rs3[:, 0:288:3], ("rs3",), 0.0)
+    ts(pm[:, 0:1], ("pm", 0, 1), T.pid[:], ("pid",), 4, None, A.arith_shift_right)
+    ts(co[:, 9:10], ("cols", 9, 10), pm[:, 0:1], ("pm", 0, 1), -48, None, A.mult)
     ts(pm[:, 1:2], ("pm", 1, 2), T.pid[:], ("pid",), 2, 3, A.arith_shift_right, A.bitwise_and)
-    ts(pm[:, 2:3], ("pm", 2, 3), T.pid[:], ("pid",), 15, None, A.bitwise_and)
-    ts(pm[:, 3:4], ("pm", 3, 4), T.pid[:], ("pid",), 4, None, A.arith_shift_right)
+    ts(pm[:, 2:3], ("pm", 2, 3), T.pid[:], ("pid",), 3, None, A.bitwise_and)
     for h in range(4):
-        ts(co[:, h:h + 1], ("cols", h, h + 1), pm[:, 0:1], ("pm", 0, 1), h, None, A.is_equal)
         ts(co[:, 4 + h:5 + h], ("cols", 4 + h, 5 + h), pm[:, 1:2], ("pm", 1, 2), h, None, A.is_equal)
-    ts(co[:, 9:10], ("cols", 9, 10), pm[:, 3:4], ("pm", 3, 4), -W, None, A.mult)
+        ts(co[:, h:h + 1], ("cols", h, h + 1), pm[:, 2:3], ("pm", 2, 3), h, None, A.is_equal)
+    aff(T.id1[:], ("id1",), [[-1, 128]], A.is_equal, 0)
 
-    def split(hi, lo, src, n0, n1, scalar=False):
-        if scalar:
-            act(T[hi][:, n0:n1], (hi, n0, n1), T[src][:, n0:n1], (src, n0, n1), AF.Copy)
-        else:
-            cpy(T[hi][:, n0:n1], (hi, n0, n1), T[src][:, n0:n1], (src, n0, n1))
-        tt("V", T[lo][:, n0:n1], (lo, n0, n1), T[src][:, n0:n1], (src, n0, n1), T[hi][:, n0:n1], (hi, n0, n1), A.subtract)
+    def weight(q0, q1, i0, i1, row, step, val):
+        aff(T.wr[:, q0:q1, :, i0:i1], ("wr", q0, q1), [[0, q1 - q0], [-16, 8], [-step, i1 - i0]], A.not_equal, -row, 1, val)
 
-    def to_inf(k, src, n0):
-        dma("Y", T.inf[k::16, :], ("inf", 0, W, k), T[src][:, n0:n0 + 384], (src, n0, n0 + 384), "d_bi")
+    weight(3, 6, 0, 3, 0, 2, 1.0)
+    weight(6, 7, 0, 3, 9, 0, -0.25)
+    weight(3, 6, 0, 3, 1, 2, 1.0)
+    weight(6, 7, 0, 3, 10, 0, -32.0)
+    weight(4, 6, 0, 3, 13, 0, B)
+    weight(6, 7, 0, 3, 6, 0, -2048.0)
+    aff(T.idn[:], ("idn",), [[0, 4], [-1, 128]], A.is_equal, 0)
+    aff(T.sel[:], ("sel",), [[-4, 32]], A.is_ge, 0)
+    weight(3, 4, 0, 3, 13, 0, -B)
+    aff(T.sel[:], ("sel",), [[4, 32]], A.is_ge, 3, -1)
+    weight(2, 3, 0, 3, 6, 1, 16.0)
+    weight(0, 1, 0, 3, 13, 0, 8.5)
+    weight(2, 3, 0, 2, 7, 1, -32.0)
+    weight(1, 2, 0, 3, 13, 0, -8.5)
+    weight(2, 3, 0, 3, 13, 0, 7.5)
+    aff(T.wg[:], ("wg",), [[0, 3], [-16, 8], [0, 3]], A.is_ge, 0)
+    for i, v in enumerate((6144.0, 3072.0, -3072.0)):
+        weight(2, 3, i, i + 1, 14, 0, v)
+    aff(T.wg[:], ("wg",), [[0, 3], [16, 8], [0, 3]], A.is_ge, 15, -1)
 
-    def to_pw(k, i, src, n0):
-        dma("Y", T.pw[k::16, W * i:W * i + W], ("pw", W * i, W * i + W, k), T[src][:, n0:n0 + 384], (src, n0, n0 + 384), "d_pw")
+    def to_inf(q, k, src, reg):
+        dma(q, T.inf[k::16, :], ("inf", 0, W, k), src, reg, "d_bi", [("gate", k, k + 1)])
 
-    act(T.pv[:, 0:384], ("pv", 0, 384), T.pv[:, 0:384], ("pv", 0, 384), AF.Identity, bias=co[:, 9:10], extra=[("cols", 9, 10)])
-    for i in range(NT):
-        split("nhi", "nlo", "n32", 384 * i, 384 * i + 384)
-        to_inf(2 * i, "nhi", 384 * i)
-        to_inf(2 * i + 1, "nlo", 384 * i)
-    split("phi", "plo", "pv", 0, 384, True)
-    to_inf(9, "phi", 0)
-    to_inf(10, "plo", 0)
-    ts(T.mi[:, 0:384], ("mi", 0, 384), T.m32[:], ("m32",), 1, None, A.bitwise_and)
-    ts(T.mi[:, 384:768], ("mi", 384, 768), T.m32[:], ("m32",), 2, None, A.bitwise_and)
-    ts(T.bits[:, 768:1152], ("bits", 768, 1152), T.m32[:], ("m32",), 4, None, A.is_ge)
-    ts(T.bits[:, 0:768], ("bits", 0, 768), T.mi[:], ("mi",), 1, None, A.is_ge)
-    for i in range(NT):
-        to_inf(6 + i, "bits", 384 * i)
-    dma("Y", T.xs[:], ("xs",), T.x[:], None, "l_x")
-    act(T.wf[:], ("wf",), T.wb[:], ("wb",), AF.Copy)
-    dma("S", T.f32[:], ("f32",), T.fro[:], None, "l_f")
+    act(*room("vr", 384, 768), *room("pv", 0, 384), AF.Identity, bias=co[:, 9:10], extra=[("cols", 9, 10)])
+    cpy(*room("fm", 0, 384), T.m32[:], ("m32",))
+    parts = [(512 * c, 512 * c + 512, "b%d" % c) for c in range(3)]
+    for a, b, bank in parts:
+        cpy(T[bank][:], (bank,), T.n32[:, a:b], ("n32", a, b))
+    for a, b, bank in parts:
+        act(*room("nhi", a, b), T[bank][:], (bank,), AF.Copy)
+        tt(*room("nlo", a, b), T[bank][:], (bank,), *room("nhi", a, b), A.subtract)
+    for n, (s, o) in enumerate(((0.5, 191.75), (0.25, 191.625))):
+        act(*room("fm", 384 * n + 384, 384 * n + 768), *room("fm", 0, 384), AF.Identity, bias=o, scale=s)
+    to_inf("Y", 15, T.x[15::16, :], None)
+    for k in (13, 14):
+        to_inf("Y", k, T.ones[:], ("ones",))
+    for n in range(2):
+        to_inf("Y", 9 + n, *room("vr", 384 * n, 384 * n + 384))
+    to_inf("Y", 6, *room("fm", 0, 384))
+    for k, src in enumerate(("nhi", "nlo")):
+        for i, row in enumerate((0, 2, 4, 11)):
+            to_inf("Y", row + k, *room(src, 0, Q, 32 * i, 32 * i + 32))
+        to_inf("Y", 7 + k, *room("fm", 384 * k + 384, 384 * k + 768))
 
-    cpy(T.lst[:], ("lst",), T.cur32[:], ("cur32",))
-    cpy(T.tf[:], ("tf",), T.typ32[:], ("typ32",))
-    cpy(T.idb[:], ("idb",), T.idf[:], ("idf",))
-    for n, v in enumerate((16.0, 0.5, -0.5, -1.0, float(BIG), W / 2.0, float(W), float(BIG))):
-        ts(T.idn[:, 128 * n:128 * n + 128], ("idn", 128 * n, 128 * n + 128), T.idb[:], ("idb",), v, None, A.mult)
-    tt("V", T.selr[:], ("selr",), T.idf[:, :, 0, :], ("idf",), T.idf[:, :, 1, :], ("idf",), A.add)
+    dma("Y", *room("wb", 0, K), T.w0[:], room("nlo", 0, Q)[1], "l_w")
+    dma("Y", T.xs[:, XA:W], ("xs", XA, W), T.x[:, XA:W], room("nlo", 0, Q)[1], "l_x")
+
+    iota(T.kz[:], ("kz",), [[0, 32], [TS, 4]], TS, 0)
+    iota(T.kc[:], ("kc",), [[16, 8]], 0, 1)
+    iota(T.km[:], ("km",), [[0, 16], [1, 16]], 0, 0)
+    for be in range(2):
+        cpy(T.lst[:, 96 * be:96 * be + 96], ("lst", 96 * be, 96 * be + 96), T.cur32[:, :, be, :], ("cur32",))
+    tt(T.selr[:], ("selr",), T.id1[:, :, 0, :], ("id1",), T.id1[:, :, 1, :], ("id1",), A.add)
     for h in (2, 3):
-        tt("V", T.selr[:], ("selr",), T.selr[:], ("selr",), T.idf[:, :, h, :], ("idf",), A.add)
-    cpy(T.wx[:, 0:24], ("wx", 0, 24), T.wnx[:], ("wnx",))
-    cpy(T.wx[:, 24:48], ("wx", 24, 48), T.wv[:], ("wv",))
-    for t in range(5, ROUNDS * FINDS + 1):
-        stamp(t)
-    fill("c72", 1.5 * W / 128)
+        tt(T.selr[:], ("selr",), T.selr[:], ("selr",), T.id1[:, :, h, :], ("id1",), A.add)
+    for h in range(4):
+        ts(T.ttl[:, :, h], ("ttl", 0, 256, h), T.typ32[:], ("typ32",), co[:, 4 + h:5 + h], None, A.mult, extra=[("cols", 4 + h, 5 + h)])
+    for be in range(2):
+        sg, ob = "sg%d" % be, "b%d" % (6 + be)
+        mm(flat(ob, 0, 32), ob, T.ttl[:, 32 * be:32 * be + 32, :], ("ttl",), T.selr[:], ("selr",), True, True)
+        for i in range(NT):
+            ts(T[sg][:, 0:32, i], (sg, 0, 32, i), flat(ob, 0, 32), (ob,), float(i), 2.0, A.is_equal, A.mult)
+        fill(T[sg][:, 32:64, :], (sg, 32, 64), -2.0)
+    act(T.wf[:, 0:H], ("wf", 0, H), *room("wb", 0, H), AF.Copy)
+    cpy(T.wf[:, H:K], ("wf", H, K), *room("wb", H, K))
+    for t in range(FINDS):
+        act(T.stl[:, t, :], ("stl", t, t + 1), *I1, AF.Copy, scale=-STAMP * (t + 2))
 
-    aff("bo", "bo", [[-16, 8], [0, 16]], A.is_ge, 0, 1)
-    aff("bo", "bo", [[16, 8], [0, 16]], A.is_ge, 15, -1)
-    aff("plw", "bo", [[-16, 8], [0, 16]], A.is_ge, -2, 1)
-    aff("plw", "plw", [[16, 8], [0, 16]], A.is_ge, 3, -1)
-    aff("lm", "bo", [[-1, 128]], A.is_gt, 0, 1)
-    op("G", lambda e: e.iota(T.kc[:], [[16, 8]], 0, 1, allow_small_or_imprecise_dtypes=True), [], [("kc",)])
-    op("G", lambda e: e.iota(T.kio[:], [[1, 128]], 0, 0, allow_small_or_imprecise_dtypes=True), [], [("kio",)])
-    op("G", lambda e: e.iota(T.km[:], [[0, 8], [1, 16]], 0, 0, allow_small_or_imprecise_dtypes=True), [], [("km",)])
+    def at(r):
+        return T.cores[r % N]
 
-    know("G", "l_x", total["l_x"])
-    total["tx"] = 0
-    for t, buf in ((0, "x1"), (1, "x2")):
-        dst, src = T.cores[(rank - 1 - t) % N], T.cores[(rank + 1 + t) % N]
+    def direct(r):
+        return not (topo.chip(at(r - 1)) == topo.chip(at(r - 2)) != topo.chip(at(r)))
+
+    def lanes(r, t):
+        e = topo.engines(at(r), at(r - 1 - t))
+        rest = [n for n in e if n not in topo.engines(at(r), at(r - 2))]
+        return rest if t == 0 and direct(r) and rest else e
+
+    def send(buf, src, dst, rx, eng):
         rid, pid, _s = topo.addr(dst)
-        rx = "rx%d" % (t + 1)
-        g.remote_dma(T[buf][:], T.xs[:], T.sem[rx], T.sem.tx, pid, rid, topo.mask(core, dst))
-        total["tx"] += len(topo.engines(core, dst))
-        total[rx] = len(topo.engines(src, core))
-        acc[buf] = [(0, 1 << 20, None, "R", rx, total[rx], True)]
+        op("G", lambda e: e.remote_dma(T[buf][:], T[src][:], T.sem[rx], T.sem.tx, pid, rid, sum(1 << n for n in eng)), [(src,), ("gate",)], [], "tx", 1.0)
+        total["tx"] = total.get("tx", 0) + len(eng)
 
-    fill("eqm", 1.0)
-    aff("eqm", "eqm", [[1, 16], [0, 8], [-1, 16]], A.is_equal, 0, 0)
-    aff("db", "eqm", [[0, 16], [-16, 8], [0, 16]], A.is_equal, -4, 1)
-    aff("df", "eqm", [[0, 16], [-16, 8], [0, 16]], A.is_ge, -5, 1)
-    aff("df", "df", [[0, 16], [16, 8], [0, 16]], A.is_ge, 6, -1)
-    aff("dp", "eqm", [[0, 16], [-16, 8], [0, 16]], A.is_ge, -2, 1)
-    aff("dp", "dp", [[0, 16], [16, 8], [0, 16]], A.is_ge, 3, -1)
+    send("x1", "xs", at(rank - 1), "rx1", lanes(rank, 0))
+    if direct(rank):
+        send("x2", "xs", at(rank - 2), "rx2", lanes(rank, 1))
+    total["rx1"] = len(lanes(rank + 1, 0))
+    total["rx2"] = len(lanes(rank + 2, 1) if direct(rank + 2) else topo.engines(at(rank + 1), core))
+    for n in ("1", "2"):
+        acc["x" + n] = [(0, 1 << 20, None, "R", "rx" + n, total["rx" + n], True)]
 
     def later():
-        act(T.pv[:, 384:1152], ("pv", 384, 1152), T.pv[:, 384:1152], ("pv", 384, 1152), AF.Identity, bias=co[:, 9:10], extra=[("cols", 9, 10)])
-        for i in range(1, NT):
-            split("phi", "plo", "pv", 384 * i, 384 * i + 384, True)
-        split("fhi", "flo", "f32", 0, 384)
         for i in range(NT):
-            for k, (src, n0) in enumerate((("nhi", 384 * i), ("nlo", 384 * i), ("phi", 384 * i), ("plo", 384 * i), ("bits", 384 * i), ("fhi", 0), ("flo", 0))):
-                to_pw(k, i, src, n0)
-        for i in range(NT):
-            for k in range(7, 16):
-                dma("Y", T.pw[k::16, W * i:W * i + W], ("pw", W * i, W * i + W, k), T.x[k::16, :], None, "d_pf")
-        cpy(co[:, 8:9], ("cols", 8, 9), pm[:, 2:3], ("pm", 2, 3))
-        ts(co[:, 10:11], ("cols", 10, 11), pm[:, 2:3], ("pm", 2, 3), 2, None, A.is_lt)
-        ts(co[:, 11:12], ("cols", 11, 12), pm[:, 3:4], ("pm", 3, 4), -16, None, A.mult)
-        ts(T.kc[:], ("kc",), T.kc[:], ("kc",), co[:, 11:12], None, A.add, extra=[("cols", 11, 12)])
+            for k, src in enumerate(("nhi", "nlo")):
+                dma("Y", T.pwb[k::16, TS * i:TS * i + W], ("pwb", TS * i, TS * i + W, k), room(src, 0, Q, 32 * i, 32 * i + 32)[0], ("xs",), "d_pb")
+        iota(T.kio[:], ("kio",), [[1, 128]], 1, 0)
+        iota(T.tri[:], ("tri",), [[0, 64]], 1, 0)
+        aff(T.tri[:], ("tri",), [[4, 64]], A.is_ge, 3, -1)
+        for n, v in (("bo", 1), ("bof", 1), ("lm", -1)):
+            iota(T[n][:], (n,), [[0, 128]], v, 0)
+            aff(T[n][:], (n,), [[-16, 8], [0, 16]], A.is_ge, 0)
+            aff(T[n][:], (n,), [[16, 8], [0, 16]], A.is_ge, 15, -1)
+        aff(T.lm[:], ("lm",), [[-1, 128]], A.is_gt, 0)
+        iota(T.wn[:], ("wn",), [[0, 128]], 0, 0)
+        for r in range(6):
+            aff(T.wn[:, :, r % 2:3:2 - r % 2], ("wn",), [[-16, 8], [0, 2]], A.not_equal, -r, 1, 0.5)
+        weight(7, 8, 0, 1, 11, 0, 1.0)
+        weight(7, 8, 0, 1, 12, 0, 1.0)
+        iota(T.r16[:], ("r16",), [[0, 16], [1, 16]], 0, 0)
+        aff(T.r16[:], ("r16",), [[0, 16], [1, 16]], A.is_equal, 0, 0, 1.0)
+        iota(T.rt[:, 64:72], ("rt", 64, 72), [[0, 8]], 0, 0)
+        iota(T.pl[:, :, 64:72], ("pl", 0, 72, 2), [[0, 16]], 0, 0)
+        fill(T.kz[:, :, 3], ("kz",), float(TS))
+        ts(pm[:, 3:4], ("pm", 3, 4), T.pid[:], ("pid",), 15, None, A.bitwise_and)
+        ts(pm[:, 4:5], ("pm", 4, 5), pm[:, 3:4], ("pm", 3, 4), 1, None, A.arith_shift_right)
+        cpy(co[:, 8:9], ("cols", 8, 9), pm[:, 3:4], ("pm", 3, 4))
+        ts(co[:, 10:11], ("cols", 10, 11), pm[:, 0:1], ("pm", 0, 1), -16, None, A.mult)
+        ts(co[:, 11:12], ("cols", 11, 12), pm[:, 4:5], ("pm", 4, 5), -TS, -TS - W / 2.0, A.mult, A.add)
+        ts(T.kc[:], ("kc",), T.kc[:], ("kc",), co[:, 10:11], None, A.add, extra=[("cols", 10, 11)])
         ts(T.km[:], ("km",), T.km[:], ("km",), co[:, 8:9], None, A.is_equal, extra=[("cols", 8, 9)])
+        ts(T.k3[:], ("k3",), T.km[:, 0:128], ("km",), 3.0, -1.0, A.mult, A.add)
         ts(T.kch[:], ("kch",), T.kc[:], ("kc",), 0.5, None, A.add)
-        ts(T.dumc[:, 0:8], ("dumc", 0, 8), T.kc[:], ("kc",), 3 * W, None, A.add)
-        ts(T.dumc[:, 8:16], ("dumc", 8, 16), T.kc[:], ("kc",), 3 * W + CAP, None, A.add)
-        ts(T.lm[:], ("lm",), T.lm[:], ("lm",), -1.0, None, A.mult)
-        fill("rt", 65536.0, 64, 72)
-        fill("ra", 16384.0, K, K + 16)
-        fill("rb", 16384.0, K, K + 16)
+        for n, v in enumerate((W, W + CAP, W + TS, W + CAP + TS)):
+            ts(T.dum[:, 8 * n:8 * n + 8], ("dum", 8 * n, 8 * n + 8), T.kc[:], ("kc",), float(v), None, A.add)
 
-    def masks(out, obuf, n0, n1, src, sreg, nscalar):
+    def masks(out, obuf, src, sreg, nscalar):
         for h in range(4):
-            o = (obuf, n0, n1, h)
+            o = (obuf, 0, 1 << 20, h)
             if h < nscalar:
                 act(out(h), o, src, sreg, AF.Copy, scale=co[:, h:h + 1], extra=[("cols", h, h + 1)])
             else:
                 ts(out(h), o, src, sreg, co[:, h:h + 1], None, A.mult, extra=[("cols", h, h + 1)])
 
-    def types_in():
-        for be in range(2):
-            for h in range(4):
-                ts(T.ttl[:, 128 * be + h:128 * be + 128:4], ("ttl", 128 * be, 128 * be + 128, h), T.tf[:, 32 * be:32 * be + 32], ("tf",), co[:, 4 + h:5 + h], None, A.mult, extra=[("cols", 4 + h, 5 + h)])
-            O, ob = T["b%d" % (6 + be)], "b%d" % (6 + be)
-            mm(O[:, 0:32], ob, T.ttl[:, 128 * be:128 * be + 128], ("ttl", 128 * be, 128 * be + 128), T.selr[:], ("selr",), True, True)
-            ac, gt = "ac%d" % be, "gt%d" % be
-            for i in range(NT):
-                act(T[ac][:, 32 * i:32 * i + 32], (ac, 32 * i, 32 * i + 32), O[:, 0:32], (ob,), AF.Abs, bias=-float(i))
-            act(T[gt][:, 0:96], (gt, 0, 96), T[ac][:], (ac,), AF.Sign, bias=0.5, scale=-1.0)
+    def own(be, bank, q, w, start, stop):
+        sg = "sg%d" % be
+        for s in range(2):
+            mm(blk(bank, q), bank, *w, T[sg][:, 32 * s:32 * s + 32, :], (sg,), start and s == 0, stop and s == 1)
 
-    def pick(be, s0, own="gt%d"):
-        st, t, u = T["st%d" % be], T["tt%d" % be], T["tu%d" % be]
-        P, pb = T["b%d" % (4 + be)], "b%d" % (4 + be)
-        mm(P[:, 128:224], pb, *IPEN, T[own % be][:, 0:96], (own % be, 0, 96), True, True)
-        tt("V", t[:], ("tt%d" % be,), P[:, 128:224], (pb,), st[:, s0:s0 + 96], ("st%d" % be, s0, s0 + 96), A.add)
-        tt("V", u[:], ("tu%d" % be,), t[:, 0:32], ("tt%d" % be,), t[:, 32:64], ("tt%d" % be,), A.max)
+    def after(be, bank, q, w, stop):
+        sg = "sg%d" % be
+        for s in range(2):
+            mm(blk(bank, q, None, 1, 3), bank, *w, T[sg][:, 32 * s:32 * s + 32, 0:2], (sg,), False, False)
+            mm(blk(bank, q, None, 0, 1), bank, *w, T[sg][:, 32 * s:32 * s + 32, 2:3], (sg,), False, stop and s == 1)
 
-    def next_list(be, more=None, own="gt%d"):
-        t, u, mp, lt = T["tt%d" % be], T["tu%d" % be], T["mp%d" % be], T["lt%d" % be]
-        pick(be, 0, own)
-        tt("V", mp[:], ("mp%d" % be,), u[:], ("tu%d" % be,), t[:, 64:96], ("tt%d" % be,), A.max)
-        masks(lambda h: lt[:, :, h, :], "lt%d" % be, 0, 128, mp[:], ("mp%d" % be,), MS)
+    def next_list(be, more=None):
+        tb, sc, lt, ob, off = [n % be for n in ("tb%d", "sc%d", "lt%d")] + ["b%d" % (6 + be), "off%d" % be]
+        scan(T[sc][:, 0:96], (sc,), T.rs3[:, 0:96], ("rs3",), T[tb][:, 0:96], (tb,), A.max)
+        masks(lambda h: T[lt][:, :, h, :], lt, T[sc][:, 2:96:3], (sc,), MS)
         if more:
             more()
-        O, ob = T["b%d" % (6 + be)], "b%d" % (6 + be)
-        mm(O[:, 0:32], ob, lt[:], ("lt%d" % be,), T.sel[:], ("sel",), True, True)
-        oi, oj, off = "oi%d" % be, "oj%d" % be, "off%d" % be
-        cpy(T[oi][:], (oi,), O[:, 0:32], (ob,))
-        ts(T[oj][:], (oj,), T[oi][:], (oi,), STAMP - 1, None, A.bitwise_and)
-        cpy(T[off][:], (off,), T[oj][:], (oj,))
+        mm(flat(ob, 0, 32), ob, T[lt][:], (lt,), T.sel[:], ("sel",), True, True)
+        cpy(T[off][:], (off,), flat(ob, 0, 32), (ob,))
 
-    def round_start(be, t):
-        X, xb, st = T["b%d" % be], "b%d" % be, "st%d" % be
-        n = 96 if t else 192
-        mm(X[:, 0:n], xb, T.stl[:, 0:128], ("stl", 0, 128), T.ones[:, 0:n], ("ones",), True, False)
+    def round_start(be):
+        xb, cb, st, tb = "b%d" % (2 + be), "b%d" % (4 + be), "st%d" % be, "tb%d" % be
+        own(be, xb, 0, IB2, True, True)
         for i in range(NT):
             buf = ("rw%d" if i % 2 == 0 else "ge%d") % be
-            l0 = 64 * i + 32 * be
-            q = "S" if (i + be) % 2 == 0 else "V"
-            lst = (T.lst[:, l0:l0 + 32], ("lst",))
-            if t:
-                gather(q, T[buf][:], (buf,), T.pw, "pw", 0, 3 * W, *lst)
-            else:
-                gather(q, T[buf][:], (buf,), T.inf, "inf", 0, W, *lst)
+            l0 = 96 * be + 32 * i
+            gather("S" if (i + be) % 2 == 0 else "V", T[buf][:], (buf,), T.inf[:, 0:W], ("inf",), T.lst[:, l0:l0 + 32], ("lst", l0, l0 + 32))
             for b in range(4):
-                end = i == NT - 1 and b == 3
-                w0 = 0 if t else 8 * i
-                mm(X[:, 32 * i + b:32 * i + 32:4], xb, T[buf][:, b::4], (buf,), T.wx[:, w0:w0 + 8], ("wx",), False, end and t > 0)
-                if t == 0:
-                    mm(X[:, 96 + 32 * i + b:128 + 32 * i:4], xb, T[buf][:, b::4], (buf,), T.wx[:, 24 + 8 * i:32 + 8 * i], ("wx",), False, end)
-        cpy(T[st][:, 0:n], (st, 0, n), X[:, 0:n], (xb,))
-        next_list(be)
+                mm(T[cb][:, b:64:4, i], cb, T[buf][:, b::4], (buf,), T.wr[:, 5:7, :, i], ("wr", 5, 7), i == 0 and b == 0, i == NT - 1 and b == 3)
+        ts(T[st][:, 0:96], (st, 0, 96), blk(cb, 0), (cb,), -B, None, A.add)
+        tt(T[tb][:, 0:96], (tb,), blk(xb, 0), (xb,), T[st][:, 0:96], (st, 0, 96), A.add)
+        next_list(be, lambda: ts(T[st][:, 96:192], (st, 96, 192), blk(cb, 1), (cb,), -STAMP, None, A.add))
 
     def find(be, q, last):
-        ge, rw, off, gt = "ge%d" % be, "rw%d" % be, "off%d" % be, "gt%d" % be
-        sg, ab, st = "sg%d" % be, "ab%d" % be, "st%d" % be
-        (X, xb), (Y, yb), (Z, zb) = [(T["b%d" % (n + be)], "b%d" % (n + be)) for n in (0, 2, 4)]
-        src = T.xs[:, 0:W].indirect(T[off][:])
-        op("V", lambda e: e.tensor_tensor(T[ge][:], src, T.wf[:, H * be:H * be + H], A.is_ge), [("xs",), (off,), ("wf", H * be, H * be + H)], [(ge,)], None, us(1.5 * H))
-        gather("S", T[rw][:], (rw,), T.inf, "inf", 0, W, T[off][:], (off,))
-        mm(Y[:, 0:192], yb, *I16, T[gt][:], (gt,), True, False)
-        mm(X[:, 0:192], xb, T.stl[:, 128 * q:128 * q + 128], ("stl", 128 * q, 128 * q + 128), T.ones[:], ("ones",), True, False)
-        mm(Z[:, 0:96], zb, *IH, T[gt][:, 0:96], (gt, 0, 96), True, False)
-        mm(Z[:, 0:32], zb, *IMH, T[gt][:, 64:96], (gt, 0, 96), False, False)
-        mm(Z[:, 32:96], zb, *IMH, T[gt][:, 0:64], (gt, 0, 96), False, False)
-        for b in range(4):
-            mm(Y[:, b:96:4], yb, T[rw][:, b::4], (rw,), T.wbit[:], ("wbit",), False, False)
-        for b in range(4):
-            mm(Y[:, b:192:4], yb, T[ge][:, b::4], (ge,), T.wcnt[:], ("wcnt",), False, b == 3)
-        for b in range(4):
-            mm(X[:, b:192:4], xb, T[rw][:, b::4], (rw,), T.wx[:], ("wx",), False, False)
-        act(T[sg][:], (sg,), Y[:, 0:192], (yb,), AF.Sign, bias=-8.5)
-        mm(Z[:, 0:96], zb, *IM, T[sg][:, 96:192], (sg,), False, True)
-        mm(X[:, 0:96], xb, *IBIG, T[sg][:, 0:96], (sg,), False, False)
-        mm(X[:, 96:192], xb, *IBIG, T[sg][:, 0:96], (sg,), False, True)
-        act(T[ab][:], (ab,), Z[:, 0:96], (zb,), AF.Abs)
-        act(T[gt][:, 0:96], (gt, 0, 96), T[ab][:], (ab,), AF.Sign, bias=-1.5)
-        tt("V", T[st][:, 0:96], (st, 0, 96), X[:, 0:96], (xb,), T[st][:, 0:96], (st, 0, 96), A.max)
+        ge, rw, off, sg, st, tb = [n % be for n in ("ge%d", "rw%d", "off%d", "sg%d", "st%d", "tb%d")]
+        yb, xb, cb = ["b%d" % (n + be) for n in (0, 2, 4)]
+        gather_tt(T[ge][:], (ge,), T.xs[:, 0:W], ("xs",), T[off][:], (off,), T.wf[:, H * be:H * be + H], ("wf", H * be, H * be + H), A.is_ge)
+        gather("S", T[rw][:], (rw,), T.inf[:, 0:W], ("inf",), T[off][:], (off,))
+        own(be, yb, 0, I16, True, False)
+        own(be, yb, 2, I16, False, False)
+        after(be, yb, 1, I16, False)
 
-        def cursors_too():
-            tt("V", T[st][:, 96:192], (st, 96, 192), X[:, 96:192], (xb,), T[st][:, 96:192], (st, 96, 192), A.max)
+        def rows(bank, n, src, w, wreg, start, stop, q0=0):
+            for b in range(4):
+                mm(T[bank][:, 32 * q0 + b:32 * (q0 + n):4, 0:3], bank, T[src][:, b::4], (src,), w, wreg, start and b == 0, stop and b == 3)
+        rows(yb, 3, rw, T.wr[:, 0:3, :, :], ("wr", 0, 3), False, False)
+        rows(yb, 3, ge, T.wg[:], ("wg",), False, True)
         if last:
-            cursors_too()
+            rows(cb, 1, rw, T.wr[:, 6, :, :], ("wr", 6, 7), True, False, 1)
         else:
-            next_list(be, cursors_too, "ab%d")
+            rows(xb, 2, rw, T.wr[:, 3:5, :, :], ("wr", 3, 5), True, False)
+            rows(cb, 2, rw, T.wr[:, 5:7, :, :], ("wr", 5, 7), True, False)
+        act(T[sg][:], (sg,), blk(yb, 0, 3), (yb,), AF.Sign)
+        mv = (T[sg][:, 64:96, :], (sg,))
+        if not last:
+            mm(blk(xb, 0), xb, *IB, *mv, False, False)
+            mm(blk(xb, 1), xb, *IMB, *mv, False, False)
+            own(be, xb, 1, IB2, False, True)
+            mm(blk(cb, 0), cb, *IMB, *mv, False, False)
+        mm(blk(cb, 1), cb, T.stl[:, q, :], ("stl", q, q + 1), *mv, False, True)
+        if last:
+            tt(T[st][:, 96:192], (st, 96, 192), blk(cb, 1), (cb,), T[st][:, 96:192], (st, 96, 192), A.min)
+            return
+        tt(T[st][:, 0:96], (st, 0, 96), blk(xb, 0), (xb,), T[st][:, 0:96], (st, 0, 96), A.max)
+        tt(T[tb][:, 0:96], (tb,), blk(xb, 1), (xb,), T[st][:, 0:96], (st, 0, 96), A.min)
+        next_list(be, lambda: tt(T[st][:], (st,), blk(cb, 0, 2), (cb,), T[st][:], (st,), A.min))
 
-    def finds(be, t):
-        round_start(be, t)
+    def finds(be):
+        round_start(be)
         for q in range(FINDS):
-            find(be, FINDS * t + q + 1, q == FINDS - 1)
-        rec[0].append(None)
+            find(be, q, q == FINDS - 1)
         places(be)
 
-    def diag(bank, c0, c1, d, src, s0, s1):
-        for i in range(16):
-            mm(T[bank][:, c0:c1], bank, T[d][:, i, :, :], (d,), T[src][:, s0 + i:s1:16], (src, s0, s1), i == 0, i == 15)
-
-    def slot_list(bank, src, stop):
-        P = T[bank]
-        mm(P[:, 128:256], bank, T[src][:], (src,), T.bo[:], ("bo",), True, True)
-        tt("V", T.lk[:], ("lk",), P[:, 128:256], (bank,), T.km[:], ("km",), A.mult)
-        mm(P[:, 0:8], bank, T.lk[:], ("lk",), T.bo[:, 0:128:16], ("bo",), True, stop)
-
     def places(be):
-        st, gt, tb, ub, ac, mp = [n % be for n in ("st%d", "gt%d", "tt%d", "tu%d", "ac%d", "mp%d")]
-        Y, yb, O, ob = T["b%d" % (2 + be)], "b%d" % (2 + be), T["b%d" % (6 + be)], "b%d" % (6 + be)
-        a, b = 64 * be, 64 * be + 64
-        mm(Y[:, 0:64], yb, T.c72[:], ("c72",), T.ones[:, 0:64], ("ones",), True, False)
+        st, ci, tb, sc, lte = [n % be for n in ("st%d", "ci%d", "tb%d", "sc%d", "lte%d")]
+        xb, ob = "b%d" % (2 + be), "b%d" % (6 + be)
+        own(be, xb, 0, IB2, True, False)
+        mm(blk(xb, 0), xb, *I1, T.kz[:, :, 1:4], ("kz",), False, False)
+        own(be, xb, 1, IB2, False, False)
+        mm(blk(xb, 2), xb, *I1, T.kz[:, :, 0:3], ("kz",), False, False)
+        after(be, xb, 2, IB2, True)
+        ts(T[ci][:, 192:288], (ci, 192, 288), T[st][:, 96:192], (st, 96, 192), -4.0, None, A.mult)
+        ts(T[ci][:, 0:96], (ci, 0, 96), T[ci][:, 192:288], (ci, 192, 288), TS - 1, None, A.bitwise_and)
+        for i in range(NT):
+            ts(T[ci][:, 96 + i:192:3], (ci, 96, 192, i), T[ci][:, 192 + i:288:3], (ci, 192, 288), TS << (i + 1) % NT, None, A.bitwise_and)
+        tt(T[tb][:, 192:288], (tb, 192, 288), blk(xb, 2), (xb,), T[ci][:, 0:96], (ci, 0, 96), A.add)
+        tt(T[tb][:, 0:192], (tb, 0, 192), blk(xb, 0, 2), (xb,), T[ci][:, 0:192], (ci, 0, 192), A.add)
+        scan(T[sc][:], (sc,), T.rs3[:], ("rs3",), T[tb][:], (tb,), A.max)
+        tt(T[tb][:, 0:32], (tb,), T[sc][:, 2:96:3], (sc,), T[sc][:, 194:288:3], (sc,), A.not_equal)
+        tt(T[sc][:, 98:192:3], (sc,), T[tb][:, 0:32], (tb,), T[sc][:, 98:192:3], (sc,), A.min)
+        masks(lambda h: T[lte][:, :, h, :], lte, T[sc][:, 2:288:3], (sc,), 2)
+        mm(flat(ob, 64, 96), ob, T[lte][:, 8:16, :, :], (lte,), T.sel[:], ("sel",), True, False)
+        if be:
+            mm(flat(ob, 96, 128), ob, T.lte0[:, 8:16, :, :], ("lte0",), T.tri[:, 32:64], ("tri",), False, False)
+        mm(flat(ob, 96, 128), ob, T[lte][:, 8:16, :, :], (lte,), T.tri[:, 0:32], ("tri",), False, True)
+        cpy(T.wp[:, :, 32 * be:32 * be + 32], ("wp", 0, 64, be), flat(ob, 64, 128), (ob,))
         for s in range(2):
-            mm(Y[:, 32 * s:32 * s + 32], yb, *IW1, T[gt][:, 0:32], (gt, 0, 96), False, False)
-            mm(Y[:, 32 * s:32 * s + 32], yb, *IW2, T[gt][:, 32:64], (gt, 0, 96), False, s == 1)
-        tt("V", T[ac][:, 0:32], (ac, 0, 32), T[st][:, 96:128], (st,), T[gt][:, 64:96], (gt, 0, 96), A.mult)
-        tt("V", T[ac][:, 32:96], (ac, 32, 96), T[st][:, 128:192], (st,), T[gt][:, 0:64], (gt, 0, 96), A.mult)
-        pick(be, 96)
-        tt("V", T.mz[:, a:a + 32], ("mz", a, a + 32), T[ub][:], (ub,), T[tb][:, 64:96], (tb,), A.max)
-        tt("V", T[mp][:], (mp,), T[ac][:, 0:32], (ac,), T[ac][:, 32:64], (ac,), A.max)
-        tt("V", T.mz[:, a + 32:b], ("mz", a + 32, b), T[mp][:], (mp,), T[ac][:, 64:96], (ac,), A.max)
-        cpy(T.mzi[:, a:b], ("mzi", a, b), T.mz[:, a:b], ("mz", a, b))
-        ts(T.mzi[:, 128 + a:128 + b], ("mzi", 128 + a, 128 + b), T.mzi[:, a:b], ("mzi", a, b), STAMP - 1, None, A.bitwise_and)
-        tt("V", T.mp4[:, 16 * be:16 * be + 16, :], ("mp4", a, b), Y[:, 0:64], (yb,), T.mzi[:, 128 + a:128 + b], ("mzi", 128 + a, 128 + b), A.add)
-        masks(lambda h: T.lte[:, 16 * be:16 * be + 16, h, :], "lte", 256 * be, 256 * be + 256, T.mp4[:, 16 * be:16 * be + 16, :], ("mp4", a, b), 2)
-        for s in range(2):
-            n = 16 * be + 8 * s
-            mm(O[:, 32 * s:32 * s + 32], ob, T.lte[:, n:n + 8, :, :], ("lte", 256 * be, 256 * be + 256), T.sel[:], ("sel",), True, True)
-        cpy(T.ot[:, a:b], ("ot", a, b), O[:, 0:64], (ob,))
-        gather("S" if be else "V", T.ra[:, H * be:H * be + H], ("ra", H * be, H * be + H), T.pw, "pw", 0, 3 * W, T.ot[:, a:a + 32], ("ot", a, b))
-        cpy(T.otf[:, a // 2:b // 2], ("otf", a // 2, b // 2), O[:, 0:32], (ob,))
-        tt("V", T.nq[:, a // 2:b // 2], ("nq", a // 2, b // 2), O[:, 32:64], (ob,), T.otf[:, a // 2:b // 2], ("otf", a // 2, b // 2), A.not_equal)
+            mm(flat(ob, 32 * s, 32 * s + 32), ob, T[lte][:, 16 * s:16 * s + 8, :, :], (lte,), T.sel[:], ("sel",), s == 0, s == 1)
+        cpy(T.pl[:, :, 32 * be:32 * be + 32], ("pl", 0, 72, be), flat(ob, 0, 64), (ob,))
 
     def swap(last):
-        gather("S", T.rb[:, H:K], ("rb", H, K), T.pw, "pw", 0, 3 * W, T.ot[:, 96:128], ("ot", 64, 128))
-        gather("V", T.rb[:, 0:H], ("rb", 0, H), T.pw, "pw", 0, 3 * W, T.ot[:, 32:64], ("ot", 0, 64))
-        diag("b2", 0, 64, "db", "ra", 0, K)
-        tt("V", T.wt[:], ("wt",), T.b2[:, 0:64], ("b2",), T.nq[:], ("nq",), A.mult)
-        op("V", lambda e: e.tensor_tensor_scan(T.pc[:], T.ones[:, 0:64], T.wt[:], 0.0, A.mult, A.add), [("ones",), ("wt",)], [("pc",)])
-        mm(T.b3[:, 0:64], "b3", T.bo[:], ("bo",), T.pc[:], ("pc",), True, True)
-        mm(T.b2[:, 64:128], "b2", T.bo[:], ("bo",), T.pc[:], ("pc",), True, False)
-        mm(T.b2[:, 64:128], "b2", T.lm[:], ("lm",), T.wt[:], ("wt",), False, True)
-        cpy(T.rt[:, 0:64], ("rt", 0, 64), T.b2[:, 64:128], ("b2",))
+        wt, pre = (T.wp[:, 0, :], ("wp",)), (T.wp[:, 1, :], ("wp",))
+        mm(flat("b3", 0, 64), "b3", T.bo[:], ("bo",), *pre, True, True)
+        mm(flat("b2", 64, 128), "b2", T.bo[:], ("bo",), *pre, True, False)
+        mm(flat("b2", 0, 64), "b2", T.bo[:], ("bo",), *pre, False, False)
+        mm(flat("b2", 0, 64), "b2", T.lm[:], ("lm",), *wt, False, True)
         for n in range(8):
-            act(T.junk[:, 64 * n:64 * n + 64], ("junk", 64 * n, 64 * n + 64), T.b3[:, 0:64], ("b3",), AF.Sign, bias=T.kch[:, n:n + 1], scale=-1.0, extra=[("kch",)], accum=T.ck[:, n:n + 1], ao=("ck", n, n + 1))
-        ts(T.ckl[:], ("ckl",), T.ck[:], ("ck",), 0.5, 32.0, A.mult, A.add)
-        src = T.rt[:, 0:72].indirect(T.ckl[:])
-        op("V", lambda e: e.tensor_tensor(T.le[:], src, T.kio[:], A.is_le), [("rt",), ("ckl",), ("kio",)], [("le",)])
-        ts(T.ckb[:], ("ckb",), T.ck[:], ("ck",), 0.5, 32.0, A.mult, A.add)
-        slot_list("b2", "le", False)
-        mm(T.b2[:, 0:8], "b2", *I16, T.ckb[:], ("ckb",), False, True)
-        cpy(T.jk[:], ("jk",), T.b2[:, 0:8], ("b2",))
-        gather("V", T.sab[:, 0:128], ("sab", 0, 128), T.ra, "ra", 0, K + 16, T.jk[:], ("jk",))
-        gather("S", T.sab[:, 128:256], ("sab", 128, 256), T.rb, "rb", 0, K + 16, T.jk[:], ("jk",))
-        mm(T.b3[:, 0:256], "b3", T.plw[:], ("plw",), T.sab[:], ("sab",), True, True)
-        diag("b6", 0, 16, "dp", "sab", 0, 256)
-        cpy(T.plr[:], ("plr",), T.b3[:, 0:256], ("b3",))
-        cpy(T.plt[:], ("plt",), T.b6[:, 0:16], ("b6",))
+            jk = (T.eq[:, 64 * n:64 * n + 64], ("eq", 64 * n, 64 * n + 64))
+            if n < NV:
+                ts(*jk, flat("b2", 64, 128), ("b2",), T.kc[:, n:n + 1], None, A.is_le, extra=[("kc",)])
+                op("V", lambda e, n=n, jk=jk: e.tensor_reduce(T.ck[:, n:n + 1], jk[0], AxisListType.X, A.add), [jk[1]], [("ck", n, n + 1)])
+            else:
+                act(*jk, flat("b3", 0, 64), ("b3",), AF.Sign, bias=T.kch[:, n:n + 1], scale=-1.0, extra=[("kch",)], accum=T.ck[:, n:n + 1], ao=("ck", n, n + 1))
+        tt(T.rt[:, 0:64], ("rt", 0, 64), flat("b2", 0, 64), ("b2",), *wt, A.mult)
+        if NV:
+            cpy(T.ckl[:, 0:NV], ("ckl", 0, NV), T.ck[:, 0:NV], ("ck", 0, NV))
+        ts(T.ckl[:, NV:8], ("ckl", NV, 8), T.ck[:, NV:8], ("ck", NV, 8), 0.5, 32.0, A.mult, A.add)
+        gather_tt(T.oh[:], ("oh",), T.rt[:, 0:72], ("rt",), T.ckl[:], ("ckl",), T.kio[:], ("kio",), A.is_equal)
+        for s in range(2):
+            gather_tt(T.pr[:, 128 * s:128 * s + 128], ("pr", s, s + 1), T.pl[:, s, :], ("pl",), T.ckl[:], ("ckl",), T.oh[:], ("oh",), A.mult)
+            mm(flat("b3", 128 * s, 128 * s + 128), "b3", T.bof[:], ("bof",), T.pr[:, 128 * s:128 * s + 128], ("pr", s, s + 1), s == 0, s == 1)
+        tt(T.mk[:], ("mk",), flat("b3", 0, 256), ("b3",), T.km[:], ("km",), A.mult)
+        scan(T.plt[:], ("plt",), T.r16[:], ("r16",), T.mk[:], ("mk",), A.add)
+        cpy(T.plr[:], ("plr",), flat("b3", 0, 256), ("b3",))
+        plt = (T.plt[:, 15::16], ("plt",))
+        cpy(T.si[:, 0:16], ("si", 0, 16), *plt)
+        act(T.ab[:], ("ab",), flat("b3", 0, 128), ("b3",), AF.Abs, bias=co[:, 11:12], extra=[("cols", 11, 12)])
+        act(flat("b2", 0, 128), ("b2",), T.ab[:], ("ab",), AF.Sign, bias=W / 2.0 + 0.5, scale=-1.0)
         for n in range(16):
             a = 256 * (n % NEQ)
-            ts(T.eq[:, a:a + 256], ("eq", a, a + 256), T.plr[:], ("plr",), T.plt[:, n:n + 1], None, A.is_equal, extra=[("plt",)])
+            ts(T.eq[:, a:a + 256], ("eq", a, a + 256), T.plr[:], ("plr",), T.plt[:, 16 * n + 15:16 * n + 16], None, A.is_equal, extra=[("plt",)], fast=0.5)
             for s in range(2):
-                mm(T.b7[:, 0:128], "b7", T.bo[:], ("bo",), T.eq[:, a + 128 * s:a + 128 * s + 128], ("eq", a, a + 256), n == 0 and s == 0, n == 15 and s == 1)
-        tt("V", T.dab[:], ("dab",), T.sab[:, 128:256], ("sab",), T.sab[:, 0:128], ("sab",), A.subtract)
-        tt("V", T.pd[:], ("pd",), T.plt[:], ("plt",), T.dumc[:], ("dumc",), A.subtract)
-        ts(T.cb[:], ("cb",), T.b7[:, 0:128], ("b7",), 2.0, 1.0 / 16, A.is_equal, A.mult)
-        ts(T.cp[:], ("cp",), T.b7[:, 0:128], ("b7",), 2.0, co[:, 10:11], A.is_equal, A.mult, extra=[("cols", 10, 11)])
-        slot_list("b3", "cb", True)
-        tt("V", T.dmv[:], ("dmv",), T.dab[:], ("dab",), T.cp[:], ("cp",), A.mult)
-        for s in range(2):
-            tt("V", T.of[:, 8 * s:8 * s + 8], ("of", 8 * s, 8 * s + 8), T.b3[:, 0:8], ("b3",), T.pd[:, 8 * s:8 * s + 8], ("pd",), A.mult)
-        tt("V", T.nv[:, 0:128], ("nv", 0, 128), T.sab[:, 0:128], ("sab",), T.dmv[:], ("dmv",), A.add)
-        tt("V", T.of[:, 16:32], ("of", 16, 32), T.of[:, 0:16], ("of", 0, 16), T.dumc[:], ("dumc",), A.add)
-        tt("V", T.nv[:, 128:256], ("nv", 128, 256), T.sab[:, 128:256], ("sab",), T.dmv[:], ("dmv",), A.subtract)
-        cpy(T.ofl[:], ("ofl",), T.of[:, 16:32], ("of", 16, 32))
-        out = T.pw[:, 0:3 * W + 2 * CAP].indirect(T.ofl[:])
-        op("V", lambda e: e.tensor_copy(out, T.nv[:]), [("nv",), ("ofl",)], [("pw",)], None, 1.0)
-        if not last:
-            for i in range(NT):
-                for k in range(2):
-                    dma("Y", T.inf[2 * i + k::16, :], ("inf", 0, W, 2 * i + k), T.pw[k::16, W * i:W * i + W], ("pw", W * i, W * i + W, k), "d_rb")
-            return
-        dma("Y", T.yh[:], ("yh",), T.pw[0::16, 0:3 * W], ("pw", 0, 3 * W, 0), "d_y1")
-        dma("Y", T.yl[:], ("yl",), T.pw[1::16, 0:3 * W], ("pw", 0, 3 * W, 1), "d_y1")
-        parts = [(384 * i, 384 * i + 384, ("b3", "b6", "b7")[i]) for i in range(NT)]
-        for a, b, bank in parts:
-            mm(T[bank][:, 0:384], bank, T.idb[:], ("idb",), T.yh[:, a:b], ("yh",), True, False)
-            mm(T[bank][:, 0:384], bank, T.idb[:], ("idb",), T.yl[:, a:b], ("yl",), False, True)
-        for n, (a, b, bank) in enumerate(parts):
+                mm(flat("b7", 0, 128), "b7", T.eq[:, a + 128 * s:a + 128 * s + 128], ("eq", a, a + 256), T.bo[:], ("bo",), n == 0 and s == 0, n == 15 and s == 1)
+            if n == 0:
+                ts(T.si[:, 16:32], ("si", 16, 32), T.si[:, 0:16], ("si", 0, 16), TS - 1, None, A.bitwise_and)
             if n == 1:
-                act(T.yf[:, a:b], ("yf", a, b), T[bank][:, 0:384], (bank,), AF.Copy)
-            else:
-                cpy(T.yf[:, a:b], ("yf", a, b), T[bank][:, 0:384], (bank,))
-        dma("Y", T.yn[:], None, T.yf[:], ("yf",), "d_yn1")
+                cpy(T.sl[:], ("sl",), T.si[:, 16:32], ("si", 16, 32))
+                gather("S", T.gs[:], ("gs",), T.inf[:, 0:W], ("inf",), T.sl[:], ("sl",))
+            if n == 2:
+                tt(T.pd[:], ("pd",), *plt, T.dum[:, 16:32], ("dum",), A.subtract)
+            if n in (7, 8):
+                a = 128 * (n - 7)
+                tt(T.gz[:, a:a + 128], ("gz", a, a + 128), flat("b2", 0, 128), ("b2",), T.gs[:, a:a + 128], ("gs",), A.mult)
+                for k, src in enumerate(("gs", "gz")):
+                    mm(flat("b3", 128 - a, 256 - a), "b3", T.wn[:], ("wn",), T[src][:, a:a + 128], (src, a, a + 128), n == 7 and k == 0, n == 8 and k == 1)
+        nv = "nvf" if last else "nvb"
+        act(T[nv][:], (nv,), flat("b3", 0, 256), ("b3",), AF.Copy)
+        tt(T.lk[:], ("lk",), flat("b7", 0, 128), ("b7",), T.k3[:], ("k3",), A.is_equal)
+        for s in range(2):
+            mm(flat("b6", 8 * s, 8 * s + 8), "b6", T.lk[:], ("lk",), T.bo[:, 0:128:16], ("bo",), s == 0, s == 1)
+        tt(T.of[:, 0:16], ("of", 0, 16), flat("b6", 0, 16), ("b6",), T.pd[:], ("pd",), A.mult)
+        tt(T.of[:, 16:32], ("of", 16, 32), T.of[:, 0:16], ("of", 0, 16), T.dum[:, 0:16], ("dum",), A.add)
+        cpy(T.ofl[:], ("ofl",), T.of[:, 16:32], ("of", 16, 32))
+        win, src = ("pwf", "nvf") if last else ("pwb", "nvb")
+        out = T[win][:, 0:PW].indirect(T.ofl[:])
+        op("V", lambda e: e.tensor_copy(out, T[src][:]), [(src,), ("ofl",)], [(win,)], None, 1.0)
+        for i in range(NT):
+            if last:
+                dma("Y", T.yn[:, W * i:W * i + W], None, T.pwf[2::16, TS * i:TS * i + W], ("pwf", TS * i, TS * i + W), "d_yn")
+                continue
+            for k in range(2):
+                dma("Y", T.inf[2 * i + k::16, :], ("inf", 0, W, 2 * i + k), T.pwb[k::16, TS * i:TS * i + W], ("pwb",), "d_rb")
+
+    def whole_numbers():
+        for k in range(2):
+            for i in range(NT):
+                o, a = T.pwf[2::16, TS * i:TS * i + W], T.pwb[k::16, TS * i:TS * i + W]
+                if k == 0:
+                    op("G", lambda e, o=o, a=a: e.dma_start(o, a), [("pwb",), ("inf",)], [("pwf", TS * i, TS * i + W)], "d_pf")
+                else:
+                    op("G", lambda e, o=o, a=a: e.dma_start(o, a, accum_op=A.add, max_dma_last_dim=4096), [("pwb",)], [("pwf", TS * i, TS * i + W)], "d_pf")
 
     def cursors(last):
         for be in range(2):
-            for h in range(4):
-                act(T.ltc[:, 24 * be:24 * be + 24, h, :], ("ltc", 384 * be, 384 * be + 384, h), T["st%d" % be][:, 96:192], ("st%d" % be,), AF.Copy, scale=co[:, h:h + 1], extra=[("cols", h, h + 1)])
-        for be in range(2):
+            ci, cf, ltc, cb = "ci%d" % be, "cf%d" % be, "ltc%d" % be, "b%d" % (4 + be)
+            late[0] = -SOON
+            cpy(T[cf][:], (cf,), T[ci][:, 0:96], (ci, 0, 96))
+            late[0] = 0.0
+            masks(lambda h: T[ltc][:, :, h, :], ltc, T[cf][:], (cf,), 4)
             for i in range(NT):
-                n = 3 * be + i
-                mm(T.b5[:, 64 * i + 32 * be:64 * i + 32 * be + 32], "b5", T.ltc[:, 8 * n:8 * n + 8, :, :], ("ltc", 384 * be, 384 * be + 384), T.sel[:], ("sel",), True, True)
-        cpy(T.ci[:, 0:192], ("ci", 0, 192), T.b5[:, 0:192], ("b5",))
-        ts(T.ci[:, 192:384], ("ci", 192, 384), T.ci[:, 0:192], ("ci", 0, 192), STAMP - 1, None, A.bitwise_and)
+                mm(flat(cb, 32 * i, 32 * i + 32), cb, T[ltc][:, :, :, i::3], (ltc,), T.sel[:], ("sel",), i == 0, i == NT - 1)
+            if last:
+                act(T.ycf[:, :, be, :], ("ycf", be, be + 1), flat(cb, 0, 96), (cb,), AF.Copy)
+            else:
+                cpy(T.lst[:, 96 * be:96 * be + 96], ("lst", 96 * be, 96 * be + 96), flat(cb, 0, 96), (cb,))
         if last:
-            cpy(T.ycf[:], ("ycf",), T.ci[:, 192:384], ("ci", 192, 384))
-            dma("Y", T.yc[:], None, T.ycf[:], ("ycf",), "d_yc")
-        else:
-            for i in range(NT):
-                a, b = 64 * i, 64 * i + 64
-                ts(T.lst[:, a:b], ("lst", a, b), T.ci[:, 192 + a:192 + b], ("ci", 192, 384), W * i, None, A.add)
+            dma("S", T.yc[:], None, T.ycf[:], ("ycf",), "d_yc")
+
+    def foreign():
+        late[0] = -SOON
+        cpy(T.mi[:, 0:64], ("mi", 0, 64), T.pl[:, 0, 0:64], ("pl",))
+        ts(T.mi[:, 64:128], ("mi", 64, 128), T.mi[:, 0:64], ("mi", 0, 64), TS - 1, None, A.bitwise_and)
+        cpy(T.ml[:], ("ml",), T.mi[:, 64:128], ("mi", 64, 128))
+        late[0] = 0.0
+        for be in range(2):
+            rw, lt, yb = "rw%d" % be, "lt%d" % be, "b%d" % be
+            gather("S", T[rw][:], (rw,), T.inf[:, 0:W], ("inf",), T.ml[:, 32 * be:32 * be + 32], ("ml",))
+            for b in range(4):
+                mm(T[yb][:, 0:8, b], yb, T[rw][:, b::4], (rw,), T.wr[:, 7, :, 0], ("wr", 7, 8), b == 0, b == 3)
+            masks(lambda h: T[lt][:, :, h, :], lt, flat(yb, 0, 32), (yb,), 4)
+            mm(flat(yb, 0, 32), yb, T[lt][:], (lt,), T.sel[:], ("sel",), True, True)
+            cpy(T.kl[:, 32 * be:32 * be + 32], ("kl", be, be + 1), flat(yb, 0, 32), (yb,))
 
     def pull(t, last):
-        diag("b4", 64, 128, "df", "ra", 0, K)
-        cpy(T.kl[:], ("kl",), T.b4[:, 64:128], ("b4",))
         xn = "x%d" % (t + 1)
         for be in range(2):
-            a, b = H * be, H * be + H
-            ysrc = T[xn][:, 0:W].indirect(T.kl[:, 32 * be:32 * be + 32])
-            op("V", lambda e, ysrc=ysrc, a=a, b=b: e.tensor_tensor(T.dd[:, a:b], ysrc, T.wf[:, a:b], A.subtract), [(xn,), ("kl",), ("wf", a, b)], [("dd", a, b)], None, us(1.5 * H))
-            D, dn = T["b%d" % be], "b%d" % be
-            ts(D[:], (dn,), T.dd[:, a:b], ("dd", a, b), 8.0, -8.0, A.min, A.max)
-            tt("V", T.wf[:, a:b], ("wf", a, b), D[:], (dn,), T.wf[:, a:b], ("wf", a, b), A.add)
+            a, b, dn = H * be, H * be + H, "b%d" % be
+            gather_tt(*room("dd", a, b), T[xn][:, 0:W], (xn,), T.kl[:, 32 * be:32 * be + 32], ("kl", be, be + 1), T.wf[:, a:b], ("wf", a, b), A.subtract)
+            ts(T[dn][:], (dn,), *room("dd", a, b), 8.0, -8.0, A.min, A.max)
+            tt(T.wf[:, a:b], ("wf", a, b), T[dn][:], (dn,), T.wf[:, a:b], ("wf", a, b), A.add)
             if last:
                 dma("S", T.yw[:, a:b], None, T.wf[:, a:b], ("wf", a, b), "d_yw%d" % be)
 
-    types_in()
+    later()
+    if not direct(rank + 1):
+        send("x2", "x1", at(rank - 1), "rx2", topo.engines(core, at(rank - 1)))
     for t in range(ROUNDS):
         last = t == ROUNDS - 1
-        streams = [(record(finds, 0, t), 0.0), (record(finds, 1, t), FB)]
-        if t == 0:
-            streams.append((record(later), LB))
-        merge(*streams)
-        merge((record(swap, last), 0.0), (record(cursors, last), CB), (record(pull, t, last), PB))
+        finds(0)
+        late[0] = FB
+        finds(1)
+        late[0] = 0.0
+        cursors(last)
+        foreign()
+        swap(last)
+        pull(t, last)
+        if not last:
+            whole_numbers()
+    if len(calls) not in PLANS:
+        PLANS[len(calls)] = plan()
+    for n in PLANS[len(calls)]:
+        emit(*calls[n][:6])
     for s in sorted(total):
         know("G", s, total[s])

@@ -9,12 +9,13 @@ TS = 8192
 PW = 2 * TS + W
 B, B2, STAMP = 16384.0, 32768.0, 16384.0
 NEQ = 4
-MS = 2
+MS = 3
+MP = (4, 2)
 NV = 3
 XA = 2048
-FB = 1.5
+FB = 0.5
 SOON = 4.0
-WAKE, FLY, RATE = 0.05, 2.0, 3e5
+WAKE, FLY, RATE = 0.12, 2.0, 3e5
 SB, BF, FP, I32, U16 = "sbuf", "bfloat16", "float32", "int32", "uint16"
 SCRATCH = {
     "xs": (SB, [128, W], BF), "x1": (SB, [128, W], BF), "x2": (SB, [128, W], BF), "inf": (SB, [128, W], BF),
@@ -25,7 +26,7 @@ SCRATCH = {
     "wr": (SB, [128, 8, 8, 3], BF), "wg": (SB, [128, 72], BF), "sel": (SB, [128, 32], FP), "tri": (SB, [128, 64], FP), "selr": (SB, [128, 32], BF),
     "rs3": (SB, [128, 288], FP), "r16": (SB, [128, 256], FP), "kz": (SB, [128, 32, 4], BF),
     "pid": (SB, [128, 1], I32), "pm": (SB, [128, 8], I32), "cols": (SB, [128, 16], FP), "ttl": (SB, [128, 64, 4], BF),
-    "bo": (SB, [128, 128], BF), "bof": (SB, [128, 128], FP), "lm": (SB, [128, 128], BF), "wn": (SB, [128, 8, 16], BF),
+    "bo": (SB, [128, 128], BF), "bof": (SB, [128, 128], FP), "idm": (SB, [128, 128], FP), "lm": (SB, [128, 128], BF), "wn": (SB, [128, 8, 16], BF),
     "km": (SB, [128, 256], BF), "k3": (SB, [128, 128], BF),
     "kc": (SB, [128, 8], FP), "kch": (SB, [128, 8], FP), "dum": (SB, [128, 32], FP), "kio": (SB, [128, 128], FP),
     "pl": (SB, [128, 2, 72], FP), "wp": (SB, [128, 2, 64], BF), "rt": (SB, [128, 72], FP),
@@ -37,7 +38,7 @@ SCRATCH = {
     "mi": (SB, [128, 128], I32), "ml": (SB, [128, 64], U16), "kl": (SB, [128, 64], U16),
 }
 ROOMS = {"fm": ("pwb", 0), "vr": ("pwb", 1152), "wb": ("pwb", 2 * TS), "nhi": ("pwb", W + 2 * CAP), "nlo": ("pwb", TS + W),
-         "pv": ("pwf", W + 2 * CAP), "dd": ("pwf", TS + W)}
+         "pv": ("pwf", W + 2 * CAP)}
 for _b in range(2):
     for _n, _s, _d in (("ge", [128, H], BF), ("rw", [128, H], BF), ("off", [128, 32], U16), ("st", [128, 192], FP), ("sg", [128, 96, 3], BF),
                        ("tb", [128, 288], FP), ("sc", [128, 288], FP), ("lt", [128, 8, 4, 4], FP), ("lte", [128, 24, 4, 4], FP),
@@ -46,9 +47,16 @@ for _b in range(2):
 for _i in range(8):
     SCRATCH["b%d" % _i] = ("psum", [128, 128, 4], FP)
 ENG = {"V": "cv", "S": "cs", "P": "cp_", "G": "cg"}
-DMAS = ["l_n", "l_m", "l_c", "l_t", "l_x", "l_w", "d_bi", "d_pb", "d_pf", "d_rb", "d_yc", "d_yw0", "d_yw1", "d_yn"]
+DMAS = ["l_n", "l_m", "l_c", "l_t", "l_x", "l_w", "d_bi", "d_fl", "d_pb", "d_pf", "d_rb", "d_yc", "d_yw0", "d_yw1", "d_yn"]
 SEMAPHORES = sorted(ENG.values()) + DMAS + ["rx1", "rx2", "tx"]
 PLANS = {}
+TURNS = {
+    "V": [("gather", 0, 0), ("list", 1, 1), ("keep", 1, 1), ("gather", 1, 0), ("max", 0, 0), ("min", 0, 0), ("scan", 0, 0), ("max", 1, 0),
+          ("mask", 0, 0), ("min", 1, 0), ("keep", 0, 0), ("scan", 1, 0), ("list", 0, 0), ("mask", 1, 0)],
+    "S": [("gather", 0, 0), ("gather", 1, 0), ("sign", 0, 0), ("sign", 1, 0), ("mask", 0, 0), ("mask", 1, 0)],
+    "P": [("list", 1, 1), ("own", 0, 0), ("count", 0, 0), ("rows", 0, 0), ("count", 1, 0), ("bounds", 0, 0), ("rows", 1, 0), ("bounds", 1, 0),
+          ("own", 1, -1), ("list", 0, 0)],
+}
 
 
 def rank_program(g, core, T, topo):
@@ -64,6 +72,7 @@ def rank_program(g, core, T, topo):
     calls = []
 
     late = [0.0]
+    mark, steps = [None], {}
 
     def know(q, sem, val):
         c = clock[q]
@@ -92,7 +101,7 @@ def rank_program(g, core, T, topo):
                     same = a[3] == q and not dma and a[4] not in DMAS
                     if not (wr or a[6]) and (not bank or same):
                         continue
-                    if same and (q == "P" or not a[6]):
+                    if same and q == "P":
                         continue
                     need[a[4]] = max(need.get(a[4], 0), a[5])
         return need
@@ -127,6 +136,10 @@ def rank_program(g, core, T, topo):
 
     def op(q, fn, reads, writes, dma=None, cost=0.1):
         calls.append((q, fn, reads, writes, dma, cost, late[0]))
+        steps.setdefault((q, mark[0]), []).append(len(calls) - 1)
+
+    def step(name):
+        mark[0] = (name,) + mark[0][1:]
 
     def plan():
         seen, before, g0 = {}, [], None
@@ -138,7 +151,7 @@ def rank_program(g, core, T, topo):
                     for a in seen.get((buf, True), []) + (seen.get((buf, False), []) if wr or bank else []):
                         same = calls[a[4]][0] == q and not dm and not calls[a[4]][4]
                         if a[0] < hi and lo < a[1] and (tag is None or a[2] is None or a[2] == tag) and (wr or a[3] or bank and not same):
-                            dep[a[4]] = max(dep.get(a[4], 0.0), 0.0 if same and (q == "P" or not a[3]) else WAKE)
+                            dep[a[4]] = max(dep.get(a[4], 0.0), 0.0 if same and q == "P" else WAKE)
             if q == "G":
                 if g0 is not None:
                     dep.setdefault(g0, None)
@@ -150,8 +163,25 @@ def rank_program(g, core, T, topo):
                     for key in ((buf, True), (buf, False)) if wr else ():
                         seen[key] = [a for a in seen.get(key, []) if not (lo <= a[0] and a[1] <= hi and (tag is None or tag == a[2]))]
                     seen.setdefault((buf, wr), []).append((lo, hi, tag, wr, n))
+        for q, turn in TURNS.items():
+            for t in range(ROUNDS):
+                line = [n for f in range(-1, FINDS + 1) for name, be, back in turn for n in steps.get((q, (name, be, t, f - back)), [])]
+                for m, n in zip(line, line[1:]):
+                    before[n].setdefault(m, 0.0)
+        after = [[] for _c in calls]
+        for n, d in enumerate(before):
+            for m in d:
+                after[m].append(n)
+        left = [len(d) for d in before]
+        order = [n for n in range(len(calls)) if not left[n]]
+        for n in order:
+            for m in after[n]:
+                left[m] -= 1
+                if not left[m]:
+                    order.append(m)
+        assert len(order) == len(calls)
         way = [0.0] * len(calls)
-        for n in range(len(calls) - 1, -1, -1):
+        for n in reversed(order):
             c = calls[n]
             way[n] += c[5] + (FLY if c[4] and c[4] != "tx" else 0.0)
             for m, lat in before[n].items():
@@ -170,10 +200,6 @@ def rank_program(g, core, T, topo):
             line.insert(k, (t, t + c))
             return t
         start, end, left = {}, {}, [len(d) for d in before]
-        after = [[] for _c in calls]
-        for n, d in enumerate(before):
-            for m in d:
-                after[m].append(n)
         ready = [n for n in range(len(calls)) if not left[n]]
         while ready:
             n = max(ready, key=lambda n: (way[n] - calls[n][6], -n))
@@ -305,11 +331,12 @@ def rank_program(g, core, T, topo):
         aff(T.wr[:, q0:q1, :, i0:i1], ("wr", q0, q1), [[0, q1 - q0], [-16, 8], [-step, i1 - i0]], A.not_equal, -row, 1, val)
 
     weight(3, 6, 0, 3, 0, 2, 1.0)
-    weight(6, 7, 0, 3, 9, 0, -0.25)
+    weight(6, 7, 0, 3, 9, 0, -1.0)
     weight(3, 6, 0, 3, 1, 2, 1.0)
-    weight(6, 7, 0, 3, 10, 0, -32.0)
+    weight(6, 7, 0, 3, 10, 0, -128.0)
     weight(4, 6, 0, 3, 13, 0, B)
-    weight(6, 7, 0, 3, 6, 0, -2048.0)
+    for i, row, v in ((0, 7, -1), (0, 8, 2), (0, 14, -192), (1, 8, -1), (1, 14, 192), (2, 6, -1), (2, 7, 2), (2, 14, -384)):
+        weight(6, 7, i, i + 1, row, 0, float(TS * v))
     aff(T.idn[:], ("idn",), [[0, 4], [-1, 128]], A.is_equal, 0)
     aff(T.sel[:], ("sel",), [[-4, 32]], A.is_ge, 0)
     weight(3, 4, 0, 3, 13, 0, -B)
@@ -348,8 +375,10 @@ def rank_program(g, core, T, topo):
             to_inf("Y", row + k, *room(src, 0, Q, 32 * i, 32 * i + 32))
         to_inf("Y", 7 + k, *room("fm", 384 * k + 384, 384 * k + 768))
 
+    late[0] = 10 * SOON
     dma("Y", *room("wb", 0, K), T.w0[:], room("nlo", 0, Q)[1], "l_w")
     dma("Y", T.xs[:, XA:W], ("xs", XA, W), T.x[:, XA:W], room("nlo", 0, Q)[1], "l_x")
+    late[0] = 0.0
 
     iota(T.kz[:], ("kz",), [[0, 32], [TS, 4]], TS, 0)
     iota(T.kc[:], ("kc",), [[16, 8]], 0, 1)
@@ -388,18 +417,26 @@ def rank_program(g, core, T, topo):
         op("G", lambda e: e.remote_dma(T[buf][:], T[src][:], T.sem[rx], T.sem.tx, pid, rid, sum(1 << n for n in eng)), [(src,), ("gate",)], [], "tx", 1.0)
         total["tx"] = total.get("tx", 0) + len(eng)
 
-    send("x1", "xs", at(rank - 1), "rx1", lanes(rank, 0))
-    if direct(rank):
-        send("x2", "xs", at(rank - 2), "rx2", lanes(rank, 1))
+    def sends():
+        send("x1", "xs", at(rank - 1), "rx1", lanes(rank, 0))
+        if direct(rank):
+            send("x2", "xs", at(rank - 2), "rx2", lanes(rank, 1))
+        for i in range(NT):
+            o = (T.pwb[:, TS * i:TS * i + W], ("pwb", TS * i, TS * i + W))
+            if i == 1:
+                dma("Y", *o, T.x[:], ("xs",), "d_fl")
+            else:
+                iota(*o, [[0, W]], 0, 0)
+            for k, src in enumerate(("nhi", "nlo")):
+                dma("Y", T.pwb[k::16, TS * i:TS * i + W], ("pwb", TS * i, TS * i + W, k), room(src, 0, Q, 32 * i, 32 * i + 32)[0], ("xs",), "d_pb")
+        if not direct(rank + 1):
+            send("x2", "x1", at(rank - 1), "rx2", topo.engines(core, at(rank - 1)))
     total["rx1"] = len(lanes(rank + 1, 0))
     total["rx2"] = len(lanes(rank + 2, 1) if direct(rank + 2) else topo.engines(at(rank + 1), core))
     for n in ("1", "2"):
         acc["x" + n] = [(0, 1 << 20, None, "R", "rx" + n, total["rx" + n], True)]
 
     def later():
-        for i in range(NT):
-            for k, src in enumerate(("nhi", "nlo")):
-                dma("Y", T.pwb[k::16, TS * i:TS * i + W], ("pwb", TS * i, TS * i + W, k), room(src, 0, Q, 32 * i, 32 * i + 32)[0], ("xs",), "d_pb")
         iota(T.kio[:], ("kio",), [[1, 128]], 1, 0)
         iota(T.tri[:], ("tri",), [[0, 64]], 1, 0)
         aff(T.tri[:], ("tri",), [[4, 64]], A.is_ge, 3, -1)
@@ -413,6 +450,10 @@ def rank_program(g, core, T, topo):
             aff(T.wn[:, :, r % 2:3:2 - r % 2], ("wn",), [[-16, 8], [0, 2]], A.not_equal, -r, 1, 0.5)
         weight(7, 8, 0, 1, 11, 0, 1.0)
         weight(7, 8, 0, 1, 12, 0, 1.0)
+        weight(7, 8, 1, 2, 0, 0, 1.0)
+        weight(7, 8, 1, 2, 1, 0, 1.0)
+        iota(T.idm[:], ("idm",), [[0, 128]], -1, 0)
+        aff(T.idm[:], ("idm",), [[-1, 128]], A.is_equal, 0)
         iota(T.r16[:], ("r16",), [[0, 16], [1, 16]], 0, 0)
         aff(T.r16[:], ("r16",), [[0, 16], [1, 16]], A.is_equal, 0, 0, 1.0)
         iota(T.rt[:, 64:72], ("rt", 64, 72), [[0, 8]], 0, 0)
@@ -451,31 +492,46 @@ def rank_program(g, core, T, topo):
 
     def next_list(be, more=None):
         tb, sc, lt, ob, off = [n % be for n in ("tb%d", "sc%d", "lt%d")] + ["b%d" % (6 + be), "off%d" % be]
+        step("scan")
         scan(T[sc][:, 0:96], (sc,), T.rs3[:, 0:96], ("rs3",), T[tb][:, 0:96], (tb,), A.max)
+        step("mask")
         masks(lambda h: T[lt][:, :, h, :], lt, T[sc][:, 2:96:3], (sc,), MS)
-        if more:
-            more()
+        step("keep")
+        more()
+        step("list")
         mm(flat(ob, 0, 32), ob, T[lt][:], (lt,), T.sel[:], ("sel",), True, True)
         cpy(T[off][:], (off,), flat(ob, 0, 32), (ob,))
 
-    def round_start(be):
-        xb, cb, st, tb = "b%d" % (2 + be), "b%d" % (4 + be), "st%d" % be, "tb%d" % be
+    def round_start(be, t):
+        xb, cb, st, tb, ci = "b%d" % (2 + be), "b%d" % (4 + be), "st%d" % be, "tb%d" % be, "ci%d" % be
         own(be, xb, 0, IB2, True, True)
-        for i in range(NT):
-            buf = ("rw%d" if i % 2 == 0 else "ge%d") % be
+        for i, (buf, c) in enumerate((("rw%d" % be, 0), ("ge%d" % be, 0), ("eq", H * be))):
             l0 = 96 * be + 32 * i
-            gather("S" if (i + be) % 2 == 0 else "V", T[buf][:], (buf,), T.inf[:, 0:W], ("inf",), T.lst[:, l0:l0 + 32], ("lst", l0, l0 + 32))
+            win = (T.pwb[:, TS * i:TS * i + W], ("pwb", TS * i, TS * i + W)) if t else (T.inf[:, 0:W], ("inf",))
+            gather("V" if (i == 1 if t else (i + be) % 2) else "S", T[buf][:, c:c + H], (buf, c, c + H), *win, T.lst[:, l0:l0 + 32], ("lst", l0, l0 + 32))
+            w = (T.wr[:, 7, :, 1], ("wr", 7, 8)) if t else (T.wr[:, 5:7, :, i], ("wr", 5, 7))
             for b in range(4):
-                mm(T[cb][:, b:64:4, i], cb, T[buf][:, b::4], (buf,), T.wr[:, 5:7, :, i], ("wr", 5, 7), i == 0 and b == 0, i == NT - 1 and b == 3)
-        ts(T[st][:, 0:96], (st, 0, 96), blk(cb, 0), (cb,), -B, None, A.add)
+                mm(T[cb][:, b:32 if t else 64:4, i], cb, T[buf][:, c + b:c + H:4], (buf, c, c + H), *w, i == 0 and b == 0, i == NT - 1 and b == 3)
+        ts(T[st][:, 0:96], (st, 0, 96), blk(cb, 0), (cb,), 0.0 if t else -B, None, A.add)
         tt(T[tb][:, 0:96], (tb,), blk(xb, 0), (xb,), T[st][:, 0:96], (st, 0, 96), A.add)
-        next_list(be, lambda: ts(T[st][:, 96:192], (st, 96, 192), blk(cb, 1), (cb,), -STAMP, None, A.add))
+
+        def stamped():
+            if t:
+                ts(T[ci][:, 0:96], (ci, 0, 96), T[ci][:, 192:288], (ci, 192, 288), int(STAMP) - 1, None, A.bitwise_and)
+                ts(T[st][:, 96:192], (st, 96, 192), T[ci][:, 0:96], (ci, 0, 96), -1.0, -STAMP, A.mult, A.add)
+            else:
+                ts(T[st][:, 96:192], (st, 96, 192), blk(cb, 1), (cb,), -STAMP, None, A.add)
+        if t:
+            stamped()
+        next_list(be, (lambda: None) if t else stamped)
 
     def find(be, q, last):
         ge, rw, off, sg, st, tb = [n % be for n in ("ge%d", "rw%d", "off%d", "sg%d", "st%d", "tb%d")]
         yb, xb, cb = ["b%d" % (n + be) for n in (0, 2, 4)]
+        step("gather")
         gather_tt(T[ge][:], (ge,), T.xs[:, 0:W], ("xs",), T[off][:], (off,), T.wf[:, H * be:H * be + H], ("wf", H * be, H * be + H), A.is_ge)
         gather("S", T[rw][:], (rw,), T.inf[:, 0:W], ("inf",), T[off][:], (off,))
+        step("own")
         own(be, yb, 0, I16, True, False)
         own(be, yb, 2, I16, False, False)
         after(be, yb, 1, I16, False)
@@ -483,32 +539,42 @@ def rank_program(g, core, T, topo):
         def rows(bank, n, src, w, wreg, start, stop, q0=0):
             for b in range(4):
                 mm(T[bank][:, 32 * q0 + b:32 * (q0 + n):4, 0:3], bank, T[src][:, b::4], (src,), w, wreg, start and b == 0, stop and b == 3)
+        step("count")
         rows(yb, 3, rw, T.wr[:, 0:3, :, :], ("wr", 0, 3), False, False)
         rows(yb, 3, ge, T.wg[:], ("wg",), False, True)
+        step("rows")
         if last:
-            rows(cb, 1, rw, T.wr[:, 6, :, :], ("wr", 6, 7), True, False, 1)
+            rows(cb, 1, rw, T.wr[:, 6, :, :], ("wr", 6, 7), True, False, 2)
         else:
-            rows(xb, 2, rw, T.wr[:, 3:5, :, :], ("wr", 3, 5), True, False)
-            rows(cb, 2, rw, T.wr[:, 5:7, :, :], ("wr", 5, 7), True, False)
+            rows(xb, 1, rw, T.wr[:, 3, :, :], ("wr", 3, 4), True, False)
+            rows(cb, 3, rw, T.wr[:, 4:7, :, :], ("wr", 4, 7), True, False)
+        step("sign")
         act(T[sg][:], (sg,), blk(yb, 0, 3), (yb,), AF.Sign)
         mv = (T[sg][:, 64:96, :], (sg,))
+        step("bounds")
         if not last:
-            mm(blk(xb, 0), xb, *IB, *mv, False, False)
-            mm(blk(xb, 1), xb, *IMB, *mv, False, False)
-            own(be, xb, 1, IB2, False, True)
+            mm(blk(xb, 0), xb, *IB, *mv, False, True)
             mm(blk(cb, 0), cb, *IMB, *mv, False, False)
-        mm(blk(cb, 1), cb, T.stl[:, q, :], ("stl", q, q + 1), *mv, False, True)
+            own(be, cb, 0, IB2, False, False)
+            mm(blk(cb, 1), cb, *IMB, *mv, False, False)
+        mm(blk(cb, 2), cb, T.stl[:, q, :], ("stl", q, q + 1), *mv, False, True)
         if last:
-            tt(T[st][:, 96:192], (st, 96, 192), blk(cb, 1), (cb,), T[st][:, 96:192], (st, 96, 192), A.min)
+            step("max")
+            tt(T[st][:, 96:192], (st, 96, 192), blk(cb, 2), (cb,), T[st][:, 96:192], (st, 96, 192), A.min)
             return
+        step("max")
         tt(T[st][:, 0:96], (st, 0, 96), blk(xb, 0), (xb,), T[st][:, 0:96], (st, 0, 96), A.max)
-        tt(T[tb][:, 0:96], (tb,), blk(xb, 1), (xb,), T[st][:, 0:96], (st, 0, 96), A.min)
-        next_list(be, lambda: tt(T[st][:], (st,), blk(cb, 0, 2), (cb,), T[st][:], (st,), A.min))
+        step("min")
+        tt(T[tb][:, 0:96], (tb,), blk(cb, 0), (cb,), T[st][:, 0:96], (st, 0, 96), A.min)
+        next_list(be, lambda: tt(T[st][:], (st,), blk(cb, 1, 3), (cb,), T[st][:], (st,), A.min))
 
-    def finds(be):
-        round_start(be)
+    def finds(be, t):
+        mark[0] = (None, be, t, -1)
+        round_start(be, t)
         for q in range(FINDS):
+            mark[0] = (None, be, t, q)
             find(be, q, q == FINDS - 1)
+        mark[0] = None
         places(be)
 
     def places(be):
@@ -519,16 +585,15 @@ def rank_program(g, core, T, topo):
         own(be, xb, 1, IB2, False, False)
         mm(blk(xb, 2), xb, *I1, T.kz[:, :, 0:3], ("kz",), False, False)
         after(be, xb, 2, IB2, True)
-        ts(T[ci][:, 192:288], (ci, 192, 288), T[st][:, 96:192], (st, 96, 192), -4.0, None, A.mult)
+        ts(T[ci][:, 192:288], (ci, 192, 288), T[st][:, 96:192], (st, 96, 192), -1.0, None, A.mult)
         ts(T[ci][:, 0:96], (ci, 0, 96), T[ci][:, 192:288], (ci, 192, 288), TS - 1, None, A.bitwise_and)
-        for i in range(NT):
-            ts(T[ci][:, 96 + i:192:3], (ci, 96, 192, i), T[ci][:, 192 + i:288:3], (ci, 192, 288), TS << (i + 1) % NT, None, A.bitwise_and)
+        ts(T[ci][:, 96:192], (ci, 96, 192), T[ci][:, 192:288], (ci, 192, 288), TS, None, A.bitwise_and)
         tt(T[tb][:, 192:288], (tb, 192, 288), blk(xb, 2), (xb,), T[ci][:, 0:96], (ci, 0, 96), A.add)
         tt(T[tb][:, 0:192], (tb, 0, 192), blk(xb, 0, 2), (xb,), T[ci][:, 0:192], (ci, 0, 192), A.add)
         scan(T[sc][:], (sc,), T.rs3[:], ("rs3",), T[tb][:], (tb,), A.max)
         tt(T[tb][:, 0:32], (tb,), T[sc][:, 2:96:3], (sc,), T[sc][:, 194:288:3], (sc,), A.not_equal)
         tt(T[sc][:, 98:192:3], (sc,), T[tb][:, 0:32], (tb,), T[sc][:, 98:192:3], (sc,), A.min)
-        masks(lambda h: T[lte][:, :, h, :], lte, T[sc][:, 2:288:3], (sc,), 2)
+        masks(lambda h: T[lte][:, :, h, :], lte, T[sc][:, 2:288:3], (sc,), MP[be])
         mm(flat(ob, 64, 96), ob, T[lte][:, 8:16, :, :], (lte,), T.sel[:], ("sel",), True, False)
         if be:
             mm(flat(ob, 96, 128), ob, T.lte0[:, 8:16, :, :], ("lte0",), T.tri[:, 32:64], ("tri",), False, False)
@@ -563,7 +628,13 @@ def rank_program(g, core, T, topo):
         scan(T.plt[:], ("plt",), T.r16[:], ("r16",), T.mk[:], ("mk",), A.add)
         cpy(T.plr[:], ("plr",), flat("b3", 0, 256), ("b3",))
         plt = (T.plt[:, 15::16], ("plt",))
+        late[0] = -SOON
         cpy(T.si[:, 0:16], ("si", 0, 16), *plt)
+        ts(T.si[:, 16:32], ("si", 16, 32), T.si[:, 0:16], ("si", 0, 16), TS - 1, None, A.bitwise_and)
+        cpy(T.sl[:], ("sl",), T.si[:, 16:32], ("si", 16, 32))
+        late[0] = 0.0
+        gather("S", T.gs[:], ("gs",), T.inf[:, 0:W], ("inf",), T.sl[:], ("sl",))
+        tt(T.pd[:], ("pd",), *plt, T.dum[:, 16:32], ("dum",), A.subtract)
         act(T.ab[:], ("ab",), flat("b3", 0, 128), ("b3",), AF.Abs, bias=co[:, 11:12], extra=[("cols", 11, 12)])
         act(flat("b2", 0, 128), ("b2",), T.ab[:], ("ab",), AF.Sign, bias=W / 2.0 + 0.5, scale=-1.0)
         for n in range(16):
@@ -571,13 +642,6 @@ def rank_program(g, core, T, topo):
             ts(T.eq[:, a:a + 256], ("eq", a, a + 256), T.plr[:], ("plr",), T.plt[:, 16 * n + 15:16 * n + 16], None, A.is_equal, extra=[("plt",)], fast=0.5)
             for s in range(2):
                 mm(flat("b7", 0, 128), "b7", T.eq[:, a + 128 * s:a + 128 * s + 128], ("eq", a, a + 256), T.bo[:], ("bo",), n == 0 and s == 0, n == 15 and s == 1)
-            if n == 0:
-                ts(T.si[:, 16:32], ("si", 16, 32), T.si[:, 0:16], ("si", 0, 16), TS - 1, None, A.bitwise_and)
-            if n == 1:
-                cpy(T.sl[:], ("sl",), T.si[:, 16:32], ("si", 16, 32))
-                gather("S", T.gs[:], ("gs",), T.inf[:, 0:W], ("inf",), T.sl[:], ("sl",))
-            if n == 2:
-                tt(T.pd[:], ("pd",), *plt, T.dum[:, 16:32], ("dum",), A.subtract)
             if n in (7, 8):
                 a = 128 * (n - 7)
                 tt(T.gz[:, a:a + 128], ("gz", a, a + 128), flat("b2", 0, 128), ("b2",), T.gs[:, a:a + 128], ("gs",), A.mult)
@@ -599,7 +663,7 @@ def rank_program(g, core, T, topo):
                 dma("Y", T.yn[:, W * i:W * i + W], None, T.pwf[2::16, TS * i:TS * i + W], ("pwf", TS * i, TS * i + W), "d_yn")
                 continue
             for k in range(2):
-                dma("Y", T.inf[2 * i + k::16, :], ("inf", 0, W, 2 * i + k), T.pwb[k::16, TS * i:TS * i + W], ("pwb",), "d_rb")
+                dma("Y", T.inf[2 * i + k::16, :], ("inf", 0, W, 2 * i + k), T.pwb[k::16, TS * i:TS * i + W], ("pwb", TS * i, TS * i + W), "d_rb")
 
     def whole_numbers():
         for k in range(2):
@@ -633,33 +697,39 @@ def rank_program(g, core, T, topo):
         cpy(T.ml[:], ("ml",), T.mi[:, 64:128], ("mi", 64, 128))
         late[0] = 0.0
         for be in range(2):
-            rw, lt, yb = "rw%d" % be, "lt%d" % be, "b%d" % be
+            rw, lt, yb = "rw%d" % be, "lt%d" % be, "b%d" % (4 + be)
             gather("S", T[rw][:], (rw,), T.inf[:, 0:W], ("inf",), T.ml[:, 32 * be:32 * be + 32], ("ml",))
             for b in range(4):
                 mm(T[yb][:, 0:8, b], yb, T[rw][:, b::4], (rw,), T.wr[:, 7, :, 0], ("wr", 7, 8), b == 0, b == 3)
             masks(lambda h: T[lt][:, :, h, :], lt, flat(yb, 0, 32), (yb,), 4)
             mm(flat(yb, 0, 32), yb, T[lt][:], (lt,), T.sel[:], ("sel",), True, True)
+            late[0] = -SOON
             cpy(T.kl[:, 32 * be:32 * be + 32], ("kl", be, be + 1), flat(yb, 0, 32), (yb,))
+            late[0] = 0.0
 
     def pull(t, last):
         xn = "x%d" % (t + 1)
         for be in range(2):
             a, b, dn = H * be, H * be + H, "b%d" % be
-            gather_tt(*room("dd", a, b), T[xn][:, 0:W], (xn,), T.kl[:, 32 * be:32 * be + 32], ("kl", be, be + 1), T.wf[:, a:b], ("wf", a, b), A.subtract)
-            ts(T[dn][:], (dn,), *room("dd", a, b), 8.0, -8.0, A.min, A.max)
-            tt(T.wf[:, a:b], ("wf", a, b), T[dn][:], (dn,), T.wf[:, a:b], ("wf", a, b), A.add)
+            ge, w = "ge%d" % be, (T.wf[:, a:b], ("wf", a, b))
+            gather("S", T[ge][:], (ge,), T[xn][:, 0:W], (xn,), T.kl[:, 32 * be:32 * be + 32], ("kl", be, be + 1))
+            for c in range(0, H, 128):
+                mm(flat(dn, c, c + 128), dn, T.idm[:], ("idm",), T.wf[:, a + c:a + c + 128], ("wf", a, b), c == 0, False)
+            mm(T[dn][:], dn, *I1, T[ge][:], (ge,), False, True)
+            ts(T[dn][:], (dn,), T[dn][:], (dn,), 8.0, -8.0, A.min, A.max)
+            tt(*w, T[dn][:], (dn,), *w, A.add)
             if last:
                 dma("S", T.yw[:, a:b], None, T.wf[:, a:b], ("wf", a, b), "d_yw%d" % be)
 
     later()
-    if not direct(rank + 1):
-        send("x2", "x1", at(rank - 1), "rx2", topo.engines(core, at(rank - 1)))
     for t in range(ROUNDS):
         last = t == ROUNDS - 1
-        finds(0)
+        finds(0, t)
         late[0] = FB
-        finds(1)
+        finds(1, t)
         late[0] = 0.0
+        if t == 0:
+            sends()
         cursors(last)
         foreign()
         swap(last)

@@ -14,31 +14,36 @@ MP = (4, 2)
 NV = 3
 XA = 2048
 FB = 0.5
-SOON = 4.0
+SOON = 1.0
+KL = 0.0
+AHEAD = (0.0, 0.0)
+ADD = (False, False)
+FILL = "YVG"
 WAKE, FLY, RATE = 0.12, 2.0, 3e5
 SB, BF, FP, I32, U16 = "sbuf", "bfloat16", "float32", "int32", "uint16"
 SCRATCH = {
     "xs": (SB, [128, W], BF), "x1": (SB, [128, W], BF), "x2": (SB, [128, W], BF), "inf": (SB, [128, W], BF),
-    "pwb": (SB, [128, PW], BF), "pwf": (SB, [128, PW], FP),
+    "pwb": (SB, [128, PW + 2 * CAP], BF), "pwf": (SB, [128, PW + 2 * CAP], FP),
     "wf": (SB, [128, K], FP), "n32": (SB, [128, Q], I32), "m32": (SB, [128, 384], I32),
     "cur32": (SB, [128, 3, 2, 32], I32), "typ32": (SB, [128, 64], I32), "lst": (SB, [128, 192], U16), "ycf": (SB, [128, 3, 2, 32], FP),
-    "ones": (SB, [128, 384], BF), "id1": (SB, [128, 8, 4, 4], BF), "idn": (SB, [128, 4, 128], BF), "stl": (SB, [128, FINDS, 128], BF),
-    "wr": (SB, [128, 8, 8, 3], BF), "wg": (SB, [128, 72], BF), "sel": (SB, [128, 32], FP), "tri": (SB, [128, 64], FP), "selr": (SB, [128, 32], BF),
-    "rs3": (SB, [128, 288], FP), "r16": (SB, [128, 256], FP), "kz": (SB, [128, 32, 4], BF),
+    "id1": (SB, [128, 8, 4, 4], BF), "idn": (SB, [128, 4, 128], BF), "stl": (SB, [128, FINDS, 128], BF),
+    "wr": (SB, [128, 9, 8, 3], BF), "wg": (SB, [128, 72], BF), "sel": (SB, [128, 32], FP), "tri": (SB, [128, 64], FP), "selr": (SB, [128, 32], BF),
+    "rs3": (SB, [128, 288], FP), "r16": (SB, [128, 128], FP), "kz": (SB, [128, 32, 4], BF),
     "pid": (SB, [128, 1], I32), "pm": (SB, [128, 8], I32), "cols": (SB, [128, 16], FP), "ttl": (SB, [128, 64, 4], BF),
-    "bo": (SB, [128, 128], BF), "bof": (SB, [128, 128], FP), "idm": (SB, [128, 128], FP), "lm": (SB, [128, 128], BF), "wn": (SB, [128, 8, 16], BF),
-    "km": (SB, [128, 256], BF), "k3": (SB, [128, 128], BF),
-    "kc": (SB, [128, 8], FP), "kch": (SB, [128, 8], FP), "dum": (SB, [128, 32], FP), "kio": (SB, [128, 128], FP),
+    "bo": (SB, [128, 128], BF), "bof": (SB, [128, 128], FP), "idm": (SB, [128, 128], FP), "lm": (SB, [128, 128], BF), "s8": (SB, [128, 8], BF),
+    "wsw": (SB, [128, 128], BF), "wkp": (SB, [128, 128], BF), "wsm": (SB, [128, 128], BF),
+    "km": (SB, [128, 128], BF), "k3": (SB, [128, 128], BF),
+    "kc": (SB, [128, 8], FP), "kch": (SB, [128, 8], FP), "dum": (SB, [128, 16], FP), "kio": (SB, [128, 128], FP),
     "pl": (SB, [128, 2, 72], FP), "wp": (SB, [128, 2, 64], BF), "rt": (SB, [128, 72], FP),
     "ck": (SB, [128, 8], FP), "ckl": (SB, [128, 8], U16), "oh": (SB, [128, 128], FP), "pr": (SB, [128, 256], FP),
     "mk": (SB, [128, 256], FP), "plt": (SB, [128, 256], FP), "plr": (SB, [128, 256], U16), "eq": (SB, [128, 256 * NEQ], BF),
-    "si": (SB, [128, 32], I32), "sl": (SB, [128, 16], U16), "ab": (SB, [128, 128], FP), "gs": (SB, [128, 256], BF), "gz": (SB, [128, 256], BF),
+    "sl": (SB, [128, 16], U16), "gs": (SB, [128, 256], BF),
     "nvb": (SB, [128, 256], BF), "nvf": (SB, [128, 256], FP), "lk": (SB, [128, 128], BF),
-    "pd": (SB, [128, 16], FP), "of": (SB, [128, 32], FP), "ofl": (SB, [128, 16], U16),
-    "mi": (SB, [128, 128], I32), "ml": (SB, [128, 64], U16), "kl": (SB, [128, 64], U16),
+    "of": (SB, [128, 16], FP), "ofl": (SB, [128, 16], U16),
+    "ml": (SB, [128, 64], U16), "kl": (SB, [128, 64], U16),
 }
 ROOMS = {"fm": ("pwb", 0), "vr": ("pwb", 1152), "wb": ("pwb", 2 * TS), "nhi": ("pwb", W + 2 * CAP), "nlo": ("pwb", TS + W),
-         "pv": ("pwf", W + 2 * CAP)}
+         "pv": ("pwf", W + 2 * CAP), "dd": ("pwf", TS + W)}
 for _b in range(2):
     for _n, _s, _d in (("ge", [128, H], BF), ("rw", [128, H], BF), ("off", [128, 32], U16), ("st", [128, 192], FP), ("sg", [128, 96, 3], BF),
                        ("tb", [128, 288], FP), ("sc", [128, 288], FP), ("lt", [128, 8, 4, 4], FP), ("lte", [128, 24, 4, 4], FP),
@@ -47,8 +52,9 @@ for _b in range(2):
 for _i in range(8):
     SCRATCH["b%d" % _i] = ("psum", [128, 128, 4], FP)
 ENG = {"V": "cv", "S": "cs", "P": "cp_", "G": "cg"}
-DMAS = ["l_n", "l_m", "l_c", "l_t", "l_x", "l_w", "d_bi", "d_fl", "d_pb", "d_pf", "d_rb", "d_yc", "d_yw0", "d_yw1", "d_yn"]
+DMAS = ["l_n", "l_m", "l_c", "l_t", "l_x", "l_w", "d_bi", "d_fl", "d_pb", "d_pf", "d_pa", "d_rb", "d_yc", "d_yw0", "d_yw1", "d_yn"]
 SEMAPHORES = sorted(ENG.values()) + DMAS + ["rx1", "rx2", "tx"]
+LOADS = DMAS[:6]
 PLANS = {}
 TURNS = {
     "V": [("gather", 0, 0), ("list", 1, 1), ("keep", 1, 1), ("gather", 1, 0), ("max", 0, 0), ("min", 0, 0), ("scan", 0, 0), ("max", 1, 0),
@@ -142,7 +148,7 @@ def rank_program(g, core, T, topo):
         mark[0] = (name,) + mark[0][1:]
 
     def plan():
-        seen, before, g0 = {}, [], None
+        seen, before, g0 = {}, [], {}
         for n, (q, _f, reads, writes, dm, cost, _l) in enumerate(calls):
             dep = {}
             for lst, wr in ((reads, False), (writes, True)):
@@ -152,10 +158,11 @@ def rank_program(g, core, T, topo):
                         same = calls[a[4]][0] == q and not dm and not calls[a[4]][4]
                         if a[0] < hi and lo < a[1] and (tag is None or a[2] is None or a[2] == tag) and (wr or a[3] or bank and not same):
                             dep[a[4]] = max(dep.get(a[4], 0.0), 0.0 if same and q == "P" else WAKE)
-            if q == "G":
-                if g0 is not None:
-                    dep.setdefault(g0, None)
-                g0 = n
+            line = "Y" if dm in LOADS else q
+            if line in "GY":
+                if line in g0:
+                    dep.setdefault(g0[line], None)
+                g0[line] = n
             before.append(dep)
             for lst, wr in ((writes, True), (reads, False)):
                 for r in lst:
@@ -183,7 +190,7 @@ def rank_program(g, core, T, topo):
         way = [0.0] * len(calls)
         for n in reversed(order):
             c = calls[n]
-            way[n] += c[5] + (FLY if c[4] and c[4] != "tx" else 0.0)
+            way[n] += c[5] + (FLY if c[4] and c[4] != "tx" else 0.0) - min(c[6], 0.0)
             for m, lat in before[n].items():
                 way[m] = max(way[m], way[n] + (lat or 0.0))
         busy = {q: [] for q in list(queues) + ["D"]}
@@ -202,7 +209,7 @@ def rank_program(g, core, T, topo):
         start, end, left = {}, {}, [len(d) for d in before]
         ready = [n for n in range(len(calls)) if not left[n]]
         while ready:
-            n = max(ready, key=lambda n: (way[n] - calls[n][6], -n))
+            n = max(ready, key=lambda n: (way[n] - max(calls[n][6], 0.0), -n))
             ready.remove(n)
             q, _f, _r, _w, dm, cost, _l = calls[n]
             t = max([0.0] + [start[m] + 1e-6 if lat is None else end[m] + lat for m, lat in before[n].items()])
@@ -301,14 +308,14 @@ def rank_program(g, core, T, topo):
     dma("Y", T.m32[:], ("m32",), T.mem[:], None, "l_m")
     dma("S", T.typ32[:], ("typ32",), T.typ[:], None, "l_t")
     dma("Y", T.cur32[:], ("cur32",), T.cur[:], None, "l_c")
-    if XA:
-        dma("Y", T.xs[:, 0:XA], ("xs", 0, XA), T.x[:, 0:XA], ("cur32",), "l_x")
+    dma("Y", T.xs[:, 0:XA], ("xs", 0, XA), T.x[:, 0:XA], None, "l_x")
 
     pm, co = T.pm, T.cols
     op("G", lambda e: e.iota(T.pid[:], [[1, 1]], 0, 1), [], [("pid",)])
     iota(*room("pv", 0, 384), [[1, 3], [0, 128]], 0, 3)
     iota(*room("vr", 0, 384), [[0, 3], [1, 128]], 0, 0)
-    fill(T.ones[:], ("ones",), 1.0)
+    for c in range(0, W, Q):
+        op("V", lambda e, c=c: e.memset(T.inf[:, c:c + Q], 1.0), [], [("inf", c, c + Q)], None, us(Q / 2))
     fill(T.wr[:], ("wr",), 0.0)
     fill(T.id1[:], ("id1",), 1.0)
     for n, v in enumerate((16.0, B, -B, B2)):
@@ -364,25 +371,20 @@ def rank_program(g, core, T, topo):
         tt(*room("nlo", a, b), T[bank][:], (bank,), *room("nhi", a, b), A.subtract)
     for n, (s, o) in enumerate(((0.5, 191.75), (0.25, 191.625))):
         act(*room("fm", 384 * n + 384, 384 * n + 768), *room("fm", 0, 384), AF.Identity, bias=o, scale=s)
-    to_inf("Y", 15, T.x[15::16, :], None)
-    for k in (13, 14):
-        to_inf("Y", k, T.ones[:], ("ones",))
     for n in range(2):
         to_inf("Y", 9 + n, *room("vr", 384 * n, 384 * n + 384))
     to_inf("Y", 6, *room("fm", 0, 384))
     for k, src in enumerate(("nhi", "nlo")):
-        for i, row in enumerate((0, 2, 4, 11)):
-            to_inf("Y", row + k, *room(src, 0, Q, 32 * i, 32 * i + 32))
+        for i in range(NT):
+            to_inf("Y", 2 * i + k, *room(src, 0, Q, 32 * i, 32 * i + 32))
         to_inf("Y", 7 + k, *room("fm", 384 * k + 384, 384 * k + 768))
 
-    late[0] = 10 * SOON
-    dma("Y", *room("wb", 0, K), T.w0[:], room("nlo", 0, Q)[1], "l_w")
-    dma("Y", T.xs[:, XA:W], ("xs", XA, W), T.x[:, XA:W], room("nlo", 0, Q)[1], "l_x")
-    late[0] = 0.0
+    dma("Y", *room("wb", 0, K), T.w0[:], None, "l_w")
+    dma("Y", T.xs[:, XA:W], ("xs", XA, W), T.x[:, XA:W], None, "l_x")
 
     iota(T.kz[:], ("kz",), [[0, 32], [TS, 4]], TS, 0)
     iota(T.kc[:], ("kc",), [[16, 8]], 0, 1)
-    iota(T.km[:], ("km",), [[0, 16], [1, 16]], 0, 0)
+    iota(T.km[:], ("km",), [[0, 8], [1, 16]], 0, 0)
     for be in range(2):
         cpy(T.lst[:, 96 * be:96 * be + 96], ("lst", 96 * be, 96 * be + 96), T.cur32[:, :, be, :], ("cur32",))
     tt(T.selr[:], ("selr",), T.id1[:, :, 0, :], ("id1",), T.id1[:, :, 1, :], ("id1",), A.add)
@@ -417,18 +419,23 @@ def rank_program(g, core, T, topo):
         op("G", lambda e: e.remote_dma(T[buf][:], T[src][:], T.sem[rx], T.sem.tx, pid, rid, sum(1 << n for n in eng)), [(src,), ("gate",)], [], "tx", 1.0)
         total["tx"] = total.get("tx", 0) + len(eng)
 
+    send("x1", "xs", at(rank - 1), "rx1", lanes(rank, 0))
+    if direct(rank):
+        send("x2", "xs", at(rank - 2), "rx2", lanes(rank, 1))
+
     def sends():
-        send("x1", "xs", at(rank - 1), "rx1", lanes(rank, 0))
-        if direct(rank):
-            send("x2", "xs", at(rank - 2), "rx2", lanes(rank, 1))
         for i in range(NT):
             o = (T.pwb[:, TS * i:TS * i + W], ("pwb", TS * i, TS * i + W))
-            if i == 1:
+            if FILL[i] == "Y":
                 dma("Y", *o, T.x[:], ("xs",), "d_fl")
-            else:
+            elif FILL[i] == "G":
                 iota(*o, [[0, W]], 0, 0)
+            else:
+                for c in range(TS * i, TS * i + W, Q // 2):
+                    op("V", lambda e, c=c: e.memset(T.pwb[:, c:c + Q // 2], 0.0), [], [("pwb", c, c + Q // 2)], None, us(Q / 4))
             for k, src in enumerate(("nhi", "nlo")):
                 dma("Y", T.pwb[k::16, TS * i:TS * i + W], ("pwb", TS * i, TS * i + W, k), room(src, 0, Q, 32 * i, 32 * i + 32)[0], ("xs",), "d_pb")
+                dma("Y", T.pwb[2 + k::16, TS * i:TS * i + W], ("pwb", TS * i, TS * i + W, 2 + k), room(src, 0, Q, 96, 128)[0], ("xs",), "d_pb")
         if not direct(rank + 1):
             send("x2", "x1", at(rank - 1), "rx2", topo.engines(core, at(rank - 1)))
     total["rx1"] = len(lanes(rank + 1, 0))
@@ -445,31 +452,32 @@ def rank_program(g, core, T, topo):
             aff(T[n][:], (n,), [[-16, 8], [0, 16]], A.is_ge, 0)
             aff(T[n][:], (n,), [[16, 8], [0, 16]], A.is_ge, 15, -1)
         aff(T.lm[:], ("lm",), [[-1, 128]], A.is_gt, 0)
-        iota(T.wn[:], ("wn",), [[0, 128]], 0, 0)
-        for r in range(6):
-            aff(T.wn[:, :, r % 2:3:2 - r % 2], ("wn",), [[-16, 8], [0, 2]], A.not_equal, -r, 1, 0.5)
-        weight(7, 8, 0, 1, 11, 0, 1.0)
-        weight(7, 8, 0, 1, 12, 0, 1.0)
-        weight(7, 8, 1, 2, 0, 0, 1.0)
-        weight(7, 8, 1, 2, 1, 0, 1.0)
+        iota(T.s8[:], ("s8",), [[0, 8]], -int(B2), 0)
+        aff(T.s8[:], ("s8",), [[-16, 8]], A.is_ge, 0)
+        aff(T.s8[:], ("s8",), [[16, 8]], A.is_ge, 15, -1)
+        aff(T.wsw[:], ("wsw",), [[16, 8], [0, 16]], A.is_ge, 1, -1, src=I1)
+        aff(T.wkp[:], ("wkp",), [[-16, 8], [0, 16]], A.is_ge, -2, 1, src=I1)
+        iota(T.wsm[:], ("wsm",), [[0, 128]], 0, 0)
+        for r in range(2):
+            aff(T.wsm[:, 0:128:16], ("wsm",), [[-16, 8]], A.not_equal, -r, 1, 1.0)
+            weight(7, 8, 0, 1, 2 + r, 0, 1.0)
+            weight(7, 9, 1, 2, r, 0, 1.0)
         iota(T.idm[:], ("idm",), [[0, 128]], -1, 0)
         aff(T.idm[:], ("idm",), [[-1, 128]], A.is_equal, 0)
-        iota(T.r16[:], ("r16",), [[0, 16], [1, 16]], 0, 0)
-        aff(T.r16[:], ("r16",), [[0, 16], [1, 16]], A.is_equal, 0, 0, 1.0)
+        iota(T.r16[:], ("r16",), [[0, 8], [1, 16]], 0, 0)
+        aff(T.r16[:], ("r16",), [[0, 8], [1, 16]], A.is_equal, 0, 0, 1.0)
         iota(T.rt[:, 64:72], ("rt", 64, 72), [[0, 8]], 0, 0)
         iota(T.pl[:, :, 64:72], ("pl", 0, 72, 2), [[0, 16]], 0, 0)
         fill(T.kz[:, :, 3], ("kz",), float(TS))
         ts(pm[:, 3:4], ("pm", 3, 4), T.pid[:], ("pid",), 15, None, A.bitwise_and)
-        ts(pm[:, 4:5], ("pm", 4, 5), pm[:, 3:4], ("pm", 3, 4), 1, None, A.arith_shift_right)
         cpy(co[:, 8:9], ("cols", 8, 9), pm[:, 3:4], ("pm", 3, 4))
         ts(co[:, 10:11], ("cols", 10, 11), pm[:, 0:1], ("pm", 0, 1), -16, None, A.mult)
-        ts(co[:, 11:12], ("cols", 11, 12), pm[:, 4:5], ("pm", 4, 5), -TS, -TS - W / 2.0, A.mult, A.add)
         ts(T.kc[:], ("kc",), T.kc[:], ("kc",), co[:, 10:11], None, A.add, extra=[("cols", 10, 11)])
         ts(T.km[:], ("km",), T.km[:], ("km",), co[:, 8:9], None, A.is_equal, extra=[("cols", 8, 9)])
         ts(T.k3[:], ("k3",), T.km[:, 0:128], ("km",), 3.0, -1.0, A.mult, A.add)
         ts(T.kch[:], ("kch",), T.kc[:], ("kc",), 0.5, None, A.add)
-        for n, v in enumerate((W, W + CAP, W + TS, W + CAP + TS)):
-            ts(T.dum[:, 8 * n:8 * n + 8], ("dum", 8 * n, 8 * n + 8), T.kc[:], ("kc",), float(v), None, A.add)
+        for n in range(2):
+            ts(T.dum[:, 8 * n:8 * n + 8], ("dum", 8 * n, 8 * n + 8), T.kc[:], ("kc",), -1.0, -float(TS + PW + CAP * n), A.mult, A.add)
 
     def masks(out, obuf, src, sreg, nscalar):
         for h in range(4):
@@ -504,26 +512,24 @@ def rank_program(g, core, T, topo):
 
     def round_start(be, t):
         xb, cb, st, tb, ci = "b%d" % (2 + be), "b%d" % (4 + be), "st%d" % be, "tb%d" % be, "ci%d" % be
-        own(be, xb, 0, IB2, True, True)
         for i, (buf, c) in enumerate((("rw%d" % be, 0), ("ge%d" % be, 0), ("eq", H * be))):
             l0 = 96 * be + 32 * i
             win = (T.pwb[:, TS * i:TS * i + W], ("pwb", TS * i, TS * i + W)) if t else (T.inf[:, 0:W], ("inf",))
             gather("V" if (i == 1 if t else (i + be) % 2) else "S", T[buf][:, c:c + H], (buf, c, c + H), *win, T.lst[:, l0:l0 + 32], ("lst", l0, l0 + 32))
-            w = (T.wr[:, 7, :, 1], ("wr", 7, 8)) if t else (T.wr[:, 5:7, :, i], ("wr", 5, 7))
+            w = (T.wr[:, 7:9, :, 1], ("wr", 7, 9)) if t else (T.wr[:, 4:7, :, i], ("wr", 4, 7))
             for b in range(4):
-                mm(T[cb][:, b:32 if t else 64:4, i], cb, T[buf][:, c + b:c + H:4], (buf, c, c + H), *w, i == 0 and b == 0, i == NT - 1 and b == 3)
-        ts(T[st][:, 0:96], (st, 0, 96), blk(cb, 0), (cb,), 0.0 if t else -B, None, A.add)
-        tt(T[tb][:, 0:96], (tb,), blk(xb, 0), (xb,), T[st][:, 0:96], (st, 0, 96), A.add)
-
-        def stamped():
-            if t:
-                ts(T[ci][:, 0:96], (ci, 0, 96), T[ci][:, 192:288], (ci, 192, 288), int(STAMP) - 1, None, A.bitwise_and)
-                ts(T[st][:, 96:192], (st, 96, 192), T[ci][:, 0:96], (ci, 0, 96), -1.0, -STAMP, A.mult, A.add)
-            else:
-                ts(T[st][:, 96:192], (st, 96, 192), blk(cb, 1), (cb,), -STAMP, None, A.add)
+                mm(T[cb][:, b:64 if t else 96:4, i], cb, T[buf][:, c + b:c + H:4], (buf, c, c + H), *w, i + b == 0, False)
+        own(be, cb, 0, IB2, False, True)
+        ts(T[tb][:, 0:96], (tb,), blk(cb, 0), (cb,), 0.0 if t else -B, None, A.add)
         if t:
-            stamped()
-        next_list(be, (lambda: None) if t else stamped)
+            ts(T[ci][:, 0:96], (ci, 0, 96), T[ci][:, 192:288], (ci, 192, 288), int(STAMP) - 1, None, A.bitwise_and)
+            ts(T[st][:, 96:192], (st, 96, 192), T[ci][:, 0:96], (ci, 0, 96), -1.0, -STAMP, A.mult, A.add)
+
+        def keep():
+            ts(T[st][:, 0:96], (st, 0, 96), blk(cb, 1), (cb,), 0.0 if t else -B, None, A.add)
+            if not t:
+                ts(T[st][:, 96:192], (st, 96, 192), blk(cb, 2), (cb,), -STAMP, None, A.add)
+        next_list(be, keep)
 
     def find(be, q, last):
         ge, rw, off, sg, st, tb = [n % be for n in ("ge%d", "rw%d", "off%d", "sg%d", "st%d", "tb%d")]
@@ -594,9 +600,9 @@ def rank_program(g, core, T, topo):
         tt(T[tb][:, 0:32], (tb,), T[sc][:, 2:96:3], (sc,), T[sc][:, 194:288:3], (sc,), A.not_equal)
         tt(T[sc][:, 98:192:3], (sc,), T[tb][:, 0:32], (tb,), T[sc][:, 98:192:3], (sc,), A.min)
         masks(lambda h: T[lte][:, :, h, :], lte, T[sc][:, 2:288:3], (sc,), MP[be])
-        mm(flat(ob, 64, 96), ob, T[lte][:, 8:16, :, :], (lte,), T.sel[:], ("sel",), True, False)
         if be:
-            mm(flat(ob, 96, 128), ob, T.lte0[:, 8:16, :, :], ("lte0",), T.tri[:, 32:64], ("tri",), False, False)
+            mm(flat(ob, 96, 128), ob, T.lte0[:, 8:16, :, :], ("lte0",), T.tri[:, 32:64], ("tri",), True, False)
+        mm(flat(ob, 64, 96), ob, T[lte][:, 8:16, :, :], (lte,), T.sel[:], ("sel",), be == 0, False)
         mm(flat(ob, 96, 128), ob, T[lte][:, 8:16, :, :], (lte,), T.tri[:, 0:32], ("tri",), False, True)
         cpy(T.wp[:, :, 32 * be:32 * be + 32], ("wp", 0, 64, be), flat(ob, 64, 128), (ob,))
         for s in range(2):
@@ -623,44 +629,42 @@ def rank_program(g, core, T, topo):
         gather_tt(T.oh[:], ("oh",), T.rt[:, 0:72], ("rt",), T.ckl[:], ("ckl",), T.kio[:], ("kio",), A.is_equal)
         for s in range(2):
             gather_tt(T.pr[:, 128 * s:128 * s + 128], ("pr", s, s + 1), T.pl[:, s, :], ("pl",), T.ckl[:], ("ckl",), T.oh[:], ("oh",), A.mult)
-            mm(flat("b3", 128 * s, 128 * s + 128), "b3", T.bof[:], ("bof",), T.pr[:, 128 * s:128 * s + 128], ("pr", s, s + 1), s == 0, s == 1)
-        tt(T.mk[:], ("mk",), flat("b3", 0, 256), ("b3",), T.km[:], ("km",), A.mult)
-        scan(T.plt[:], ("plt",), T.r16[:], ("r16",), T.mk[:], ("mk",), A.add)
-        cpy(T.plr[:], ("plr",), flat("b3", 0, 256), ("b3",))
+            mm(flat("b%d" % (3 - s), 0, 128), "b%d" % (3 - s), T.bof[:], ("bof",), T.pr[:, 128 * s:128 * s + 128], ("pr", s, s + 1), True, True)
+        for s in range(2):
+            a, b, bank = 128 * s, 128 * s + 128, "b%d" % (3 - s)
+            tt(T.mk[:, a:b], ("mk", a, b), flat(bank, 0, 128), (bank,), T.km[:], ("km",), A.mult)
+            scan(T.plt[:, a:b], ("plt", a, b), T.r16[:], ("r16",), T.mk[:, a:b], ("mk", a, b), A.add)
+            cpy(T.plr[:, a:b], ("plr", a, b), flat(bank, 0, 128), (bank,))
         plt = (T.plt[:, 15::16], ("plt",))
         late[0] = -SOON
-        cpy(T.si[:, 0:16], ("si", 0, 16), *plt)
-        ts(T.si[:, 16:32], ("si", 16, 32), T.si[:, 0:16], ("si", 0, 16), TS - 1, None, A.bitwise_and)
-        cpy(T.sl[:], ("sl",), T.si[:, 16:32], ("si", 16, 32))
+        ts(T.sl[:], ("sl",), *plt, -TS, None, A.add)
         late[0] = 0.0
-        gather("S", T.gs[:], ("gs",), T.inf[:, 0:W], ("inf",), T.sl[:], ("sl",))
-        tt(T.pd[:], ("pd",), *plt, T.dum[:, 16:32], ("dum",), A.subtract)
-        act(T.ab[:], ("ab",), flat("b3", 0, 128), ("b3",), AF.Abs, bias=co[:, 11:12], extra=[("cols", 11, 12)])
-        act(flat("b2", 0, 128), ("b2",), T.ab[:], ("ab",), AF.Sign, bias=W / 2.0 + 0.5, scale=-1.0)
+        gather("S", T.gs[:], ("gs",), T.pwb[:, 0:PW], ("pwb",), T.sl[:], ("sl",))
+        for s in range(2):
+            a, b = 128 * s, 128 - 128 * s
+            wn = "wsm" if last else "wsw"
+            mm(flat("b2", a, a + 128), "b2", T[wn][:], (wn,), T.gs[:, b:b + 128], ("gs",), s == 0, last and s == 1)
+            if not last:
+                mm(flat("b2", a, a + 128), "b2", T.wkp[:], ("wkp",), T.gs[:, a:a + 128], ("gs",), False, s == 1)
+        nv = "nvf" if last else "nvb"
+        act(T[nv][:], (nv,), flat("b2", 0, 256), ("b2",), AF.Copy)
+        mm(flat("b6", 0, 16), "b6", T.idm[:], ("idm",), T.dum[:], ("dum",), True, False)
         for n in range(16):
             a = 256 * (n % NEQ)
-            ts(T.eq[:, a:a + 256], ("eq", a, a + 256), T.plr[:], ("plr",), T.plt[:, 16 * n + 15:16 * n + 16], None, A.is_equal, extra=[("plt",)], fast=0.5)
+            ts(T.eq[:, a:a + 256], ("eq", a, a + 256), T.plr[:], ("plr",), T.plt[:, 16 * n + 15:16 * n + 16], None, A.is_equal, extra=[("plt", 16 * n, 16 * n + 16)], fast=0.5)
             for s in range(2):
                 mm(flat("b7", 0, 128), "b7", T.eq[:, a + 128 * s:a + 128 * s + 128], ("eq", a, a + 256), T.bo[:], ("bo",), n == 0 and s == 0, n == 15 and s == 1)
-            if n in (7, 8):
-                a = 128 * (n - 7)
-                tt(T.gz[:, a:a + 128], ("gz", a, a + 128), flat("b2", 0, 128), ("b2",), T.gs[:, a:a + 128], ("gs",), A.mult)
-                for k, src in enumerate(("gs", "gz")):
-                    mm(flat("b3", 128 - a, 256 - a), "b3", T.wn[:], ("wn",), T[src][:, a:a + 128], (src, a, a + 128), n == 7 and k == 0, n == 8 and k == 1)
-        nv = "nvf" if last else "nvb"
-        act(T[nv][:], (nv,), flat("b3", 0, 256), ("b3",), AF.Copy)
         tt(T.lk[:], ("lk",), flat("b7", 0, 128), ("b7",), T.k3[:], ("k3",), A.is_equal)
         for s in range(2):
-            mm(flat("b6", 8 * s, 8 * s + 8), "b6", T.lk[:], ("lk",), T.bo[:, 0:128:16], ("bo",), s == 0, s == 1)
-        tt(T.of[:, 0:16], ("of", 0, 16), flat("b6", 0, 16), ("b6",), T.pd[:], ("pd",), A.mult)
-        tt(T.of[:, 16:32], ("of", 16, 32), T.of[:, 0:16], ("of", 0, 16), T.dum[:, 0:16], ("dum",), A.add)
-        cpy(T.ofl[:], ("ofl",), T.of[:, 16:32], ("of", 16, 32))
+            mm(flat("b6", 8 * s, 8 * s + 8), "b6", T.lk[:], ("lk",), T.s8[:], ("s8",), False, s == 1)
+        tt(T.of[:], ("of",), flat("b6", 0, 16), ("b6",), *plt, A.max)
+        ts(T.ofl[:], ("ofl",), T.of[:], ("of",), -TS, None, A.add)
         win, src = ("pwf", "nvf") if last else ("pwb", "nvb")
-        out = T[win][:, 0:PW].indirect(T.ofl[:])
+        out = T[win][:].indirect(T.ofl[:])
         op("V", lambda e: e.tensor_copy(out, T[src][:]), [(src,), ("ofl",)], [(win,)], None, 1.0)
         for i in range(NT):
             if last:
-                dma("Y", T.yn[:, W * i:W * i + W], None, T.pwf[2::16, TS * i:TS * i + W], ("pwf", TS * i, TS * i + W), "d_yn")
+                dma("Y", T.yn[:, W * i:W * i + W], None, T.pwf[0::16, TS * i:TS * i + W], ("pwf", TS * i, TS * i + W), "d_yn")
                 continue
             for k in range(2):
                 dma("Y", T.inf[2 * i + k::16, :], ("inf", 0, W, 2 * i + k), T.pwb[k::16, TS * i:TS * i + W], ("pwb", TS * i, TS * i + W), "d_rb")
@@ -668,11 +672,11 @@ def rank_program(g, core, T, topo):
     def whole_numbers():
         for k in range(2):
             for i in range(NT):
-                o, a = T.pwf[2::16, TS * i:TS * i + W], T.pwb[k::16, TS * i:TS * i + W]
+                o, a = T.pwf[0::16, TS * i:TS * i + W], T.pwb[k::16, TS * i:TS * i + W]
                 if k == 0:
                     op("G", lambda e, o=o, a=a: e.dma_start(o, a), [("pwb",), ("inf",)], [("pwf", TS * i, TS * i + W)], "d_pf")
                 else:
-                    op("G", lambda e, o=o, a=a: e.dma_start(o, a, accum_op=A.add, max_dma_last_dim=4096), [("pwb",)], [("pwf", TS * i, TS * i + W)], "d_pf")
+                    op("G", lambda e, o=o, a=a: e.dma_start(o, a, accum_op=A.add, max_dma_last_dim=4096), [("pwb",)], [("pwf", TS * i, TS * i + W)], "d_pa")
 
     def cursors(last):
         for be in range(2):
@@ -691,21 +695,17 @@ def rank_program(g, core, T, topo):
             dma("S", T.yc[:], None, T.ycf[:], ("ycf",), "d_yc")
 
     def foreign():
-        late[0] = -SOON
-        cpy(T.mi[:, 0:64], ("mi", 0, 64), T.pl[:, 0, 0:64], ("pl",))
-        ts(T.mi[:, 64:128], ("mi", 64, 128), T.mi[:, 0:64], ("mi", 0, 64), TS - 1, None, A.bitwise_and)
-        cpy(T.ml[:], ("ml",), T.mi[:, 64:128], ("mi", 64, 128))
-        late[0] = 0.0
         for be in range(2):
-            rw, lt, yb = "rw%d" % be, "lt%d" % be, "b%d" % (4 + be)
-            gather("S", T[rw][:], (rw,), T.inf[:, 0:W], ("inf",), T.ml[:, 32 * be:32 * be + 32], ("ml",))
+            rw, lt, yb, ob = "rw%d" % be, "lt%d" % be, "b%d" % (4 + be), "b%d" % (6 + be)
+            ts(T.ml[:, 32 * be:32 * be + 32], ("ml", be, be + 1), T.pl[:, 0, 32 * be:32 * be + 32], ("pl", 0, 72, be), -TS, None, A.add)
+            gather("S", T[rw][:], (rw,), T.pwb[:, 0:PW], ("pwb",), T.ml[:, 32 * be:32 * be + 32], ("ml", be, be + 1))
             for b in range(4):
                 mm(T[yb][:, 0:8, b], yb, T[rw][:, b::4], (rw,), T.wr[:, 7, :, 0], ("wr", 7, 8), b == 0, b == 3)
             masks(lambda h: T[lt][:, :, h, :], lt, flat(yb, 0, 32), (yb,), 4)
             mm(flat(yb, 0, 32), yb, T[lt][:], (lt,), T.sel[:], ("sel",), True, True)
-            late[0] = -SOON
+            late[0] -= KL
             cpy(T.kl[:, 32 * be:32 * be + 32], ("kl", be, be + 1), flat(yb, 0, 32), (yb,))
-            late[0] = 0.0
+            late[0] += KL
 
     def pull(t, last):
         xn = "x%d" % (t + 1)
@@ -716,8 +716,17 @@ def rank_program(g, core, T, topo):
             for c in range(0, H, 128):
                 mm(flat(dn, c, c + 128), dn, T.idm[:], ("idm",), T.wf[:, a + c:a + c + 128], ("wf", a, b), c == 0, False)
             mm(T[dn][:], dn, *I1, T[ge][:], (ge,), False, True)
-            ts(T[dn][:], (dn,), T[dn][:], (dn,), 8.0, -8.0, A.min, A.max)
-            tt(*w, T[dn][:], (dn,), *w, A.add)
+            if ADD[t]:
+                for c in range(0, H, 256):
+                    ts(*room("dd", a + c, a + c + 256), flat(dn, c, c + 256), (dn,), 8.0, -8.0, A.min, A.max)
+                for k in range(2):
+                    for c in range(0, H, 128):
+                        src = room("dd", a + c, a + c + 128) if k else (T.wf[:, a + c:a + c + 128], ("wf", a, b))
+                        mm(flat(dn, c, c + 128), dn, T.idm[:], ("idm",), *src, c + k == 0, k and c + 128 == H)
+                act(*w, T[dn][:], (dn,), AF.Copy, scale=-1.0)
+            else:
+                ts(T[dn][:], (dn,), T[dn][:], (dn,), 8.0, -8.0, A.min, A.max)
+                tt(*w, T[dn][:], (dn,), *w, A.add)
             if last:
                 dma("S", T.yw[:, a:b], None, T.wf[:, a:b], ("wf", a, b), "d_yw%d" % be)
 
@@ -730,10 +739,14 @@ def rank_program(g, core, T, topo):
         late[0] = 0.0
         if t == 0:
             sends()
-        cursors(last)
+        late[0] = -AHEAD[t]
         foreign()
+        late[0] = 0.0
+        cursors(last)
         swap(last)
+        late[0] = -AHEAD[t]
         pull(t, last)
+        late[0] = 0.0
         if not last:
             whole_numbers()
     if len(calls) not in PLANS:

@@ -10,23 +10,25 @@ PW = 2 * TS + W
 B, B2, STAMP = 16384.0, 32768.0, 16384.0
 NEQ = 4
 MS = 3
-MP = (4, 2)
-NV = 3
+MP = (3, 2)
+NV = 4
 XA = 2048
 FB = 0.5
 SOON = 1.0
-KL = 0.0
-AHEAD = (0.0, 0.0)
-ADD = (False, False)
-FILL = "YVG"
-WAKE, FLY, RATE = 0.12, 2.0, 3e5
+CUT = 352
+CP = "SVSS"
+RS = ("SVSVSV", "SVSSVS")
+FILL = "YYG"
+PIECE, EARLY, BYS = 512, 30.0, 4096
+TRIES, SHAKE = 1400, 0.4
+WAKE, FLY, RATE = 0.13, 2.0, 6e5
 SB, BF, FP, I32, U16 = "sbuf", "bfloat16", "float32", "int32", "uint16"
 SCRATCH = {
     "xs": (SB, [128, W], BF), "x1": (SB, [128, W], BF), "x2": (SB, [128, W], BF), "inf": (SB, [128, W], BF),
     "pwb": (SB, [128, PW + 2 * CAP], BF), "pwf": (SB, [128, PW + 2 * CAP], FP),
     "wf": (SB, [128, K], FP), "n32": (SB, [128, Q], I32), "m32": (SB, [128, 384], I32),
     "cur32": (SB, [128, 3, 2, 32], I32), "typ32": (SB, [128, 64], I32), "lst": (SB, [128, 192], U16), "ycf": (SB, [128, 3, 2, 32], FP),
-    "id1": (SB, [128, 8, 4, 4], BF), "idn": (SB, [128, 4, 128], BF), "stl": (SB, [128, FINDS, 128], BF),
+    "id1": (SB, [128, 8, 4, 4], BF), "idn": (SB, [128, 5, 128], BF), "stl": (SB, [128, FINDS, 128], BF),
     "wr": (SB, [128, 9, 8, 3], BF), "wg": (SB, [128, 72], BF), "sel": (SB, [128, 32], FP), "tri": (SB, [128, 64], FP), "selr": (SB, [128, 32], BF),
     "rs3": (SB, [128, 288], FP), "r16": (SB, [128, 128], FP), "kz": (SB, [128, 32, 4], BF),
     "pid": (SB, [128, 1], I32), "pm": (SB, [128, 8], I32), "cols": (SB, [128, 16], FP), "ttl": (SB, [128, 64, 4], BF),
@@ -43,7 +45,7 @@ SCRATCH = {
     "ml": (SB, [128, 64], U16), "kl": (SB, [128, 64], U16),
 }
 ROOMS = {"fm": ("pwb", 0), "vr": ("pwb", 1152), "wb": ("pwb", 2 * TS), "nhi": ("pwb", W + 2 * CAP), "nlo": ("pwb", TS + W),
-         "pv": ("pwf", W + 2 * CAP), "dd": ("pwf", TS + W)}
+         "pv": ("pwf", W + 2 * CAP)}
 for _b in range(2):
     for _n, _s, _d in (("ge", [128, H], BF), ("rw", [128, H], BF), ("off", [128, 32], U16), ("st", [128, 192], FP), ("sg", [128, 96, 3], BF),
                        ("tb", [128, 288], FP), ("sc", [128, 288], FP), ("lt", [128, 8, 4, 4], FP), ("lte", [128, 24, 4, 4], FP),
@@ -52,24 +54,58 @@ for _b in range(2):
 for _i in range(8):
     SCRATCH["b%d" % _i] = ("psum", [128, 128, 4], FP)
 ENG = {"V": "cv", "S": "cs", "P": "cp_", "G": "cg"}
-DMAS = ["l_n", "l_m", "l_c", "l_t", "l_x", "l_w", "d_bi", "d_fl", "d_pb", "d_pf", "d_pa", "d_rb", "d_yc", "d_yw0", "d_yw1", "d_yn"]
+DMAS = ["l_n", "l_m", "l_c", "l_t", "l_a", "l_x", "l_w", "d_bi", "d_fl", "d_pb", "d_pf", "d_pa", "d_rb", "d_yc", "d_yw0", "d_yw1", "d_yn"]
 SEMAPHORES = sorted(ENG.values()) + DMAS + ["rx1", "rx2", "tx"]
-LOADS = DMAS[:6]
+LOADS = DMAS[:7]
 PLANS = {}
 TURNS = {
-    "V": [("gather", 0, 0), ("list", 1, 1), ("keep", 1, 1), ("gather", 1, 0), ("max", 0, 0), ("min", 0, 0), ("scan", 0, 0), ("max", 1, 0),
-          ("mask", 0, 0), ("min", 1, 0), ("keep", 0, 0), ("scan", 1, 0), ("list", 0, 0), ("mask", 1, 0)],
+    "V": [("gather", 0, 0), ("list", 1, 1), ("rest", 0, 0), ("gather", 1, 0), ("keep", 1, 1), ("max", 0, 0), ("min", 0, 0), ("scan", 0, 0), ("max", 1, 0),
+          ("mask", 0, 0), ("min", 1, 0), ("scan", 1, 0), ("keep", 0, 0), ("list", 0, 0), ("mask", 1, 0)],
     "S": [("gather", 0, 0), ("gather", 1, 0), ("sign", 0, 0), ("sign", 1, 0), ("mask", 0, 0), ("mask", 1, 0)],
-    "P": [("list", 1, 1), ("own", 0, 0), ("count", 0, 0), ("rows", 0, 0), ("count", 1, 0), ("bounds", 0, 0), ("rows", 1, 0), ("bounds", 1, 0),
-          ("own", 1, -1), ("list", 0, 0)],
+    "P": [("own", 0, 0), ("list", 1, 1), ("count", 0, 0), ("hits", 0, 0), ("rows", 0, 0), ("more", 0, 0), ("count", 1, 0), ("low", 0, 0),
+          ("hits", 1, 0), ("bounds", 0, 0), ("rows", 1, 0), ("low", 1, 0), ("stamp", 0, 0), ("bounds", 1, 0), ("more", 1, 0), ("stamp", 1, 0),
+          ("list", 0, 0), ("own", 1, -1)],
 }
+
+
+def routes(cores, topo):
+    out = []
+    for r, c in enumerate(cores):
+        first, second = cores[r - 1], cores[r - 2]
+        far = topo.engines(c, second)
+        hands = [h for h in topo.cores_of(c) if h not in cores and topo.may_write(h, first) and topo.may_write(h, second)]
+        near = [n for n in topo.engines(c, hands[0]) if n not in far] or far
+        once = topo.chip(first) == topo.chip(second) != topo.chip(c)
+        buf = "x1" if once else "x2"
+        for h, a, eng in ((hands[0], 0, far), (hands[-1], W // 2, near)):
+            out.append((c, h, "xs", buf, a, a + W // 2, eng))
+            out.append((h, first, buf, "x1", a, a + W // 2, near if topo.chip(first) == topo.chip(c) else far))
+            if not once:
+                out.append((h, second, buf, "x2", a, a + W // 2, far))
+        if once:
+            out.append((first, second, "x1", "x2", 0, W, topo.engines(first, second)))
+    return out
 
 
 def rank_program(g, core, T, topo):
     rank = T.rank_of(core)
+    mine = [w for w in routes(list(T.cores), topo) if w[0] == core]
+    counts = {"tx": sum(len(w[6]) for w in mine)}
+    for w in routes(list(T.cores), topo):
+        if w[1] == core:
+            counts["r" + w[3]] = counts.get("r" + w[3], 0) + len(w[6])
+
+    def write(w):
+        rid, pid, _s = topo.addr(w[1])
+        g.remote_dma(T[w[3]][:, w[4]:w[5]], T[w[2]][:, w[4]:w[5]], T.sem["r" + w[3]], T.sem.tx, pid, rid, sum(1 << n for n in w[6]))
+
     if rank is None:
+        for w in sorted(mine, key=lambda w: (w[3], w[2])):
+            g.wait_ge(T.sem["r" + w[2]], counts["r" + w[2]])
+            write(w)
+        if mine:
+            g.wait_ge(T.sem.tx, counts["tx"])
         return
-    N = len(T.cores)
     queues = {"V": g.vector, "S": g.scalar, "P": g.tensor, "G": g, "Y": g.sync}
     clock = {q: {} for q in queues}
     total = {}
@@ -187,12 +223,35 @@ def rank_program(g, core, T, topo):
                 if not left[m]:
                     order.append(m)
         assert len(order) == len(calls)
-        way = [0.0] * len(calls)
+        way, beside = [0.0] * len(calls), [0.0] * len(calls)
         for n in reversed(order):
             c = calls[n]
             way[n] += c[5] + (FLY if c[4] and c[4] != "tx" else 0.0) - min(c[6], 0.0)
+            way[n] = max(way[n], beside[n])
             for m, lat in before[n].items():
-                way[m] = max(way[m], way[n] + (lat or 0.0))
+                if lat is None and calls[m][4] and calls[m][4] != "tx":
+                    beside[m] = max(beside[m], way[n] + 0.05)
+                else:
+                    way[m] = max(way[m], way[n] + (lat or 0.0))
+        rank0 = [way[n] - max(c[6], 0.0) for n, c in enumerate(calls)]
+        best = lay(rank0, before, after)
+        free = [n for (q, m), ns in steps.items() if m is None or m[3] in (-1, FINDS - 1) for n in ns]
+        seed = 1
+        for _try in range(TRIES):
+            seed = (seed * 1103515245 + 12345) % (1 << 31)
+            t0 = best[0] * seed / (1 << 31)
+            new = list(rank0)
+            for n in free:
+                if abs(best[2][n] - t0) < 3.0:
+                    seed = (seed * 1103515245 + 12345) % (1 << 31)
+                    new[n] += SHAKE * (seed / (1 << 30) - 1.0)
+            if new != rank0:
+                now = lay(new, before, after)
+                if now[0] <= best[0]:
+                    best, rank0 = now, new
+        return best[1]
+
+    def lay(rank0, before, after):
         busy = {q: [] for q in list(queues) + ["D"]}
 
         def place(q, t, c):
@@ -209,7 +268,7 @@ def rank_program(g, core, T, topo):
         start, end, left = {}, {}, [len(d) for d in before]
         ready = [n for n in range(len(calls)) if not left[n]]
         while ready:
-            n = max(ready, key=lambda n: (way[n] - max(calls[n][6], 0.0), -n))
+            n = max(ready, key=lambda n: rank0[n])
             ready.remove(n)
             q, _f, _r, _w, dm, cost, _l = calls[n]
             t = max([0.0] + [start[m] + 1e-6 if lat is None else end[m] + lat for m, lat in before[n].items()])
@@ -223,10 +282,22 @@ def rank_program(g, core, T, topo):
                 left[m] -= 1
                 if not left[m]:
                     ready.append(m)
-        return sorted(range(len(calls)), key=lambda n: (start[n], n))
+        order = sorted(range(len(calls)), key=lambda n: (start[n], n))
+        now = dict.fromkeys(busy, 0.0)
+        for n in order:
+            q, _f, _r, _w, dm, cost, _l = calls[n]
+            t = max([now[q]] + [start[m] if lat is None else end[m] + lat for m, lat in before[n].items()])
+            start[n] = t
+            if dm and dm != "tx":
+                now[q] = t + 0.05
+                now["D"] = max(now["D"], t + 0.7 * FLY) + cost
+                end[n] = now["D"] + 0.3 * FLY
+            else:
+                end[n] = now[q] = t + cost
+        return max(end.values()), order, start
 
     I1 = (T.id1[:], ("id1",))
-    I16, IB, IMB, IB2 = [(T.idn[:, n, :], ("idn",)) for n in range(4)]
+    I16, IB, IMB, IB2, IRD = [(T.idn[:, n, :], ("idn",)) for n in range(5)]
 
     def cols(ap):
         n = 1
@@ -272,13 +343,19 @@ def rank_program(g, core, T, topo):
         else:
             op("S", lambda e: e.activation(out, a, f, bias=bias, scale=scale, accum_out=accum), [ra] + list(extra), [o, ao], None, c)
 
+    def copy(q, out, o, a, ra):
+        if q == "V":
+            cpy(out, o, a, ra)
+        else:
+            act(out, o, a, ra, AF.Copy)
+
     def mm(out, bank, l, rl, r, rr, start, stop):
         four = 4 if SCRATCH[rl[0]][2] == FP else 1
         op("P", lambda e: e.matmul(out, l, r, start, stop), [rl, rr], [(bank,)], None, max(64, cols(r)) * 0.0005 * four)
 
     def dma(q, out, o, a, ra, sem, also=()):
         size = out.shape[0] * cols(out) * (2 if o and SCRATCH[o[0]][2] == BF else 4)
-        op(q, lambda e: e.dma_start(out, a), [ra] if ra else [], ([o] if o else []) + list(also), sem, size / RATE)
+        op(q, lambda e: e.dma_start(out, a), [ra] if ra else [], ([o] if o else []) + list(also), sem, size / RATE + 0.002 * max(out.shape[0], a.shape[0]))
 
     def fill(ap, o, v):
         op("V", lambda e: e.memset(ap, v), [], [o])
@@ -308,7 +385,7 @@ def rank_program(g, core, T, topo):
     dma("Y", T.m32[:], ("m32",), T.mem[:], None, "l_m")
     dma("S", T.typ32[:], ("typ32",), T.typ[:], None, "l_t")
     dma("Y", T.cur32[:], ("cur32",), T.cur[:], None, "l_c")
-    dma("Y", T.xs[:, 0:XA], ("xs", 0, XA), T.x[:, 0:XA], None, "l_x")
+    dma("Y", T.xs[:, 0:XA], ("xs", 0, XA), T.x[:, 0:XA], None, "l_a")
 
     pm, co = T.pm, T.cols
     op("G", lambda e: e.iota(T.pid[:], [[1, 1]], 0, 1), [], [("pid",)])
@@ -318,7 +395,7 @@ def rank_program(g, core, T, topo):
         op("V", lambda e, c=c: e.memset(T.inf[:, c:c + Q], 1.0), [], [("inf", c, c + Q)], None, us(Q / 2))
     fill(T.wr[:], ("wr",), 0.0)
     fill(T.id1[:], ("id1",), 1.0)
-    for n, v in enumerate((16.0, B, -B, B2)):
+    for n, v in enumerate((16.0, B, -B, B2, -STAMP * FINDS)):
         fill(T.idn[:, n, :], ("idn", n, n + 1), v)
     fill(T.wg[:, 0:24], ("wg", 0, 24), -1.0)
     fill(T.wg[:, 24:72], ("wg", 24, 72), 1.0)
@@ -344,7 +421,7 @@ def rank_program(g, core, T, topo):
     weight(4, 6, 0, 3, 13, 0, B)
     for i, row, v in ((0, 7, -1), (0, 8, 2), (0, 14, -192), (1, 8, -1), (1, 14, 192), (2, 6, -1), (2, 7, 2), (2, 14, -384)):
         weight(6, 7, i, i + 1, row, 0, float(TS * v))
-    aff(T.idn[:], ("idn",), [[0, 4], [-1, 128]], A.is_equal, 0)
+    aff(T.idn[:], ("idn",), [[0, 5], [-1, 128]], A.is_equal, 0)
     aff(T.sel[:], ("sel",), [[-4, 32]], A.is_ge, 0)
     weight(3, 4, 0, 3, 13, 0, -B)
     aff(T.sel[:], ("sel",), [[4, 32]], A.is_ge, 3, -1)
@@ -403,27 +480,25 @@ def rank_program(g, core, T, topo):
     for t in range(FINDS):
         act(T.stl[:, t, :], ("stl", t, t + 1), *I1, AF.Copy, scale=-STAMP * (t + 2))
 
-    def at(r):
-        return T.cores[r % N]
+    def send(src, gate="gate"):
+        for w in mine:
+            if w[2] == src:
+                op("G", lambda e, w=w: write(w), [(src,), (gate,)], [], "tx", 1.0)
 
-    def direct(r):
-        return not (topo.chip(at(r - 1)) == topo.chip(at(r - 2)) != topo.chip(at(r)))
+    iota(T.tri[:], ("tri",), [[0, 64]], 1, 0)
+    iota(T.bo[:], ("bo",), [[0, 128]], 1, 0)
+    aff(T.tri[:], ("tri",), [[4, 64]], A.is_ge, 3, -1)
+    aff(T.bo[:], ("bo",), [[-16, 8], [0, 16]], A.is_ge, 0)
+    iota(T.kio[:], ("kio",), [[1, 128]], 1, 0)
+    aff(T.bo[:], ("bo",), [[16, 8], [0, 16]], A.is_ge, 15, -1)
+    iota(T.idm[:], ("idm",), [[0, 128]], -1, 0)
+    iota(T.lm[:], ("lm",), [[0, 128]], -1, 0)
+    aff(T.idm[:], ("idm",), [[-1, 128]], A.is_equal, 0)
+    aff(T.lm[:], ("lm",), [[-16, 8], [0, 16]], A.is_ge, 0)
+    aff(T.bof[:], ("bof",), [[0, 128]], A.is_ge, 0, src=(T.bo[:], ("bo",)))
+    aff(T.lm[:], ("lm",), [[16, 8], [0, 16]], A.is_ge, 15, -1)
 
-    def lanes(r, t):
-        e = topo.engines(at(r), at(r - 1 - t))
-        rest = [n for n in e if n not in topo.engines(at(r), at(r - 2))]
-        return rest if t == 0 and direct(r) and rest else e
-
-    def send(buf, src, dst, rx, eng):
-        rid, pid, _s = topo.addr(dst)
-        op("G", lambda e: e.remote_dma(T[buf][:], T[src][:], T.sem[rx], T.sem.tx, pid, rid, sum(1 << n for n in eng)), [(src,), ("gate",)], [], "tx", 1.0)
-        total["tx"] = total.get("tx", 0) + len(eng)
-
-    send("x1", "xs", at(rank - 1), "rx1", lanes(rank, 0))
-    if direct(rank):
-        send("x2", "xs", at(rank - 2), "rx2", lanes(rank, 1))
-
-    def sends():
+    def window():
         for i in range(NT):
             o = (T.pwb[:, TS * i:TS * i + W], ("pwb", TS * i, TS * i + W))
             if FILL[i] == "Y":
@@ -431,29 +506,28 @@ def rank_program(g, core, T, topo):
             elif FILL[i] == "G":
                 iota(*o, [[0, W]], 0, 0)
             else:
-                for c in range(TS * i, TS * i + W, Q // 2):
-                    op("V", lambda e, c=c: e.memset(T.pwb[:, c:c + Q // 2], 0.0), [], [("pwb", c, c + Q // 2)], None, us(Q / 4))
+                late[0] = -EARLY
+                for c in range(TS * i, TS * i + W, PIECE):
+                    if c < TS * i + BYS:
+                        act(T.pwb[:, c:c + PIECE], ("pwb", c, c + PIECE), T.xs[:, 0:PIECE], ("xs", 0, PIECE), AF.Copy)
+                    else:
+                        op("V", lambda e, c=c: e.memset(T.pwb[:, c:c + PIECE], 0.0), [], [("pwb", c, c + PIECE)], None, us(PIECE / 2))
+                late[0] = 0.0
+        for i in range(NT):
             for k, src in enumerate(("nhi", "nlo")):
                 dma("Y", T.pwb[k::16, TS * i:TS * i + W], ("pwb", TS * i, TS * i + W, k), room(src, 0, Q, 32 * i, 32 * i + 32)[0], ("xs",), "d_pb")
                 dma("Y", T.pwb[2 + k::16, TS * i:TS * i + W], ("pwb", TS * i, TS * i + W, 2 + k), room(src, 0, Q, 96, 128)[0], ("xs",), "d_pb")
-        if not direct(rank + 1):
-            send("x2", "x1", at(rank - 1), "rx2", topo.engines(core, at(rank - 1)))
-    total["rx1"] = len(lanes(rank + 1, 0))
-    total["rx2"] = len(lanes(rank + 2, 1) if direct(rank + 2) else topo.engines(at(rank + 1), core))
-    for n in ("1", "2"):
-        acc["x" + n] = [(0, 1 << 20, None, "R", "rx" + n, total["rx" + n], True)]
+
+    total.update(counts)
+    for n in ("x1", "x2"):
+        acc[n] = [(0, 1 << 20, None, "R", "r" + n, total["r" + n], True)]
 
     def later():
-        iota(T.kio[:], ("kio",), [[1, 128]], 1, 0)
-        iota(T.tri[:], ("tri",), [[0, 64]], 1, 0)
-        aff(T.tri[:], ("tri",), [[4, 64]], A.is_ge, 3, -1)
-        for n, v in (("bo", 1), ("bof", 1), ("lm", -1)):
-            iota(T[n][:], (n,), [[0, 128]], v, 0)
-            aff(T[n][:], (n,), [[-16, 8], [0, 16]], A.is_ge, 0)
-            aff(T[n][:], (n,), [[16, 8], [0, 16]], A.is_ge, 15, -1)
         aff(T.lm[:], ("lm",), [[-1, 128]], A.is_gt, 0)
         iota(T.s8[:], ("s8",), [[0, 8]], -int(B2), 0)
+        iota(T.rt[:, 64:72], ("rt", 64, 72), [[0, 8]], 0, 0)
         aff(T.s8[:], ("s8",), [[-16, 8]], A.is_ge, 0)
+        iota(T.pl[:, :, 64:72], ("pl", 0, 72, 2), [[0, 16]], 0, 0)
         aff(T.s8[:], ("s8",), [[16, 8]], A.is_ge, 15, -1)
         aff(T.wsw[:], ("wsw",), [[16, 8], [0, 16]], A.is_ge, 1, -1, src=I1)
         aff(T.wkp[:], ("wkp",), [[-16, 8], [0, 16]], A.is_ge, -2, 1, src=I1)
@@ -462,12 +536,8 @@ def rank_program(g, core, T, topo):
             aff(T.wsm[:, 0:128:16], ("wsm",), [[-16, 8]], A.not_equal, -r, 1, 1.0)
             weight(7, 8, 0, 1, 2 + r, 0, 1.0)
             weight(7, 9, 1, 2, r, 0, 1.0)
-        iota(T.idm[:], ("idm",), [[0, 128]], -1, 0)
-        aff(T.idm[:], ("idm",), [[-1, 128]], A.is_equal, 0)
         iota(T.r16[:], ("r16",), [[0, 8], [1, 16]], 0, 0)
         aff(T.r16[:], ("r16",), [[0, 8], [1, 16]], A.is_equal, 0, 0, 1.0)
-        iota(T.rt[:, 64:72], ("rt", 64, 72), [[0, 8]], 0, 0)
-        iota(T.pl[:, :, 64:72], ("pl", 0, 72, 2), [[0, 16]], 0, 0)
         fill(T.kz[:, :, 3], ("kz",), float(TS))
         ts(pm[:, 3:4], ("pm", 3, 4), T.pid[:], ("pid",), 15, None, A.bitwise_and)
         cpy(co[:, 8:9], ("cols", 8, 9), pm[:, 3:4], ("pm", 3, 4))
@@ -490,16 +560,16 @@ def rank_program(g, core, T, topo):
     def own(be, bank, q, w, start, stop):
         sg = "sg%d" % be
         for s in range(2):
-            mm(blk(bank, q), bank, *w, T[sg][:, 32 * s:32 * s + 32, :], (sg,), start and s == 0, stop and s == 1)
+            mm(blk(bank, q), bank, *w, T[sg][:, 32 * s:32 * s + 32, :], (sg, 0, 64), start and s == 0, stop and s == 1)
 
     def after(be, bank, q, w, stop):
         sg = "sg%d" % be
         for s in range(2):
-            mm(blk(bank, q, None, 1, 3), bank, *w, T[sg][:, 32 * s:32 * s + 32, 0:2], (sg,), False, False)
-            mm(blk(bank, q, None, 0, 1), bank, *w, T[sg][:, 32 * s:32 * s + 32, 2:3], (sg,), False, stop and s == 1)
+            mm(blk(bank, q, None, 1, 3), bank, *w, T[sg][:, 32 * s:32 * s + 32, 0:2], (sg, 0, 64), False, False)
+            mm(blk(bank, q, None, 0, 1), bank, *w, T[sg][:, 32 * s:32 * s + 32, 2:3], (sg, 0, 64), False, stop and s == 1)
 
     def next_list(be, more=None):
-        tb, sc, lt, ob, off = [n % be for n in ("tb%d", "sc%d", "lt%d")] + ["b%d" % (6 + be), "off%d" % be]
+        tb, sc, lt, ob, off = [n % be for n in ("tb%d", "sc%d", "lt%d")] + ["b%d" % (2 + be), "off%d" % be]
         step("scan")
         scan(T[sc][:, 0:96], (sc,), T.rs3[:, 0:96], ("rs3",), T[tb][:, 0:96], (tb,), A.max)
         step("mask")
@@ -515,28 +585,28 @@ def rank_program(g, core, T, topo):
         for i, (buf, c) in enumerate((("rw%d" % be, 0), ("ge%d" % be, 0), ("eq", H * be))):
             l0 = 96 * be + 32 * i
             win = (T.pwb[:, TS * i:TS * i + W], ("pwb", TS * i, TS * i + W)) if t else (T.inf[:, 0:W], ("inf",))
-            gather("V" if (i == 1 if t else (i + be) % 2) else "S", T[buf][:, c:c + H], (buf, c, c + H), *win, T.lst[:, l0:l0 + 32], ("lst", l0, l0 + 32))
+            gather(RS[t][3 * be + i], T[buf][:, c:c + H], (buf, c, c + H), *win, T.lst[:, l0:l0 + 32], ("lst", l0, l0 + 32))
             w = (T.wr[:, 7:9, :, 1], ("wr", 7, 9)) if t else (T.wr[:, 4:7, :, i], ("wr", 4, 7))
             for b in range(4):
                 mm(T[cb][:, b:64 if t else 96:4, i], cb, T[buf][:, c + b:c + H:4], (buf, c, c + H), *w, i + b == 0, False)
         own(be, cb, 0, IB2, False, True)
         ts(T[tb][:, 0:96], (tb,), blk(cb, 0), (cb,), 0.0 if t else -B, None, A.add)
-        if t:
-            ts(T[ci][:, 0:96], (ci, 0, 96), T[ci][:, 192:288], (ci, 192, 288), int(STAMP) - 1, None, A.bitwise_and)
-            ts(T[st][:, 96:192], (st, 96, 192), T[ci][:, 0:96], (ci, 0, 96), -1.0, -STAMP, A.mult, A.add)
 
         def keep():
-            ts(T[st][:, 0:96], (st, 0, 96), blk(cb, 1), (cb,), 0.0 if t else -B, None, A.add)
+            act(T[st][:, 0:96], (st, 0, 96), blk(cb, 1), (cb,), AF.Identity, bias=0.0 if t else -B)
             if not t:
-                ts(T[st][:, 96:192], (st, 96, 192), blk(cb, 2), (cb,), -STAMP, None, A.add)
+                act(T[st][:, 96:192], (st, 96, 192), blk(cb, 2), (cb,), AF.Identity, bias=-STAMP)
         next_list(be, keep)
 
     def find(be, q, last):
         ge, rw, off, sg, st, tb = [n % be for n in ("ge%d", "rw%d", "off%d", "sg%d", "st%d", "tb%d")]
         yb, xb, cb = ["b%d" % (n + be) for n in (0, 2, 4)]
         step("gather")
-        gather_tt(T[ge][:], (ge,), T.xs[:, 0:W], ("xs",), T[off][:], (off,), T.wf[:, H * be:H * be + H], ("wf", H * be, H * be + H), A.is_ge)
         gather("S", T[rw][:], (rw,), T.inf[:, 0:W], ("inf",), T[off][:], (off,))
+        for a, b in ((0, CUT), (CUT, H)) if be == 0 else ((0, H),):
+            c = H * be
+            gather_tt(T[ge][:, a:b], (ge, a, b), T.xs[:, 0:W], ("xs",), T[off][:, a // 16:b // 16], (off,), T.wf[:, c + a:c + b], ("wf", c, c + H), A.is_ge)
+            step("rest")
         step("own")
         own(be, yb, 0, I16, True, False)
         own(be, yb, 2, I16, False, False)
@@ -547,32 +617,42 @@ def rank_program(g, core, T, topo):
                 mm(T[bank][:, 32 * q0 + b:32 * (q0 + n):4, 0:3], bank, T[src][:, b::4], (src,), w, wreg, start and b == 0, stop and b == 3)
         step("count")
         rows(yb, 3, rw, T.wr[:, 0:3, :, :], ("wr", 0, 3), False, False)
+        step("hits")
         rows(yb, 3, ge, T.wg[:], ("wg",), False, True)
         step("rows")
+        kb = "b%d" % (6 + be)
         if last:
-            rows(cb, 1, rw, T.wr[:, 6, :, :], ("wr", 6, 7), True, False, 2)
+            rows(kb, 1, rw, T.wr[:, 6, :, :], ("wr", 6, 7), True, False, 1)
         else:
             rows(xb, 1, rw, T.wr[:, 3, :, :], ("wr", 3, 4), True, False)
-            rows(cb, 3, rw, T.wr[:, 4:7, :, :], ("wr", 4, 7), True, False)
+            rows(cb, 1, rw, T.wr[:, 4, :, :], ("wr", 4, 5), True, False)
+            step("more")
+            rows(kb, 2, rw, T.wr[:, 5:7, :, :], ("wr", 5, 7), True, False)
         step("sign")
-        act(T[sg][:], (sg,), blk(yb, 0, 3), (yb,), AF.Sign)
-        mv = (T[sg][:, 64:96, :], (sg,))
-        step("bounds")
+        mv = (T[sg][:, 64:96, :], (sg, 64, 96))
+        act(*mv, blk(yb, 2), (yb,), AF.Sign)
+        act(T[sg][:, 0:64, :], (sg, 0, 64), blk(yb, 0, 2), (yb,), AF.Sign)
+        step("low")
         if not last:
             mm(blk(xb, 0), xb, *IB, *mv, False, True)
+        step("bounds")
+        if not last:
             mm(blk(cb, 0), cb, *IMB, *mv, False, False)
-            own(be, cb, 0, IB2, False, False)
-            mm(blk(cb, 1), cb, *IMB, *mv, False, False)
-        mm(blk(cb, 2), cb, T.stl[:, q, :], ("stl", q, q + 1), *mv, False, True)
+            own(be, cb, 0, IB2, False, True)
+            step("stamp")
+            mm(blk(kb, 0), kb, *IMB, *mv, False, False)
+        for _t in range(mark[0][2]):
+            mm(blk(kb, 1), kb, *IRD, *mv, False, False)
+        mm(blk(kb, 1), kb, T.stl[:, q, :], ("stl", q, q + 1), *mv, False, True)
         if last:
             step("max")
-            tt(T[st][:, 96:192], (st, 96, 192), blk(cb, 2), (cb,), T[st][:, 96:192], (st, 96, 192), A.min)
+            tt(T[st][:, 96:192], (st, 96, 192), blk(kb, 1), (kb,), T[st][:, 96:192], (st, 96, 192), A.min)
             return
         step("max")
         tt(T[st][:, 0:96], (st, 0, 96), blk(xb, 0), (xb,), T[st][:, 0:96], (st, 0, 96), A.max)
         step("min")
         tt(T[tb][:, 0:96], (tb,), blk(cb, 0), (cb,), T[st][:, 0:96], (st, 0, 96), A.min)
-        next_list(be, lambda: tt(T[st][:], (st,), blk(cb, 1, 3), (cb,), T[st][:], (st,), A.min))
+        next_list(be, lambda: tt(T[st][:], (st,), blk(kb, 0, 2), (kb,), T[st][:], (st,), A.min))
 
     def finds(be, t):
         mark[0] = (None, be, t, -1)
@@ -604,10 +684,10 @@ def rank_program(g, core, T, topo):
             mm(flat(ob, 96, 128), ob, T.lte0[:, 8:16, :, :], ("lte0",), T.tri[:, 32:64], ("tri",), True, False)
         mm(flat(ob, 64, 96), ob, T[lte][:, 8:16, :, :], (lte,), T.sel[:], ("sel",), be == 0, False)
         mm(flat(ob, 96, 128), ob, T[lte][:, 8:16, :, :], (lte,), T.tri[:, 0:32], ("tri",), False, True)
-        cpy(T.wp[:, :, 32 * be:32 * be + 32], ("wp", 0, 64, be), flat(ob, 64, 128), (ob,))
+        copy(CP[be], T.wp[:, :, 32 * be:32 * be + 32], ("wp", 0, 64, be), flat(ob, 64, 128), (ob,))
         for s in range(2):
             mm(flat(ob, 32 * s, 32 * s + 32), ob, T[lte][:, 16 * s:16 * s + 8, :, :], (lte,), T.sel[:], ("sel",), s == 0, s == 1)
-        cpy(T.pl[:, :, 32 * be:32 * be + 32], ("pl", 0, 72, be), flat(ob, 0, 64), (ob,))
+        copy(CP[2 + be], T.pl[:, :, 32 * be:32 * be + 32], ("pl", 0, 72, be), flat(ob, 0, 64), (ob,))
 
     def swap(last):
         wt, pre = (T.wp[:, 0, :], ("wp",)), (T.wp[:, 1, :], ("wp",))
@@ -703,9 +783,7 @@ def rank_program(g, core, T, topo):
                 mm(T[yb][:, 0:8, b], yb, T[rw][:, b::4], (rw,), T.wr[:, 7, :, 0], ("wr", 7, 8), b == 0, b == 3)
             masks(lambda h: T[lt][:, :, h, :], lt, flat(yb, 0, 32), (yb,), 4)
             mm(flat(yb, 0, 32), yb, T[lt][:], (lt,), T.sel[:], ("sel",), True, True)
-            late[0] -= KL
             cpy(T.kl[:, 32 * be:32 * be + 32], ("kl", be, be + 1), flat(yb, 0, 32), (yb,))
-            late[0] += KL
 
     def pull(t, last):
         xn = "x%d" % (t + 1)
@@ -716,20 +794,13 @@ def rank_program(g, core, T, topo):
             for c in range(0, H, 128):
                 mm(flat(dn, c, c + 128), dn, T.idm[:], ("idm",), T.wf[:, a + c:a + c + 128], ("wf", a, b), c == 0, False)
             mm(T[dn][:], dn, *I1, T[ge][:], (ge,), False, True)
-            if ADD[t]:
-                for c in range(0, H, 256):
-                    ts(*room("dd", a + c, a + c + 256), flat(dn, c, c + 256), (dn,), 8.0, -8.0, A.min, A.max)
-                for k in range(2):
-                    for c in range(0, H, 128):
-                        src = room("dd", a + c, a + c + 128) if k else (T.wf[:, a + c:a + c + 128], ("wf", a, b))
-                        mm(flat(dn, c, c + 128), dn, T.idm[:], ("idm",), *src, c + k == 0, k and c + 128 == H)
-                act(*w, T[dn][:], (dn,), AF.Copy, scale=-1.0)
-            else:
-                ts(T[dn][:], (dn,), T[dn][:], (dn,), 8.0, -8.0, A.min, A.max)
-                tt(*w, T[dn][:], (dn,), *w, A.add)
+            ts(T[dn][:], (dn,), T[dn][:], (dn,), 8.0, -8.0, A.min, A.max)
+            tt(*w, T[dn][:], (dn,), *w, A.add)
             if last:
                 dma("S", T.yw[:, a:b], None, T.wf[:, a:b], ("wf", a, b), "d_yw%d" % be)
 
+    send("xs")
+    window()
     later()
     for t in range(ROUNDS):
         last = t == ROUNDS - 1
@@ -737,21 +808,17 @@ def rank_program(g, core, T, topo):
         late[0] = FB
         finds(1, t)
         late[0] = 0.0
-        if t == 0:
-            sends()
-        late[0] = -AHEAD[t]
         foreign()
-        late[0] = 0.0
         cursors(last)
         swap(last)
-        late[0] = -AHEAD[t]
         pull(t, last)
-        late[0] = 0.0
         if not last:
+            send("x1", "inf")
             whole_numbers()
-    if len(calls) not in PLANS:
-        PLANS[len(calls)] = plan()
-    for n in PLANS[len(calls)]:
+    kind = tuple(w[2] for w in mine)
+    if kind not in PLANS:
+        PLANS[kind] = plan()
+    for n in PLANS[kind]:
         emit(*calls[n][:6])
     for s in sorted(total):
         know("G", s, total[s])

from concourse.mybir import AluOpType, ActivationFunctionType, AxisListType

A = AluOpType
AF = ActivationFunctionType
W, K, NT, ROUNDS, FINDS, CAP = 6144, 1024, 3, 2, 8, 128
H = K // 2
Q = W // 4
TS = 8192
PW = 2 * TS + W
B, B2, STAMP = 16384.0, 32768.0, 16384.0
NEQ = 4
MS = 3
MP = (3, 2)
NV = 4
XA = 2048
FB = 0.5
SOON = 1.0
CUT = 352
CP = "SVSS"
RS = ("SVSVSV", "SVSSVS")
FILL = "YYG"
PIECE, EARLY, BYS = 512, 30.0, 4096
TRIES, SHAKE = 1400, 0.4
WAKE, FLY, RATE = 0.13, 2.0, 6e5
SB, BF, FP, I32, U16 = "sbuf", "bfloat16", "float32", "int32", "uint16"
SCRATCH = {
    "xs": (SB, [128, W], BF), "x1": (SB, [128, W], BF), "x2": (SB, [128, W], BF), "inf": (SB, [128, W], BF),
    "pwb": (SB, [128, PW + 2 * CAP], BF), "pwf": (SB, [128, PW + 2 * CAP], FP),
    "wf": (SB, [128, K], FP), "n32": (SB, [128, Q], I32), "m32": (SB, [128, 384], I32),
    "cur32": (SB, [128, 3, 2, 32], I32), "typ32": (SB, [128, 64], I32), "lst": (SB, [128, 192], U16), "ycf": (SB, [128, 3, 2, 32], FP),
    "id1": (SB, [128, 8, 4, 4], BF), "idn": (SB, [128, 5, 128], BF), "stl": (SB, [128, FINDS, 128], BF),
    "wr": (SB, [128, 9, 8, 3], BF), "wg": (SB, [128, 72], BF), "sel": (SB, [128, 32], FP), "tri": (SB, [128, 64], FP), "selr": (SB, [128, 32], BF),
    "rs3": (SB, [128, 288], FP), "r16": (SB, [128, 128], FP), "kz": (SB, [128, 32, 4], BF),
    "pid": (SB, [128, 1], I32), "pm": (SB, [128, 8], I32), "cols": (SB, [128, 16], FP), "ttl": (SB, [128, 64, 4], BF),
    "bo": (SB, [128, 128], BF), "bof": (SB, [128, 128], FP), "idm": (SB, [128, 128], FP), "lm": (SB, [128, 128], BF), "s8": (SB, [128, 8], BF),
    "wsw": (SB, [128, 128], BF), "wkp": (SB, [128, 128], BF), "wsm": (SB, [128, 128], BF),
    "km": (SB, [128, 128], BF), "k3": (SB, [128, 128], BF),
    "kc": (SB, [128, 8], FP), "kch": (SB, [128, 8], FP), "dum": (SB, [128, 16], FP), "kio": (SB, [128, 128], FP),
    "pl": (SB, [128, 2, 72], FP), "wp": (SB, [128, 2, 64], BF), "rt": (SB, [128, 72], FP),
    "ck": (SB, [128, 8], FP), "ckl": (SB, [128, 8], U16), "oh": (SB, [128, 128], FP), "pr": (SB, [128, 256], FP),
    "mk": (SB, [128, 256], FP), "plt": (SB, [128, 256], FP), "plr": (SB, [128, 256], U16), "eq": (SB, [128, 256 * NEQ], BF),
    "sl": (SB, [128, 16], U16), "gs": (SB, [128, 256], BF),
    "nvb": (SB, [128, 256], BF), "nvf": (SB, [128, 256], FP), "lk": (SB, [128, 128], BF),
    "of": (SB, [128, 16], FP), "ofl": (SB, [128, 16], U16),
    "ml": (SB, [128, 64], U16), "kl": (SB, [128, 64], U16),
}
ROOMS = {"fm": ("pwb", 0), "vr": ("pwb", 1152), "wb": ("pwb", 2 * TS), "nhi": ("pwb", W + 2 * CAP), "nlo": ("pwb", TS + W),
         "pv": ("pwf", W + 2 * CAP)}
for _b in range(2):
    for _n, _s, _d in (("ge", [128, H], BF), ("rw", [128, H], BF), ("off", [128, 32], U16), ("st", [128, 192], FP), ("sg", [128, 96, 3], BF),
                       ("tb", [128, 288], FP), ("sc", [128, 288], FP), ("lt", [128, 8, 4, 4], FP), ("lte", [128, 24, 4, 4], FP),
                       ("ltc", [128, 8, 4, 12], FP), ("ci", [128, 288], I32), ("cf", [128, 96], FP)):
        SCRATCH["%s%d" % (_n, _b)] = (SB, _s, _d)
for _i in range(8):
    SCRATCH["b%d" % _i] = ("psum", [128, 128, 4], FP)
ENG = {"V": "cv", "S": "cs", "P": "cp_", "G": "cg"}
DMAS = ["l_n", "l_m", "l_c", "l_t", "l_a", "l_x", "l_w", "d_bi", "d_fl", "d_pb", "d_pf", "d_pa", "d_rb", "d_yc", "d_yw0", "d_yw1", "d_yn"]
SEMAPHORES = sorted(ENG.values()) + DMAS + ["rx1", "rx2", "tx"]
LOADS = DMAS[:7]
PLANS = {}
TURNS = {
    "V": [("gather", 0, 0), ("list", 1, 1), ("rest", 0, 0), ("gather", 1, 0), ("keep", 1, 1), ("max", 0, 0), ("min", 0, 0), ("scan", 0, 0), ("max", 1, 0),
          ("mask", 0, 0), ("min", 1, 0), ("scan", 1, 0), ("keep", 0, 0), ("list", 0, 0), ("mask", 1, 0)],
    "S": [("gather", 0, 0), ("gather", 1, 0), ("sign", 0, 0), ("sign", 1, 0), ("mask", 0, 0), ("mask", 1, 0)],
    "P": [("own", 0, 0), ("list", 1, 1), ("count", 0, 0), ("hits", 0, 0), ("rows", 0, 0), ("more", 0, 0), ("count", 1, 0), ("low", 0, 0),
          ("hits", 1, 0), ("bounds", 0, 0), ("rows", 1, 0), ("low", 1, 0), ("stamp", 0, 0), ("bounds", 1, 0), ("more", 1, 0), ("stamp", 1, 0),
          ("list", 0, 0), ("own", 1, -1)],
}


def routes(cores, topo):
    out = []
    for r, c in enumerate(cores):
        first, second = cores[r - 1], cores[r - 2]
        far = topo.engines(c, second)
        hands = [h for h in topo.cores_of(c) if h not in cores and topo.may_write(h, first) and topo.may_write(h, second)]
        near = [n for n in topo.engines(c, hands[0]) if n not in far] or far
        once = topo.chip(first) == topo.chip(second) != topo.chip(c)
        buf = "x1" if once else "x2"
        for h, a, eng in ((hands[0], 0, far), (hands[-1], W // 2, near)):
            out.append((c, h, "xs", buf, a, a + W // 2, eng))
            out.append((h, first, buf, "x1", a, a + W // 2, near if topo.chip(first) == topo.chip(c) else far))
            if not once:
                out.append((h, second, buf, "x2", a, a + W // 2, far))
        if once:
            out.append((first, second, "x1", "x2", 0, W, topo.engines(first, second)))
    return out


def rank_program(g, core, T, topo):
    rank = T.rank_of(core)
    mine = [w for w in routes(list(T.cores), topo) if w[0] == core]
    counts = {"tx": sum(len(w[6]) for w in mine)}
    for w in routes(list(T.cores), topo):
        if w[1] == core:
            counts["r" + w[3]] = counts.get("r" + w[3], 0) + len(w[6])

    def write(w):
        rid, pid, _s = topo.addr(w[1])
        g.remote_dma(T[w[3]][:, w[4]:w[5]], T[w[2]][:, w[4]:w[5]], T.sem["r" + w[3]], T.sem.tx, pid, rid, sum(1 << n for n in w[6]))

    if rank is None:
        for w in sorted(mine, key=lambda w: (w[3], w[2])):
            g.wait_ge(T.sem["r" + w[2]], counts["r" + w[2]])
            write(w)
        if mine:
            g.wait_ge(T.sem.tx, counts["tx"])
        return
    queues = {"V": g.vector, "S": g.scalar, "P": g.tensor, "G": g, "Y": g.sync}
    clock = {q: {} for q in queues}
    total = {}
    snap = {}
    acc = {}
    calls = []

    late = [0.0]
    mark, steps = [None], {}

    def know(q, sem, val):
        c = clock[q]
        if c.get(sem, 0) >= val:
            return
        queues[q].wait_ge(T.sem[sem], val)
        for s, v in snap.get((sem, val), {}).items():
            if v > c.get(s, 0):
                c[s] = v
        c[sem] = val

    def region(r):
        buf, lo, hi, tag = (r + (0, 1 << 20, None))[:4] if len(r) == 1 else (r + (None,))[:4]
        if SCRATCH.get(buf, ("", 0, 0))[0] == "psum":
            return buf, 0, 512, None, True
        return buf, lo, hi, tag, False

    def needs(q, reads, writes, dma):
        need = {}
        for lst, wr in ((reads, False), (writes, True)):
            for r in lst:
                buf, lo, hi, tag, bank = region(r)
                for a in acc.get(buf, ()):
                    if a[1] <= lo or hi <= a[0] or (tag is not None and a[2] is not None and a[2] != tag):
                        continue
                    same = a[3] == q and not dma and a[4] not in DMAS
                    if not (wr or a[6]) and (not bank or same):
                        continue
                    if same and q == "P":
                        continue
                    need[a[4]] = max(need.get(a[4], 0), a[5])
        return need

    def emit(q, fn, reads, writes, dma, cost):
        need = needs(q, reads, writes, dma)
        for s in sorted(need):
            know(q, s, total[s] if s in DMAS else need[s])
        ins = fn(queues[q])
        if dma == "tx":
            return
        sem, inc = (dma, 16) if dma else (ENG[q], 1)
        ins.then_inc(T.sem[sem], inc)
        total[sem] = total.get(sem, 0) + inc
        val = total[sem]
        s = dict(clock[q])
        for k2, v2 in snap.get((sem, val - inc), {}).items():
            s[k2] = max(v2, s.get(k2, 0))
        s[sem] = val
        snap[(sem, val)] = s
        for lst, wr in ((writes, True), (reads, False)):
            for r in lst:
                buf, lo, hi, tag, bank = region(r)
                keep = []
                for a in acc.get(buf, []):
                    inside = lo <= a[0] and a[1] <= hi and (tag is None or tag == a[2])
                    if inside and (wr or (not a[6] and a[3] == q and a[4] == sem)):
                        continue
                    keep.append(a)
                keep.append((lo, hi, tag, q, sem, val, wr))
                acc[buf] = keep

    def op(q, fn, reads, writes, dma=None, cost=0.1):
        calls.append((q, fn, reads, writes, dma, cost, late[0]))
        steps.setdefault((q, mark[0]), []).append(len(calls) - 1)

    def step(name):
        mark[0] = (name,) + mark[0][1:]

    def plan():
        seen, before, g0 = {}, [], {}
        for n, (q, _f, reads, writes, dm, cost, _l) in enumerate(calls):
            dep = {}
            for lst, wr in ((reads, False), (writes, True)):
                for r in lst:
                    buf, lo, hi, tag, bank = region(r)
                    for a in seen.get((buf, True), []) + (seen.get((buf, False), []) if wr or bank else []):
                        same = calls[a[4]][0] == q and not dm and not calls[a[4]][4]
                        if a[0] < hi and lo < a[1] and (tag is None or a[2] is None or a[2] == tag) and (wr or a[3] or bank and not same):
                            dep[a[4]] = max(dep.get(a[4], 0.0), 0.0 if same and q == "P" else WAKE)
            line = "Y" if dm in LOADS else q
            if line in "GY":
                if line in g0:
                    dep.setdefault(g0[line], None)
                g0[line] = n
            before.append(dep)
            for lst, wr in ((writes, True), (reads, False)):
                for r in lst:
                    buf, lo, hi, tag, bank = region(r)
                    for key in ((buf, True), (buf, False)) if wr else ():
                        seen[key] = [a for a in seen.get(key, []) if not (lo <= a[0] and a[1] <= hi and (tag is None or tag == a[2]))]
                    seen.setdefault((buf, wr), []).append((lo, hi, tag, wr, n))
        for q, turn in TURNS.items():
            for t in range(ROUNDS):
                line = [n for f in range(-1, FINDS + 1) for name, be, back in turn for n in steps.get((q, (name, be, t, f - back)), [])]
                for m, n in zip(line, line[1:]):
                    before[n].setdefault(m, 0.0)
        after = [[] for _c in calls]
        for n, d in enumerate(before):
            for m in d:
                after[m].append(n)
        left = [len(d) for d in before]
        order = [n for n in range(len(calls)) if not left[n]]
        for n in order:
            for m in after[n]:
                left[m] -= 1
                if not left[m]:
                    order.append(m)
        assert len(order) == len(calls)
        way, beside = [0.0] * len(calls), [0.0] * len(calls)
        for n in reversed(order):
            c = calls[n]
            way[n] += c[5] + (FLY if c[4] and c[4] != "tx" else 0.0) - min(c[6], 0.0)
            way[n] = max(way[n], beside[n])
            for m, lat in before[n].items():
                if lat is None and calls[m][4] and calls[m][4] != "tx":
                    beside[m] = max(beside[m], way[n] + 0.05)
                else:
                    way[m] = max(way[m], way[n] + (lat or 0.0))
        rank0 = [way[n] - max(c[6], 0.0) for n, c in enumerate(calls)]
        best = lay(rank0, before, after)
        free = [n for (q, m), ns in steps.items() if m is None or m[3] in (-1, FINDS - 1) for n in ns]
        seed = 1
        for _try in range(TRIES):
            seed = (seed * 1103515245 + 12345) % (1 << 31)
            t0 = best[0] * seed / (1 << 31)
            new = list(rank0)
            for n in free:
                if abs(best[2][n] - t0) < 3.0:
                    seed = (seed * 1103515245 + 12345) % (1 << 31)
                    new[n] += SHAKE * (seed / (1 << 30) - 1.0)
            if new != rank0:
                now = lay(new, before, after)
                if now[0] <= best[0]:
                    best, rank0 = now, new
        return best[1]

    def lay(rank0, before, after):
        busy = {q: [] for q in list(queues) + ["D"]}

        def place(q, t, c):
            line = busy[q]
            k = len(line)
            while k and line[k - 1][0] >= t:
                k -= 1
            t = max(t, line[k - 1][1]) if k else t
            while k < len(line) and line[k][0] < t + c:
                t = line[k][1]
                k += 1
            line.insert(k, (t, t + c))
            return t
        start, end, left = {}, {}, [len(d) for d in before]
        ready = [n for n in range(len(calls)) if not left[n]]
        while ready:
            n = max(ready, key=lambda n: rank0[n])
            ready.remove(n)
            q, _f, _r, _w, dm, cost, _l = calls[n]
            t = max([0.0] + [start[m] + 1e-6 if lat is None else end[m] + lat for m, lat in before[n].items()])
            if dm and dm != "tx":
                start[n] = place(q, t, 0.05)
                end[n] = place("D", start[n] + 0.7 * FLY, cost) + cost + 0.3 * FLY
            else:
                start[n] = place(q, t, cost)
                end[n] = start[n] + cost
            for m in after[n]:
                left[m] -= 1
                if not left[m]:
                    ready.append(m)
        order = sorted(range(len(calls)), key=lambda n: (start[n], n))
        now = dict.fromkeys(busy, 0.0)
        for n in order:
            q, _f, _r, _w, dm, cost, _l = calls[n]
            t = max([now[q]] + [start[m] if lat is None else end[m] + lat for m, lat in before[n].items()])
            start[n] = t
            if dm and dm != "tx":
                now[q] = t + 0.05
                now["D"] = max(now["D"], t + 0.7 * FLY) + cost
                end[n] = now["D"] + 0.3 * FLY
            else:
                end[n] = now[q] = t + cost
        return max(end.values()), order, start

    I1 = (T.id1[:], ("id1",))
    I16, IB, IMB, IB2, IRD = [(T.idn[:, n, :], ("idn",)) for n in range(5)]

    def cols(ap):
        n = 1
        for d in list(ap.shape)[1:]:
            n *= d
        return n

    def us(cycles):
        return 0.04 + 0.00096 * cycles

    def blk(bank, q0, q1=None, i0=0, i1=3):
        return T[bank][:, 32 * q0:32 * (q0 + 1 if q1 is None else q1), i0:i1]

    def room(name, a, b, p0=0, p1=128):
        buf, c = ROOMS[name]
        return T[buf][p0:p1, c + a:c + b], (buf, c + a, c + b)

    def flat(bank, a, b):
        return T[bank][:, a // 4:b // 4, :]

    def tt(out, o, a, ra, b, rb, f):
        n = cols(out)
        bank = any(region(r)[4] for r in (ra, rb))
        op("V", lambda e: e.tensor_tensor(out, a, b, f), [ra, rb], [o], None, us(max(64, n if bank else 2 * n)))

    def ts(out, o, a, ra, s1, s2, f1, f2=None, extra=(), fast=1.0):
        c = us(max(64, fast * cols(out)))
        if f2 is None:
            op("V", lambda e: e.tensor_scalar(out, a, s1, None, f1), [ra] + list(extra), [o], None, c)
        else:
            op("V", lambda e: e.tensor_scalar(out, a, s1, s2, f1, f2), [ra] + list(extra), [o], None, c)

    def cpy(out, o, a, ra):
        op("V", lambda e: e.tensor_copy(out, a), [ra], [o], None, us(max(64, cols(out))))

    def scan(out, o, d0, r0, d1, r1, f):
        op("V", lambda e: e.tensor_tensor_scan(out, d0, d1, 0.0, A.mult, f), [r0, r1], [o], None, us(max(64, cols(out))))

    def act(out, o, a, ra, f, bias=0.0, scale=1.0, extra=(), accum=None, ao=None):
        c = us(cols(out)) + 0.03
        if accum is None:
            op("S", lambda e: e.activation(out, a, f, bias=bias, scale=scale), [ra] + list(extra), [o], None, c)
        else:
            op("S", lambda e: e.activation(out, a, f, bias=bias, scale=scale, accum_out=accum), [ra] + list(extra), [o, ao], None, c)

    def copy(q, out, o, a, ra):
        if q == "V":
            cpy(out, o, a, ra)
        else:
            act(out, o, a, ra, AF.Copy)

    def mm(out, bank, l, rl, r, rr, start, stop):
        four = 4 if SCRATCH[rl[0]][2] == FP else 1
        op("P", lambda e: e.matmul(out, l, r, start, stop), [rl, rr], [(bank,)], None, max(64, cols(r)) * 0.0005 * four)

    def dma(q, out, o, a, ra, sem, also=()):
        size = out.shape[0] * cols(out) * (2 if o and SCRATCH[o[0]][2] == BF else 4)
        op(q, lambda e: e.dma_start(out, a), [ra] if ra else [], ([o] if o else []) + list(also), sem, size / RATE + 0.002 * max(out.shape[0], a.shape[0]))

    def fill(ap, o, v):
        op("V", lambda e: e.memset(ap, v), [], [o])

    def aff(ap, o, pat, cmp, base, mult=1, val=0.0, src=None):
        s, rs = src or (ap, o)
        op("G", lambda e: e.affine_select(ap, s, pat, cmp, val, base, mult), [rs], [o], None, 0.17 + 0.002 * cols(ap))

    def iota(ap, o, pat, base, mult):
        op("G", lambda e: e.iota(ap, pat, base, mult, allow_small_or_imprecise_dtypes=True), [], [o], None, 0.13 + 0.002 * cols(ap))

    def gather(q, out, oreg, win, wreg, off, offreg):
        src = win.indirect(off)
        c = us(1.56 * cols(out))
        if q == "V":
            op("V", lambda e: e.tensor_copy(out, src), [wreg, offreg], [oreg], None, c)
        else:
            op("S", lambda e: e.activation(out, src, AF.Copy), [wreg, offreg], [oreg], None, c)

    def gather_tt(out, oreg, win, wreg, off, offreg, b, rb, f):
        src = win.indirect(off)
        op("V", lambda e: e.tensor_tensor(out, src, b, f), [wreg, offreg, rb], [oreg], None, us(1.56 * cols(out)))

    for i in range(NT):
        dma("YS"[i % 2], T.n32[32 * i:32 * i + 32, :], ("n32", 0, Q, i), T.nxt[:, W * i:W * i + W], None, "l_n")
    dma("S", T.n32[96:128, :], ("n32", 0, Q, 3), T.fro[:], None, "l_n")
    dma("Y", T.m32[:], ("m32",), T.mem[:], None, "l_m")
    dma("S", T.typ32[:], ("typ32",), T.typ[:], None, "l_t")
    dma("Y", T.cur32[:], ("cur32",), T.cur[:], None, "l_c")
    dma("Y", T.xs[:, 0:XA], ("xs", 0, XA), T.x[:, 0:XA], None, "l_a")

    pm, co = T.pm, T.cols
    op("G", lambda e: e.iota(T.pid[:], [[1, 1]], 0, 1), [], [("pid",)])
    iota(*room("pv", 0, 384), [[1, 3], [0, 128]], 0, 3)
    iota(*room("vr", 0, 384), [[0, 3], [1, 128]], 0, 0)
    for c in range(0, W, Q):
        op("V", lambda e, c=c: e.memset(T.inf[:, c:c + Q], 1.0), [], [("inf", c, c + Q)], None, us(Q / 2))
    fill(T.wr[:], ("wr",), 0.0)
    fill(T.id1[:], ("id1",), 1.0)
    for n, v in enumerate((16.0, B, -B, B2, -STAMP * FINDS)):
        fill(T.idn[:, n, :], ("idn", n, n + 1), v)
    fill(T.wg[:, 0:24], ("wg", 0, 24), -1.0)
    fill(T.wg[:, 24:72], ("wg", 24, 72), 1.0)
    fill(T.sel[:], ("sel",), 1.0)
    fill(T.rs3[:], ("rs3",), 1.0)
    fill(T.rs3[:, 0:288:3], ("rs3",), 0.0)
    ts(pm[:, 0:1], ("pm", 0, 1), T.pid[:], ("pid",), 4, None, A.arith_shift_right)
    ts(co[:, 9:10], ("cols", 9, 10), pm[:, 0:1], ("pm", 0, 1), -48, None, A.mult)
    ts(pm[:, 1:2], ("pm", 1, 2), T.pid[:], ("pid",), 2, 3, A.arith_shift_right, A.bitwise_and)
    ts(pm[:, 2:3], ("pm", 2, 3), T.pid[:], ("pid",), 3, None, A.bitwise_and)
    for h in range(4):
        ts(co[:, 4 + h:5 + h], ("cols", 4 + h, 5 + h), pm[:, 1:2], ("pm", 1, 2), h, None, A.is_equal)
        ts(co[:, h:h + 1], ("cols", h, h + 1), pm[:, 2:3], ("pm", 2, 3), h, None, A.is_equal)
    aff(T.id1[:], ("id1",), [[-1, 128]], A.is_equal, 0)

    def weight(q0, q1, i0, i1, row, step, val):
        aff(T.wr[:, q0:q1, :, i0:i1], ("wr", q0, q1), [[0, q1 - q0], [-16, 8], [-step, i1 - i0]], A.not_equal, -row, 1, val)

    weight(3, 6, 0, 3, 0, 2, 1.0)
    weight(6, 7, 0, 3, 9, 0, -1.0)
    weight(3, 6, 0, 3, 1, 2, 1.0)
    weight(6, 7, 0, 3, 10, 0, -128.0)
    weight(4, 6, 0, 3, 13, 0, B)
    for i, row, v in ((0, 7, -1), (0, 8, 2), (0, 14, -192), (1, 8, -1), (1, 14, 192), (2, 6, -1), (2, 7, 2), (2, 14, -384)):
        weight(6, 7, i, i + 1, row, 0, float(TS * v))
    aff(T.idn[:], ("idn",), [[0, 5], [-1, 128]], A.is_equal, 0)
    aff(T.sel[:], ("sel",), [[-4, 32]], A.is_ge, 0)
    weight(3, 4, 0, 3, 13, 0, -B)
    aff(T.sel[:], ("sel",), [[4, 32]], A.is_ge, 3, -1)
    weight(2, 3, 0, 3, 6, 1, 16.0)
    weight(0, 1, 0, 3, 13, 0, 8.5)
    weight(2, 3, 0, 2, 7, 1, -32.0)
    weight(1, 2, 0, 3, 13, 0, -8.5)
    weight(2, 3, 0, 3, 13, 0, 7.5)
    aff(T.wg[:], ("wg",), [[0, 3], [-16, 8], [0, 3]], A.is_ge, 0)
    for i, v in enumerate((6144.0, 3072.0, -3072.0)):
        weight(2, 3, i, i + 1, 14, 0, v)
    aff(T.wg[:], ("wg",), [[0, 3], [16, 8], [0, 3]], A.is_ge, 15, -1)

    def to_inf(q, k, src, reg):
        dma(q, T.inf[k::16, :], ("inf", 0, W, k), src, reg, "d_bi", [("gate", k, k + 1)])

    act(*room("vr", 384, 768), *room("pv", 0, 384), AF.Identity, bias=co[:, 9:10], extra=[("cols", 9, 10)])
    cpy(*room("fm", 0, 384), T.m32[:], ("m32",))
    parts = [(512 * c, 512 * c + 512, "b%d" % c) for c in range(3)]
    for a, b, bank in parts:
        cpy(T[bank][:], (bank,), T.n32[:, a:b], ("n32", a, b))
    for a, b, bank in parts:
        act(*room("nhi", a, b), T[bank][:], (bank,), AF.Copy)
        tt(*room("nlo", a, b), T[bank][:], (bank,), *room("nhi", a, b), A.subtract)
    for n, (s, o) in enumerate(((0.5, 191.75), (0.25, 191.625))):
        act(*room("fm", 384 * n + 384, 384 * n + 768), *room("fm", 0, 384), AF.Identity, bias=o, scale=s)
    for n in range(2):
        to_inf("Y", 9 + n, *room("vr", 384 * n, 384 * n + 384))
    to_inf("Y", 6, *room("fm", 0, 384))
    for k, src in enumerate(("nhi", "nlo")):
        for i in range(NT):
            to_inf("Y", 2 * i + k, *room(src, 0, Q, 32 * i, 32 * i + 32))
        to_inf("Y", 7 + k, *room("fm", 384 * k + 384, 384 * k + 768))

    dma("Y", *room("wb", 0, K), T.w0[:], None, "l_w")
    dma("Y", T.xs[:, XA:W], ("xs", XA, W), T.x[:, XA:W], None, "l_x")

    iota(T.kz[:], ("kz",), [[0, 32], [TS, 4]], TS, 0)
    iota(T.kc[:], ("kc",), [[16, 8]], 0, 1)
    iota(T.km[:], ("km",), [[0, 8], [1, 16]], 0, 0)
    for be in range(2):
        cpy(T.lst[:, 96 * be:96 * be + 96], ("lst", 96 * be, 96 * be + 96), T.cur32[:, :, be, :], ("cur32",))
    tt(T.selr[:], ("selr",), T.id1[:, :, 0, :], ("id1",), T.id1[:, :, 1, :], ("id1",), A.add)
    for h in (2, 3):
        tt(T.selr[:], ("selr",), T.selr[:], ("selr",), T.id1[:, :, h, :], ("id1",), A.add)
    for h in range(4):
        ts(T.ttl[:, :, h], ("ttl", 0, 256, h), T.typ32[:], ("typ32",), co[:, 4 + h:5 + h], None, A.mult, extra=[("cols", 4 + h, 5 + h)])
    for be in range(2):
        sg, ob = "sg%d" % be, "b%d" % (6 + be)
        mm(flat(ob, 0, 32), ob, T.ttl[:, 32 * be:32 * be + 32, :], ("ttl",), T.selr[:], ("selr",), True, True)
        for i in range(NT):
            ts(T[sg][:, 0:32, i], (sg, 0, 32, i), flat(ob, 0, 32), (ob,), float(i), 2.0, A.is_equal, A.mult)
        fill(T[sg][:, 32:64, :], (sg, 32, 64), -2.0)
    act(T.wf[:, 0:H], ("wf", 0, H), *room("wb", 0, H), AF.Copy)
    cpy(T.wf[:, H:K], ("wf", H, K), *room("wb", H, K))
    for t in range(FINDS):
        act(T.stl[:, t, :], ("stl", t, t + 1), *I1, AF.Copy, scale=-STAMP * (t + 2))

    def send(src, gate="gate"):
        for w in mine:
            if w[2] == src:
                op("G", lambda e, w=w: write(w), [(src,), (gate,)], [], "tx", 1.0)

    iota(T.tri[:], ("tri",), [[0, 64]], 1, 0)
    iota(T.bo[:], ("bo",), [[0, 128]], 1, 0)
    aff(T.tri[:], ("tri",), [[4, 64]], A.is_ge, 3, -1)
    aff(T.bo[:], ("bo",), [[-16, 8], [0, 16]], A.is_ge, 0)
    iota(T.kio[:], ("kio",), [[1, 128]], 1, 0)
    aff(T.bo[:], ("bo",), [[16, 8], [0, 16]], A.is_ge, 15, -1)
    iota(T.idm[:], ("idm",), [[0, 128]], -1, 0)
    iota(T.lm[:], ("lm",), [[0, 128]], -1, 0)
    aff(T.idm[:], ("idm",), [[-1, 128]], A.is_equal, 0)
    aff(T.lm[:], ("lm",), [[-16, 8], [0, 16]], A.is_ge, 0)
    aff(T.bof[:], ("bof",), [[0, 128]], A.is_ge, 0, src=(T.bo[:], ("bo",)))
    aff(T.lm[:], ("lm",), [[16, 8], [0, 16]], A.is_ge, 15, -1)

    def window():
        for i in range(NT):
            o = (T.pwb[:, TS * i:TS * i + W], ("pwb", TS * i, TS * i + W))
            if FILL[i] == "Y":
                dma("Y", *o, T.x[:], ("xs",), "d_fl")
            elif FILL[i] == "G":
                iota(*o, [[0, W]], 0, 0)
            else:
                late[0] = -EARLY
                for c in range(TS * i, TS * i + W, PIECE):
                    if c < TS * i + BYS:
                        act(T.pwb[:, c:c + PIECE], ("pwb", c, c + PIECE), T.xs[:, 0:PIECE], ("xs", 0, PIECE), AF.Copy)
                    else:
                        op("V", lambda e, c=c: e.memset(T.pwb[:, c:c + PIECE], 0.0), [], [("pwb", c, c + PIECE)], None, us(PIECE / 2))
                late[0] = 0.0
        for i in range(NT):
            for k, src in enumerate(("nhi", "nlo")):
                dma("Y", T.pwb[k::16, TS * i:TS * i + W], ("pwb", TS * i, TS * i + W, k), room(src, 0, Q, 32 * i, 32 * i + 32)[0], ("xs",), "d_pb")
                dma("Y", T.pwb[2 + k::16, TS * i:TS * i + W], ("pwb", TS * i, TS * i + W, 2 + k), room(src, 0, Q, 96, 128)[0], ("xs",), "d_pb")

    total.update(counts)
    for n in ("x1", "x2"):
        acc[n] = [(0, 1 << 20, None, "R", "r" + n, total["r" + n], True)]

    def later():
        aff(T.lm[:], ("lm",), [[-1, 128]], A.is_gt, 0)
        iota(T.s8[:], ("s8",), [[0, 8]], -int(B2), 0)
        iota(T.rt[:, 64:72], ("rt", 64, 72), [[0, 8]], 0, 0)
        aff(T.s8[:], ("s8",), [[-16, 8]], A.is_ge, 0)
        iota(T.pl[:, :, 64:72], ("pl", 0, 72, 2), [[0, 16]], 0, 0)
        aff(T.s8[:], ("s8",), [[16, 8]], A.is_ge, 15, -1)
        aff(T.wsw[:], ("wsw",), [[16, 8], [0, 16]], A.is_ge, 1, -1, src=I1)
        aff(T.wkp[:], ("wkp",), [[-16, 8], [0, 16]], A.is_ge, -2, 1, src=I1)
        iota(T.wsm[:], ("wsm",), [[0, 128]], 0, 0)
        for r in range(2):
            aff(T.wsm[:, 0:128:16], ("wsm",), [[-16, 8]], A.not_equal, -r, 1, 1.0)
            weight(7, 8, 0, 1, 2 + r, 0, 1.0)
            weight(7, 9, 1, 2, r, 0, 1.0)
        iota(T.r16[:], ("r16",), [[0, 8], [1, 16]], 0, 0)
        aff(T.r16[:], ("r16",), [[0, 8], [1, 16]], A.is_equal, 0, 0, 1.0)
        fill(T.kz[:, :, 3], ("kz",), float(TS))
        ts(pm[:, 3:4], ("pm", 3, 4), T.pid[:], ("pid",), 15, None, A.bitwise_and)
        cpy(co[:, 8:9], ("cols", 8, 9), pm[:, 3:4], ("pm", 3, 4))
        ts(co[:, 10:11], ("cols", 10, 11), pm[:, 0:1], ("pm", 0, 1), -16, None, A.mult)
        ts(T.kc[:], ("kc",), T.kc[:], ("kc",), co[:, 10:11], None, A.add, extra=[("cols", 10, 11)])
        ts(T.km[:], ("km",), T.km[:], ("km",), co[:, 8:9], None, A.is_equal, extra=[("cols", 8, 9)])
        ts(T.k3[:], ("k3",), T.km[:, 0:128], ("km",), 3.0, -1.0, A.mult, A.add)
        ts(T.kch[:], ("kch",), T.kc[:], ("kc",), 0.5, None, A.add)
        for n in range(2):
            ts(T.dum[:, 8 * n:8 * n + 8], ("dum", 8 * n, 8 * n + 8), T.kc[:], ("kc",), -1.0, -float(TS + PW + CAP * n), A.mult, A.add)

    def masks(out, obuf, src, sreg, nscalar):
        for h in range(4):
            o = (obuf, 0, 1 << 20, h)
            if h < nscalar:
                act(out(h), o, src, sreg, AF.Copy, scale=co[:, h:h + 1], extra=[("cols", h, h + 1)])
            else:
                ts(out(h), o, src, sreg, co[:, h:h + 1], None, A.mult, extra=[("cols", h, h + 1)])

    def own(be, bank, q, w, start, stop):
        sg = "sg%d" % be
        for s in range(2):
            mm(blk(bank, q), bank, *w, T[sg][:, 32 * s:32 * s + 32, :], (sg, 0, 64), start and s == 0, stop and s == 1)

    def after(be, bank, q, w, stop):
        sg = "sg%d" % be
        for s in range(2):
            mm(blk(bank, q, None, 1, 3), bank, *w, T[sg][:, 32 * s:32 * s + 32, 0:2], (sg, 0, 64), False, False)
            mm(blk(bank, q, None, 0, 1), bank, *w, T[sg][:, 32 * s:32 * s + 32, 2:3], (sg, 0, 64), False, stop and s == 1)

    def next_list(be, more=None):
        tb, sc, lt, ob, off = [n % be for n in ("tb%d", "sc%d", "lt%d")] + ["b%d" % (2 + be), "off%d" % be]
        step("scan")
        scan(T[sc][:, 0:96], (sc,), T.rs3[:, 0:96], ("rs3",), T[tb][:, 0:96], (tb,), A.max)
        step("mask")
        masks(lambda h: T[lt][:, :, h, :], lt, T[sc][:, 2:96:3], (sc,), MS)
        step("keep")
        more()
        step("list")
        mm(flat(ob, 0, 32), ob, T[lt][:], (lt,), T.sel[:], ("sel",), True, True)
        cpy(T[off][:], (off,), flat(ob, 0, 32), (ob,))

    def round_start(be, t):
        xb, cb, st, tb, ci = "b%d" % (2 + be), "b%d" % (4 + be), "st%d" % be, "tb%d" % be, "ci%d" % be
        for i, (buf, c) in enumerate((("rw%d" % be, 0), ("ge%d" % be, 0), ("eq", H * be))):
            l0 = 96 * be + 32 * i
            win = (T.pwb[:, TS * i:TS * i + W], ("pwb", TS * i, TS * i + W)) if t else (T.inf[:, 0:W], ("inf",))
            gather(RS[t][3 * be + i], T[buf][:, c:c + H], (buf, c, c + H), *win, T.lst[:, l0:l0 + 32], ("lst", l0, l0 + 32))
            w = (T.wr[:, 7:9, :, 1], ("wr", 7, 9)) if t else (T.wr[:, 4:7, :, i], ("wr", 4, 7))
            for b in range(4):
                mm(T[cb][:, b:64 if t else 96:4, i], cb, T[buf][:, c + b:c + H:4], (buf, c, c + H), *w, i + b == 0, False)
        own(be, cb, 0, IB2, False, True)
        ts(T[tb][:, 0:96], (tb,), blk(cb, 0), (cb,), 0.0 if t else -B, None, A.add)

        def keep():
            act(T[st][:, 0:96], (st, 0, 96), blk(cb, 1), (cb,), AF.Identity, bias=0.0 if t else -B)
            if not t:
                act(T[st][:, 96:192], (st, 96, 192), blk(cb, 2), (cb,), AF.Identity, bias=-STAMP)
        next_list(be, keep)

    def find(be, q, last):
        ge, rw, off, sg, st, tb = [n % be for n in ("ge%d", "rw%d", "off%d", "sg%d", "st%d", "tb%d")]
        yb, xb, cb = ["b%d" % (n + be) for n in (0, 2, 4)]
        step("gather")
        gather("S", T[rw][:], (rw,), T.inf[:, 0:W], ("inf",), T[off][:], (off,))
        for a, b in ((0, CUT), (CUT, H)) if be == 0 else ((0, H),):
            c = H * be
            gather_tt(T[ge][:, a:b], (ge, a, b), T.xs[:, 0:W], ("xs",), T[off][:, a // 16:b // 16], (off,), T.wf[:, c + a:c + b], ("wf", c, c + H), A.is_ge)
            step("rest")
        step("own")
        own(be, yb, 0, I16, True, False)
        own(be, yb, 2, I16, False, False)
        after(be, yb, 1, I16, False)

        def rows(bank, n, src, w, wreg, start, stop, q0=0):
            for b in range(4):
                mm(T[bank][:, 32 * q0 + b:32 * (q0 + n):4, 0:3], bank, T[src][:, b::4], (src,), w, wreg, start and b == 0, stop and b == 3)
        step("count")
        rows(yb, 3, rw, T.wr[:, 0:3, :, :], ("wr", 0, 3), False, False)
        step("hits")
        rows(yb, 3, ge, T.wg[:], ("wg",), False, True)
        step("rows")
        kb = "b%d" % (6 + be)
        if last:
            rows(kb, 1, rw, T.wr[:, 6, :, :], ("wr", 6, 7), True, False, 1)
        else:
            rows(xb, 1, rw, T.wr[:, 3, :, :], ("wr", 3, 4), True, False)
            rows(cb, 1, rw, T.wr[:, 4, :, :], ("wr", 4, 5), True, False)
            step("more")
            rows(kb, 2, rw, T.wr[:, 5:7, :, :], ("wr", 5, 7), True, False)
        step("sign")
        mv = (T[sg][:, 64:96, :], (sg, 64, 96))
        act(*mv, blk(yb, 2), (yb,), AF.Sign)
        act(T[sg][:, 0:64, :], (sg, 0, 64), blk(yb, 0, 2), (yb,), AF.Sign)
        step("low")
        if not last:
            mm(blk(xb, 0), xb, *IB, *mv, False, True)
        step("bounds")
        if not last:
            mm(blk(cb, 0), cb, *IMB, *mv, False, False)
            own(be, cb, 0, IB2, False, True)
            step("stamp")
            mm(blk(kb, 0), kb, *IMB, *mv, False, False)
        for _t in range(mark[0][2]):
            mm(blk(kb, 1), kb, *IRD, *mv, False, False)
        mm(blk(kb, 1), kb, T.stl[:, q, :], ("stl", q, q + 1), *mv, False, True)
        if last:
            step("max")
            tt(T[st][:, 96:192], (st, 96, 192), blk(kb, 1), (kb,), T[st][:, 96:192], (st, 96, 192), A.min)
            return
        step("max")
        tt(T[st][:, 0:96], (st, 0, 96), blk(xb, 0), (xb,), T[st][:, 0:96], (st, 0, 96), A.max)
        step("min")
        tt(T[tb][:, 0:96], (tb,), blk(cb, 0), (cb,), T[st][:, 0:96], (st, 0, 96), A.min)
        next_list(be, lambda: tt(T[st][:], (st,), blk(kb, 0, 2), (kb,), T[st][:], (st,), A.min))

    def finds(be, t):
        mark[0] = (None, be, t, -1)
        round_start(be, t)
        for q in range(FINDS):
            mark[0] = (None, be, t, q)
            find(be, q, q == FINDS - 1)
        mark[0] = None
        places(be)

    def places(be):
        st, ci, tb, sc, lte = [n % be for n in ("st%d", "ci%d", "tb%d", "sc%d", "lte%d")]
        xb, ob = "b%d" % (2 + be), "b%d" % (6 + be)
        own(be, xb, 0, IB2, True, False)
        mm(blk(xb, 0), xb, *I1, T.kz[:, :, 1:4], ("kz",), False, False)
        own(be, xb, 1, IB2, False, False)
        mm(blk(xb, 2), xb, *I1, T.kz[:, :, 0:3], ("kz",), False, False)
        after(be, xb, 2, IB2, True)
        ts(T[ci][:, 192:288], (ci, 192, 288), T[st][:, 96:192], (st, 96, 192), -1.0, None, A.mult)
        ts(T[ci][:, 0:96], (ci, 0, 96), T[ci][:, 192:288], (ci, 192, 288), TS - 1, None, A.bitwise_and)
        ts(T[ci][:, 96:192], (ci, 96, 192), T[ci][:, 192:288], (ci, 192, 288), TS, None, A.bitwise_and)
        tt(T[tb][:, 192:288], (tb, 192, 288), blk(xb, 2), (xb,), T[ci][:, 0:96], (ci, 0, 96), A.add)
        tt(T[tb][:, 0:192], (tb, 0, 192), blk(xb, 0, 2), (xb,), T[ci][:, 0:192], (ci, 0, 192), A.add)
        scan(T[sc][:], (sc,), T.rs3[:], ("rs3",), T[tb][:], (tb,), A.max)
        tt(T[tb][:, 0:32], (tb,), T[sc][:, 2:96:3], (sc,), T[sc][:, 194:288:3], (sc,), A.not_equal)
        tt(T[sc][:, 98:192:3], (sc,), T[tb][:, 0:32], (tb,), T[sc][:, 98:192:3], (sc,), A.min)
        masks(lambda h: T[lte][:, :, h, :], lte, T[sc][:, 2:288:3], (sc,), MP[be])
        if be:
            mm(flat(ob, 96, 128), ob, T.lte0[:, 8:16, :, :], ("lte0",), T.tri[:, 32:64], ("tri",), True, False)
        mm(flat(ob, 64, 96), ob, T[lte][:, 8:16, :, :], (lte,), T.sel[:], ("sel",), be == 0, False)
        mm(flat(ob, 96, 128), ob, T[lte][:, 8:16, :, :], (lte,), T.tri[:, 0:32], ("tri",), False, True)
        copy(CP[be], T.wp[:, :, 32 * be:32 * be + 32], ("wp", 0, 64, be), flat(ob, 64, 128), (ob,))
        for s in range(2):
            mm(flat(ob, 32 * s, 32 * s + 32), ob, T[lte][:, 16 * s:16 * s + 8, :, :], (lte,), T.sel[:], ("sel",), s == 0, s == 1)
        copy(CP[2 + be], T.pl[:, :, 32 * be:32 * be + 32], ("pl", 0, 72, be), flat(ob, 0, 64), (ob,))

    def swap(last):
        wt, pre = (T.wp[:, 0, :], ("wp",)), (T.wp[:, 1, :], ("wp",))
        mm(flat("b3", 0, 64), "b3", T.bo[:], ("bo",), *pre, True, True)
        mm(flat("b2", 64, 128), "b2", T.bo[:], ("bo",), *pre, True, False)
        mm(flat("b2", 0, 64), "b2", T.bo[:], ("bo",), *pre, False, False)
        mm(flat("b2", 0, 64), "b2", T.lm[:], ("lm",), *wt, False, True)
        for n in range(8):
            jk = (T.eq[:, 64 * n:64 * n + 64], ("eq", 64 * n, 64 * n + 64))
            if n < NV:
                ts(*jk, flat("b2", 64, 128), ("b2",), T.kc[:, n:n + 1], None, A.is_le, extra=[("kc",)])
                op("V", lambda e, n=n, jk=jk: e.tensor_reduce(T.ck[:, n:n + 1], jk[0], AxisListType.X, A.add), [jk[1]], [("ck", n, n + 1)])
            else:
                act(*jk, flat("b3", 0, 64), ("b3",), AF.Sign, bias=T.kch[:, n:n + 1], scale=-1.0, extra=[("kch",)], accum=T.ck[:, n:n + 1], ao=("ck", n, n + 1))
        tt(T.rt[:, 0:64], ("rt", 0, 64), flat("b2", 0, 64), ("b2",), *wt, A.mult)
        if NV:
            cpy(T.ckl[:, 0:NV], ("ckl", 0, NV), T.ck[:, 0:NV], ("ck", 0, NV))
        ts(T.ckl[:, NV:8], ("ckl", NV, 8), T.ck[:, NV:8], ("ck", NV, 8), 0.5, 32.0, A.mult, A.add)
        gather_tt(T.oh[:], ("oh",), T.rt[:, 0:72], ("rt",), T.ckl[:], ("ckl",), T.kio[:], ("kio",), A.is_equal)
        for s in range(2):
            gather_tt(T.pr[:, 128 * s:128 * s + 128], ("pr", s, s + 1), T.pl[:, s, :], ("pl",), T.ckl[:], ("ckl",), T.oh[:], ("oh",), A.mult)
            mm(flat("b%d" % (3 - s), 0, 128), "b%d" % (3 - s), T.bof[:], ("bof",), T.pr[:, 128 * s:128 * s + 128], ("pr", s, s + 1), True, True)
        for s in range(2):
            a, b, bank = 128 * s, 128 * s + 128, "b%d" % (3 - s)
            tt(T.mk[:, a:b], ("mk", a, b), flat(bank, 0, 128), (bank,), T.km[:], ("km",), A.mult)
            scan(T.plt[:, a:b], ("plt", a, b), T.r16[:], ("r16",), T.mk[:, a:b], ("mk", a, b), A.add)
            cpy(T.plr[:, a:b], ("plr", a, b), flat(bank, 0, 128), (bank,))
        plt = (T.plt[:, 15::16], ("plt",))
        late[0] = -SOON
        ts(T.sl[:], ("sl",), *plt, -TS, None, A.add)
        late[0] = 0.0
        gather("S", T.gs[:], ("gs",), T.pwb[:, 0:PW], ("pwb",), T.sl[:], ("sl",))
        for s in range(2):
            a, b = 128 * s, 128 - 128 * s
            wn = "wsm" if last else "wsw"
            mm(flat("b2", a, a + 128), "b2", T[wn][:], (wn,), T.gs[:, b:b + 128], ("gs",), s == 0, last and s == 1)
            if not last:
                mm(flat("b2", a, a + 128), "b2", T.wkp[:], ("wkp",), T.gs[:, a:a + 128], ("gs",), False, s == 1)
        nv = "nvf" if last else "nvb"
        act(T[nv][:], (nv,), flat("b2", 0, 256), ("b2",), AF.Copy)
        mm(flat("b6", 0, 16), "b6", T.idm[:], ("idm",), T.dum[:], ("dum",), True, False)
        for n in range(16):
            a = 256 * (n % NEQ)
            ts(T.eq[:, a:a + 256], ("eq", a, a + 256), T.plr[:], ("plr",), T.plt[:, 16 * n + 15:16 * n + 16], None, A.is_equal, extra=[("plt", 16 * n, 16 * n + 16)], fast=0.5)
            for s in range(2):
                mm(flat("b7", 0, 128), "b7", T.eq[:, a + 128 * s:a + 128 * s + 128], ("eq", a, a + 256), T.bo[:], ("bo",), n == 0 and s == 0, n == 15 and s == 1)
        tt(T.lk[:], ("lk",), flat("b7", 0, 128), ("b7",), T.k3[:], ("k3",), A.is_equal)
        for s in range(2):
            mm(flat("b6", 8 * s, 8 * s + 8), "b6", T.lk[:], ("lk",), T.s8[:], ("s8",), False, s == 1)
        tt(T.of[:], ("of",), flat("b6", 0, 16), ("b6",), *plt, A.max)
        ts(T.ofl[:], ("ofl",), T.of[:], ("of",), -TS, None, A.add)
        win, src = ("pwf", "nvf") if last else ("pwb", "nvb")
        out = T[win][:].indirect(T.ofl[:])
        op("V", lambda e: e.tensor_copy(out, T[src][:]), [(src,), ("ofl",)], [(win,)], None, 1.0)
        for i in range(NT):
            if last:
                dma("Y", T.yn[:, W * i:W * i + W], None, T.pwf[0::16, TS * i:TS * i + W], ("pwf", TS * i, TS * i + W), "d_yn")
                continue
            for k in range(2):
                dma("Y", T.inf[2 * i + k::16, :], ("inf", 0, W, 2 * i + k), T.pwb[k::16, TS * i:TS * i + W], ("pwb", TS * i, TS * i + W), "d_rb")

    def whole_numbers():
        for k in range(2):
            for i in range(NT):
                o, a = T.pwf[0::16, TS * i:TS * i + W], T.pwb[k::16, TS * i:TS * i + W]
                if k == 0:
                    op("G", lambda e, o=o, a=a: e.dma_start(o, a), [("pwb",), ("inf",)], [("pwf", TS * i, TS * i + W)], "d_pf")
                else:
                    op("G", lambda e, o=o, a=a: e.dma_start(o, a, accum_op=A.add, max_dma_last_dim=4096), [("pwb",)], [("pwf", TS * i, TS * i + W)], "d_pa")

    def cursors(last):
        for be in range(2):
            ci, cf, ltc, cb = "ci%d" % be, "cf%d" % be, "ltc%d" % be, "b%d" % (4 + be)
            late[0] = -SOON
            cpy(T[cf][:], (cf,), T[ci][:, 0:96], (ci, 0, 96))
            late[0] = 0.0
            masks(lambda h: T[ltc][:, :, h, :], ltc, T[cf][:], (cf,), 4)
            for i in range(NT):
                mm(flat(cb, 32 * i, 32 * i + 32), cb, T[ltc][:, :, :, i::3], (ltc,), T.sel[:], ("sel",), i == 0, i == NT - 1)
            if last:
                act(T.ycf[:, :, be, :], ("ycf", be, be + 1), flat(cb, 0, 96), (cb,), AF.Copy)
            else:
                cpy(T.lst[:, 96 * be:96 * be + 96], ("lst", 96 * be, 96 * be + 96), flat(cb, 0, 96), (cb,))
        if last:
            dma("S", T.yc[:], None, T.ycf[:], ("ycf",), "d_yc")

    def foreign():
        for be in range(2):
            rw, lt, yb, ob = "rw%d" % be, "lt%d" % be, "b%d" % (4 + be), "b%d" % (6 + be)
            ts(T.ml[:, 32 * be:32 * be + 32], ("ml", be, be + 1), T.pl[:, 0, 32 * be:32 * be + 32], ("pl", 0, 72, be), -TS, None, A.add)
            gather("S", T[rw][:], (rw,), T.pwb[:, 0:PW], ("pwb",), T.ml[:, 32 * be:32 * be + 32], ("ml", be, be + 1))
            for b in range(4):
                mm(T[yb][:, 0:8, b], yb, T[rw][:, b::4], (rw,), T.wr[:, 7, :, 0], ("wr", 7, 8), b == 0, b == 3)
            masks(lambda h: T[lt][:, :, h, :], lt, flat(yb, 0, 32), (yb,), 4)
            mm(flat(yb, 0, 32), yb, T[lt][:], (lt,), T.sel[:], ("sel",), True, True)
            cpy(T.kl[:, 32 * be:32 * be + 32], ("kl", be, be + 1), flat(yb, 0, 32), (yb,))

    def pull(t, last):
        xn = "x%d" % (t + 1)
        for be in range(2):
            a, b, dn = H * be, H * be + H, "b%d" % be
            ge, w = "ge%d" % be, (T.wf[:, a:b], ("wf", a, b))
            gather("S", T[ge][:], (ge,), T[xn][:, 0:W], (xn,), T.kl[:, 32 * be:32 * be + 32], ("kl", be, be + 1))
            for c in range(0, H, 128):
                mm(flat(dn, c, c + 128), dn, T.idm[:], ("idm",), T.wf[:, a + c:a + c + 128], ("wf", a, b), c == 0, False)
            mm(T[dn][:], dn, *I1, T[ge][:], (ge,), False, True)
            ts(T[dn][:], (dn,), T[dn][:], (dn,), 8.0, -8.0, A.min, A.max)
            tt(*w, T[dn][:], (dn,), *w, A.add)
            if last:
                dma("S", T.yw[:, a:b], None, T.wf[:, a:b], ("wf", a, b), "d_yw%d" % be)

    send("xs")
    window()
    later()
    for t in range(ROUNDS):
        last = t == ROUNDS - 1
        finds(0, t)
        late[0] = FB
        finds(1, t)
        late[0] = 0.0
        foreign()
        cursors(last)
        swap(last)
        pull(t, last)
        if not last:
            send("x1", "inf")
            whole_numbers()
    kind = tuple(w[2] for w in mine)
    if kind not in PLANS:
        PLANS[kind] = plan()
    for n in PLANS[kind]:
        emit(*calls[n][:6])
    for s in sorted(total):
        know("G", s, total[s])
